import numpy as np
import ml_dtypes


def mxq(x, axis, fmt="e4m3"):
    dtype, down = {"e4m3": (ml_dtypes.float8_e4m3fn, 7), "e5m2": (ml_dtypes.float8_e5m2, 14)}[fmt]
    v = np.moveaxis(np.asarray(x, np.float32).astype(ml_dtypes.bfloat16).astype(np.float64), axis, -1)
    blocks = v.reshape(v.shape[:-1] + (-1, 32))
    amax = np.abs(blocks).max(-1, keepdims=True)
    byte = np.maximum(np.where(amax > 0, np.frexp(amax)[1] - 1 + 127, 0) - down, 1)
    scale = np.exp2(byte - 127.0)
    codes = (blocks / scale).astype(np.float32).astype(dtype).astype(np.float64)
    return np.moveaxis((codes * scale).reshape(v.shape), -1, axis)


WIDE = False


def mx_kscale(k):
    if not WIDE:
        return np.ones(k)
    levels = np.array([30, -30])
    if k % 512:
        return np.exp2(np.random.permutation(np.resize(levels, k // 32))).repeat(32)
    a = np.empty((k // 512, 16))
    for p in range(k // 512):
        a[p, :8] = np.random.permutation(np.resize(levels, 8))
        for g in range(8):
            far = levels[np.abs(levels - a[p, g]) >= 10]
            a[p, g + 8] = far[np.random.randint(len(far))]
    return np.exp2(a.ravel()).repeat(32)


def f64(x):
    return np.asarray(x).astype(np.float64)


def striped(idx):
    return np.tile(idx.reshape(-1, 16).T, (8, 1)).astype(np.uint16)


def unstriped(offs):
    return offs[:16].T.reshape(-1).astype(np.int64)


E2M1 = np.array([0.0, 0.5, 1.0, 1.5, 2.0, 3.0, 4.0, 6.0, -0.0, -0.5, -1.0, -1.5, -2.0, -3.0, -4.0, -6.0])


def pack_weight(w, fmt):
    k, n = w.shape
    w = f64(np.asarray(w, np.float32).astype(ml_dtypes.bfloat16)).reshape(k // 32, 32, n)
    amax = np.abs(w).max(1)
    if fmt == "e4m3":
        byte = np.frexp(amax)[1] - 1 + 127 - 7
    elif fmt == "e5m2":
        byte = np.frexp(amax)[1] - 1 + 127 - 14
    else:
        mant, ex = np.frexp(amax / 6.0)
        byte = np.where(mant > 0.5, ex, ex - 1) + 127
    byte = np.clip(np.where(amax > 0, byte, 1), 1, 254)
    scaled = (w * np.exp2(127.0 - byte)[:, None, :]).reshape(k, n).astype(np.float32)
    by_word = np.ascontiguousarray(scaled.reshape(k // 512, 128, 4, n).transpose(0, 1, 3, 2))
    if fmt == "e4m3":
        words = by_word.astype(ml_dtypes.float8_e4m3fn).view(np.uint8)
    elif fmt == "e5m2":
        words = by_word.astype(ml_dtypes.float8_e5m2).view(np.uint8)
    else:
        c = by_word.astype(ml_dtypes.float4_e2m1fn).view(np.uint8) & 0xF
        words = (c[..., 0::2] | (c[..., 1::2] << 4)).reshape(k // 512, 128, 2 * n)
    return np.ascontiguousarray(words), np.ascontiguousarray(byte.astype(np.uint8).reshape(k // 512, 16, n))


def unpack_weight(words, scales, fmt):
    g, _, n = scales.shape
    words = np.ascontiguousarray(words).reshape(g, 128, n, -1)
    if fmt == "e4m3":
        vals = words.view(ml_dtypes.float8_e4m3fn).astype(np.float64)
    elif fmt == "e5m2":
        vals = words.view(ml_dtypes.float8_e5m2).astype(np.float64)
    else:
        nib = np.empty((g, 128, n, 4), np.uint8)
        nib[..., 0::2] = words & 0xF
        nib[..., 1::2] = words >> 4
        vals = E2M1[nib]
    vals = vals * np.repeat(np.exp2(scales.astype(np.float64) - 127.0), 8, axis=1)[..., None]
    return vals.transpose(0, 1, 3, 2).reshape(g * 512, n)


def d_relu(v):
    return (v > 0).astype(np.float64)


K, T, E, C, H, N = 256, 1280, 5, 512, 512, 512


def by_expert(wq, xq):
    return np.concatenate([wq[e].T @ xq[:, e * C:(e + 1) * C] for e in range(E)], axis=1)


def setup_inputs():
    n = np.random.standard_normal
    s = mx_kscale(N)[:, None]
    u = mx_kscale(H)
    first = np.random.permutation(np.repeat(np.arange(E), T // E))
    second = (first + 1 + np.random.permutation(np.repeat(np.arange(E - 1), -(-T // (E - 1)))[:T])) % E
    while np.bincount(second, minlength=E).max() != T // E:
        load = np.bincount(second, minlength=E); hi, lo = int(load.argmax()), int(load.argmin())
        t = np.flatnonzero((second == hi) & (first != lo))[0]; second[t] = lo
    slot_token = np.empty(E * C, np.int64); pos = np.empty((2, T), np.int64); fill = np.zeros(E, np.int64)
    place = np.stack([np.random.permutation(C) for _ in range(E)])
    for r, deal in enumerate((first, second)):
        for t in np.random.permutation(T):
            e = deal[t]; j = e * C + place[e, fill[e]]; fill[e] += 1; slot_token[j] = t; pos[r, t] = j
    g = np.random.uniform(0.2, 0.8, T)
    w_slot = np.empty(E * C); w_slot[pos[0]] = g; w_slot[pos[1]] = 1.0 - g
    dy = pack_weight(n((N, T)) * s, "e5m2")
    return {
        "dy_words": dy[0],
        "dy_scales": dy[1],
        "a": n((H, E * C)).astype(np.float32),
        "w2": (n((E, N, H)) / np.sqrt(N) / s[None] * u[None, None, :]).astype(np.float32),
        "w1": (n((E, H, K)) / np.sqrt(H) / u[None, :, None]).astype(np.float32),
        "gate": np.tile(w_slot, (H, 1)).astype(np.float32),
        "offs": striped(slot_token),
        "pos1": striped(pos[0]),
        "pos2": striped(pos[1]),
    }


def reference(dy_words, dy_scales, a, w2, w1, gate, offs, pos1, pos2):
    idx = unstriped(offs)
    gq = unpack_weight(dy_words, dy_scales, "e5m2")[:, idx]
    dh = f64(gate) * by_expert(mxq(f64(w2), 1, "e4m3"), gq)
    da = dh * d_relu(f64(a))
    dx = by_expert(mxq(f64(w1), 1, "e4m3"), mxq(da, 0, "e5m2"))
    return dx[:, unstriped(pos1)] + dx[:, unstriped(pos2)]

@@ -1,0 +1,225 @@
+from contextlib import ExitStack
+
+import concourse.mybir as mybir
+from concourse.masks import make_identity
+
+K, T, E, C, H, N = 256, 1280, 5, 512, 512, 512
+S = E * C
+
+FLOPS = 2 * S * N * H + 2 * S * H * K
+BYTES = N * T + (N // 32) * T + 4 * (H * S + E * N * H + E * H * K + S + K * T) + 2 * 128 * (S + 2 * T) // 16
+
+F32 = mybir.dt.float32
+BF16 = mybir.dt.bfloat16
+I32 = mybir.dt.int32
+U32 = mybir.dt.uint32
+U16 = mybir.dt.uint16
+U8 = mybir.dt.uint8
+E4M3 = mybir.dt.float8_e4m3fn_x4
+E5M2 = mybir.dt.float8_e5m2_x4
+COPY = mybir.ActivationFunctionType.Copy
+MULT = mybir.AluOpType.mult
+ADD = mybir.AluOpType.add
+IS_GT = mybir.AluOpType.is_gt
+
+P = 128
+PACK = 4
+LIST = 16
+HALF = C // 2
+KIB = 1024
+REGION = 19 * KIB // 2
+ROUNDED_AT = (0, KIB, 2 * KIB, 11 * KIB // 2)
+LAST_ROUNDED_AT = (3 * KIB, 0, KIB, 2 * KIB)
+GATHERED_AT = 3 * KIB
+GROUPED_AT = 11 * KIB // 2
+SPARE = E * REGION
+TOKEN_CUTS = ((0, 640, 1280), (0, 640, 960, 1280))
+
+
+def planes_view(raw):
+    return raw.rearrange("p t (c i) -> p c t i", i=2)
+
+
+def packed_view(grouped):
+    return grouped.rearrange("p (c i) t -> p c t i", i=2)
+
+
+def tile_moe_bdx_mlp_relu_kernel(tc, dy_words, dy_scales, a, w2, w1, gate, offs, pos1, pos2, out):
+    nc = tc.nc
+    with ExitStack() as ctx:
+        keep = ctx.enter_context(tc.tile_pool(name="keep", bufs=1))
+        arena = ctx.enter_context(tc.tile_pool(name="arena", bufs=1))
+        ring = ctx.enter_context(tc.tile_pool(name="ring", bufs=2))
+        psum = ctx.enter_context(tc.psum_pool(name="psum", bufs=1))
+
+        def placed(shape, dtype, name, offset):
+            return arena.tile(shape, dtype, name=name, offset=offset, align_bytes=64)
+
+        offs_sb = keep.tile([P, S // LIST], U16, name="offs_sb")
+        pos1_sb = keep.tile([P, T // LIST], U16, name="pos1_sb")
+        pos2_sb = keep.tile([P, T // LIST], U16, name="pos2_sb")
+        dy_w = keep.tile([P, T], U32, name="dy_w", align_bytes=64)
+        dy_s = keep.tile([P, T], U8, name="dy_s", align_bytes=64)
+        gate_rows = keep.tile([P, P], F32, name="gate_rows")
+        gate_cols = keep.tile([P, S // P], F32, name="gate_cols")
+        ident = keep.tile([P, P], F32, name="ident")
+        w2_raw = [placed([P, PACK, H], F32, f"w2_raw{e}", e * REGION) for e in range(E)]
+        w1_raw = [keep.tile([P, PACK, K], F32, name=f"w1_raw{e}") for e in range(E)]
+        a_raw = [keep.tile([P, PACK, C], F32, name=f"a_raw{e}") for e in range(E)]
+        w2_w = [keep.tile([P, H], U32, name=f"w2_w{e}", align_bytes=64) for e in range(E)]
+        w2_s = [keep.tile([P, H], U8, name=f"w2_s{e}", align_bytes=64) for e in range(E)]
+        da_w = [keep.tile([P, C], U32, name=f"da_w{e}", align_bytes=64) for e in range(E)]
+        da_s = [keep.tile([P, C], U8, name=f"da_s{e}", align_bytes=64) for e in range(E)]
+        dx = [keep.tile([P, S], F32, name=f"dx{h}") for h in range(K // P)]
+        sums = [psum.tile([P, C], F32, name=f"sums{b}") for b in range(4)]
+        turned = [psum.tile([P, C], F32, name=f"turned{b}") for b in range(4)]
+
+        nc.vector.memset(dy_s[:].bitcast(I32), 0)
+        nc.vector.memset(gate_rows[:], 0.0)
+        make_identity(nc, ident[:])
+
+        nc.sync.dma_start(offs_sb[:], offs)
+        nc.sync.dma_start(dy_w[:].bitcast(I32), dy_words[0].rearrange("p t d -> p (t d)").bitcast(I32))
+        for q in range(4):
+            nc.scalar.dma_start(dy_s[32 * q : 32 * q + 4, :].bitcast(I32), dy_scales[0, 4 * q : 4 * q + 4, :].bitcast(I32))
+        nc.scalar.dma_start(gate_rows[0 : S // P, :], gate[0].rearrange("(c p) -> c p", p=P))
+        a_rows = a.rearrange("(p t) s -> p t s", t=PACK)
+        nc.sync.dma_start(w2_raw[0][:], w2[0].rearrange("(p t) i -> p t i", t=PACK))
+        for e in range(E):
+            if e + 1 < E:
+                nc.sync.dma_start(w2_raw[e + 1][:], w2[e + 1].rearrange("(p t) i -> p t i", t=PACK))
+            nc.sync.dma_start(a_raw[e][:], a_rows[:, :, e * C : (e + 1) * C])
+            nc.sync.dma_start(w1_raw[e][:], w1[e].rearrange("(p t) k -> p t k", t=PACK))
+        nc.sync.dma_start(pos1_sb[:], pos1)
+        nc.sync.dma_start(pos2_sb[:], pos2)
+
+        nc.tensor.transpose(turned[3][:, 0:P], gate_rows[:], ident[:])
+        nc.vector.tensor_copy(gate_cols[:], turned[3][:, 0 : S // P])
+
+        gathered = {}
+        rounded = {}
+        w1_low = {}
+
+        def grouped_at(e):
+            return SPARE + e * 4 * KIB if e < 2 else (e - 1) * REGION + GROUPED_AT
+
+        def rounded_at(e, s):
+            return (e + 1) * REGION + ROUNDED_AT[s] if e + 1 < E else LAST_ROUNDED_AT[s]
+
+        def da_at(e):
+            return SPARE + (2 + e % 2) * 4 * KIB
+
+        def gather(e):
+            at = SPARE + 16 * KIB + e * 3 * KIB if e < 2 else (e - 1) * REGION + GATHERED_AT
+            slots = offs_sb[:, e * C // LIST : (e + 1) * C // LIST]
+            g_w = placed([P, C], U32, f"g_w{e}", at)
+            g_s = placed([P, C], U8, f"g_s{e}", at + 2 * KIB)
+            nc.vector.tensor_copy(g_w[:], dy_w[:].indirect(slots))
+            nc.vector.tensor_copy(g_s[:], dy_s[:].indirect(slots))
+            gathered[e] = (g_w, g_s)
+
+        def quantise_w2(e):
+            w2_bf = placed([P, H, PACK], BF16, f"w2_bf{e}", grouped_at(e))
+            nc.scalar.copy(packed_view(w2_bf[:]), planes_view(w2_raw[e][:]))
+            nc.vector.quantize_mx(out=w2_w[e][:].bitcast(E4M3), scales=w2_s[e][:], in_=w2_bf[:].rearrange("p i t -> p (i t)"))
+
+        def first_product(e, s):
+            g_w, g_s = gathered[e]
+            cols = slice(s * P, (s + 1) * P)
+            nc.tensor.matmul_mx(
+                out=sums[s][:], lhsT=g_w[:, cols].bitcast(E5M2), lhsT_scale=g_s[:, cols],
+                rhs=w2_w[e][:].bitcast(E4M3), rhs_scale=w2_s[e][:], start=True, stop=True,
+            )
+
+        def gate_and_round(e, s):
+            dh_bf = placed([P, H], BF16, f"dh_bf{e}_{s}", rounded_at(e, s))
+            col = e * (C // P) + s
+            nc.scalar.activation(
+                dh_bf[:].rearrange("s (u p x) -> s u p x", u=2, x=2),
+                sums[s][:].rearrange("s (p u x) -> s u p x", u=2, x=2),
+                COPY, scale=gate_cols[:, col : col + 1],
+            )
+            rounded[e, s] = dh_bf
+
+        def turn(e, half):
+            bank = turned[2 * (e % 2) + half]
+            for s in range(2):
+                pairs = rounded[e, 2 * half + s][:].bitcast(F32)
+                for u in range(2):
+                    at = u * HALF + s * P
+                    nc.tensor.transpose(bank[:, at : at + P], pairs[:, u * P : (u + 1) * P], ident[:])
+
+        def quantise_da(e):
+            mask = placed([P, C, PACK], BF16, f"mask{e}", grouped_at(min(e + 1, E - 1)))
+            nc.vector.tensor_scalar(packed_view(mask[:]), planes_view(a_raw[e][:]), 0.0, None, IS_GT)
+            da_bf = placed([P, C, PACK], BF16, f"da_bf{e}", da_at(e))
+            for half in range(2):
+                cols = slice(half * HALF, (half + 1) * HALF)
+                nc.vector.tensor_tensor(
+                    da_bf[:, cols, :].rearrange("p n (u x) -> p n u x", u=2),
+                    turned[2 * (e % 2) + half][:].bitcast(BF16).rearrange("p (u n x) -> p n u x", u=2, x=2),
+                    mask[:, cols, :].rearrange("p n (u x) -> p n u x", u=2),
+                    MULT,
+                )
+            nc.vector.quantize_mx(out=da_w[e][:].bitcast(E5M2), scales=da_s[e][:], in_=da_bf[:].rearrange("p n t -> p (n t)"))
+
+        def quantise_w1_low(e):
+            w1_bf = placed([P, P, PACK], BF16, f"w1_bf{e}", rounded_at(e, 1))
+            nc.scalar.copy(packed_view(w1_bf[:]), planes_view(w1_raw[e][:, :, 0:P]))
+            w1_w = keep.tile([P, P], U32, name=f"w1_w{e}", align_bytes=64)
+            w1_s = keep.tile([P, P], U8, name=f"w1_s{e}", align_bytes=64)
+            nc.vector.quantize_mx(out=w1_w[:].bitcast(E4M3), scales=w1_s[:], in_=w1_bf[:].rearrange("p k t -> p (k t)"))
+            w1_low[e] = (w1_w[:], w1_s[:])
+
+        def second_product(e, h, w1_w, w1_s, bank):
+            nc.tensor.matmul_mx(
+                out=bank[:], lhsT=w1_w.bitcast(E4M3), lhsT_scale=w1_s,
+                rhs=da_w[e][:].bitcast(E5M2), rhs_scale=da_s[e][:], start=True, stop=True,
+            )
+            nc.scalar.copy(dx[h][:, e * C : (e + 1) * C], bank[:])
+
+        gather(0)
+        gather(1)
+        quantise_w2(0)
+        for s in range(4):
+            first_product(0, s)
+        for e in range(E):
+            if e + 1 < E:
+                quantise_w2(e + 1)
+            if e + 2 < E:
+                gather(e + 2)
+            for s in range(4):
+                gate_and_round(e, s)
+                if s % 2 == 1:
+                    turn(e, s // 2)
+                if s == 1 and e > 0:
+                    second_product(e - 1, 0, *w1_low[e - 1], sums[1])
+                if e + 1 < E:
+                    first_product(e + 1, s)
+            quantise_da(e)
+            quantise_w1_low(e)
+
+        second_product(E - 1, 0, *w1_low[E - 1], sums[0])
+
+        high_bf = placed([P, E * P, PACK], BF16, "high_bf", LAST_ROUNDED_AT[0])
+        for e in range(E):
+            nc.scalar.copy(packed_view(high_bf[:, e * P : (e + 1) * P, :]), planes_view(w1_raw[e][:, :, P:K]))
+        high_w = placed([P, E * P], U32, "high_w", da_at(E - 1))
+        high_s = placed([P, E * P], U8, "high_s", da_at(E - 1) + 5 * KIB // 2)
+        for cols in (slice(0, 4 * P), slice(4 * P, E * P)):
+            nc.vector.quantize_mx(out=high_w[:, cols].bitcast(E4M3), scales=high_s[:, cols], in_=high_bf[:, cols, :].rearrange("p k t -> p (k t)"))
+        for e in range(E):
+            cols = slice(e * P, (e + 1) * P)
+            second_product(e, 1, high_w[:, cols], high_s[:, cols], sums[(e + 1) % 4])
+
+        for h in range(K // P):
+            cuts = TOKEN_CUTS[h]
+            for j in range(len(cuts) - 1):
+                lo, hi = cuts[j], cuts[j + 1]
+                first = ring.tile([P, hi - lo], F32, name="first")
+                second = ring.tile([P, hi - lo], F32, name="second")
+                total = keep.tile([P, hi - lo], F32, name=f"total{h}_{j}")
+                nc.vector.tensor_copy(first[:], dx[h][:].indirect(pos1_sb[:, lo // LIST : hi // LIST]))
+                nc.vector.tensor_copy(second[:], dx[h][:].indirect(pos2_sb[:, lo // LIST : hi // LIST]))
+                nc.vector.tensor_tensor(total[:], first[:], second[:], ADD)
+                nc.sync.dma_start(out[h * P : (h + 1) * P, lo:hi], total[:])

@@ -29,19 +29,21 @@ HALF = C // 2
 KIB = 1024
 REGION = 19 * KIB // 2
 ROUNDED_AT = (0, KIB, 2 * KIB, 11 * KIB // 2)
-LAST_ROUNDED_AT = (3 * KIB, 0, KIB, 2 * KIB)
+ROUNDED_REGION = (1, 2, 3, 4, 0)
+MASK_ON = (1, 3, 4, 3, 4)
+W1_LOW_ON = ((0, 0), (1, 0), (2, 0), (4, 0), (4, 1))
+LATE_AT = 3 * REGION + 13 * KIB // 2
 GATHERED_AT = 3 * KIB
-GROUPED_AT = 11 * KIB // 2
 SPARE = E * REGION
 TOKEN_CUTS = ((0, 640, 1280), (0, 640, 960, 1280))
 
 
 def planes_view(raw):
-    return raw.rearrange("p t (c i) -> p c t i", i=2)
+    return raw.rearrange("p t (c i) -> p c t i", i=4)
 
 
 def packed_view(grouped):
-    return grouped.rearrange("p (c i) t -> p c t i", i=2)
+    return grouped.rearrange("p (c i) t -> p c t i", i=4)
 
 
 def tile_moe_bdx_mlp_relu_kernel(tc, dy_words, dy_scales, a, w2, w1, gate, offs, pos1, pos2, out):
@@ -74,22 +76,29 @@ def tile_moe_bdx_mlp_relu_kernel(tc, dy_words, dy_scales, a, w2, w1, gate, offs,
         sums = [psum.tile([P, C], F32, name=f"sums{b}") for b in range(4)]
         turned = [psum.tile([P, C], F32, name=f"turned{b}") for b in range(4)]
 
-        nc.vector.memset(dy_s[:].bitcast(I32), 0)
+        nc.gpsimd.memset(dy_s[:].bitcast(I32), 0)
         nc.vector.memset(gate_rows[:], 0.0)
         make_identity(nc, ident[:])
 
-        nc.sync.dma_start(offs_sb[:], offs)
-        nc.sync.dma_start(dy_w[:].bitcast(I32), dy_words[0].rearrange("p t d -> p (t d)").bitcast(I32))
-        for q in range(4):
-            nc.scalar.dma_start(dy_s[32 * q : 32 * q + 4, :].bitcast(I32), dy_scales[0, 4 * q : 4 * q + 4, :].bitcast(I32))
-        nc.scalar.dma_start(gate_rows[0 : S // P, :], gate[0].rearrange("(c p) -> c p", p=P))
         a_rows = a.rearrange("(p t) s -> p t s", t=PACK)
-        nc.sync.dma_start(w2_raw[0][:], w2[0].rearrange("(p t) i -> p t i", t=PACK))
-        for e in range(E):
+
+        def load_w2(queue, e, cols=slice(0, H)):
+            queue.dma_start(w2_raw[e][:, :, cols], w2[e].rearrange("(p t) i -> p t i", t=PACK)[:, :, cols])
+
+        load_w2(nc.scalar, 0, slice(0, H // 2))
+        nc.scalar.dma_start(gate_rows[0 : S // P, :], gate[0].rearrange("(c p) -> c p", p=P))
+        nc.sync.dma_start(offs_sb[:], offs)
+        for q in range(4):
+            nc.sync.dma_start(dy_s[32 * q : 32 * q + 4, :].bitcast(I32), dy_scales[0, 4 * q : 4 * q + 4, :].bitcast(I32))
+        nc.sync.dma_start(dy_w[:].bitcast(I32), dy_words[0].rearrange("p t d -> p (t d)").bitcast(I32))
+        load_w2(nc.sync, 0, slice(H // 2, H))
+        for e in range(E + 1):
             if e + 1 < E:
-                nc.sync.dma_start(w2_raw[e + 1][:], w2[e + 1].rearrange("(p t) i -> p t i", t=PACK))
-            nc.sync.dma_start(a_raw[e][:], a_rows[:, :, e * C : (e + 1) * C])
-            nc.sync.dma_start(w1_raw[e][:], w1[e].rearrange("(p t) k -> p t k", t=PACK))
+                load_w2(nc.sync, e + 1)
+            if e >= 1:
+                nc.sync.dma_start(w1_raw[e - 1][:], w1[e - 1].rearrange("(p t) k -> p t k", t=PACK))
+            if e < E:
+                nc.sync.dma_start(a_raw[e][:], a_rows[:, :, e * C : (e + 1) * C])
         nc.sync.dma_start(pos1_sb[:], pos1)
         nc.sync.dma_start(pos2_sb[:], pos2)
 
@@ -101,26 +110,27 @@ def tile_moe_bdx_mlp_relu_kernel(tc, dy_words, dy_scales, a, w2, w1, gate, offs,
         w1_low = {}
 
         def grouped_at(e):
-            return SPARE + e * 4 * KIB if e < 2 else (e - 1) * REGION + GROUPED_AT
+            return SPARE + e * 4 * KIB if e < 3 else rounded_at(e - 3, 3)
 
         def rounded_at(e, s):
-            return (e + 1) * REGION + ROUNDED_AT[s] if e + 1 < E else LAST_ROUNDED_AT[s]
+            return ROUNDED_REGION[e] * REGION + ROUNDED_AT[s]
 
         def da_at(e):
-            return SPARE + (2 + e % 2) * 4 * KIB
+            return SPARE + (3 + e % 2) * 4 * KIB
 
         def gather(e):
-            at = SPARE + 16 * KIB + e * 3 * KIB if e < 2 else (e - 1) * REGION + GATHERED_AT
+            at = SPARE + 20 * KIB + e * 3 * KIB if e < 3 else (e - 2) * REGION + GATHERED_AT
             slots = offs_sb[:, e * C // LIST : (e + 1) * C // LIST]
-            g_w = placed([P, C], U32, f"g_w{e}", at)
+            g_w = placed([P, C], U32, f"g_w{e}", grouped_at(0) + (e - 1) * 2 * KIB if e in (1, 2) else at)
             g_s = placed([P, C], U8, f"g_s{e}", at + 2 * KIB)
-            nc.vector.tensor_copy(g_w[:], dy_w[:].indirect(slots))
             nc.vector.tensor_copy(g_s[:], dy_s[:].indirect(slots))
+            nc.vector.tensor_copy(g_w[:], dy_w[:].indirect(slots))
             gathered[e] = (g_w, g_s)
 
         def quantise_w2(e):
             w2_bf = placed([P, H, PACK], BF16, f"w2_bf{e}", grouped_at(e))
-            nc.scalar.copy(packed_view(w2_bf[:]), planes_view(w2_raw[e][:]))
+            for cols in (slice(0, H // 2), slice(H // 2, H)) if e == 0 else (slice(0, H),):
+                nc.scalar.copy(packed_view(w2_bf[:, cols, :]), planes_view(w2_raw[e][:, :, cols]))
             nc.vector.quantize_mx(out=w2_w[e][:].bitcast(E4M3), scales=w2_s[e][:], in_=w2_bf[:].rearrange("p i t -> p (i t)"))
 
         def first_product(e, s):
@@ -150,7 +160,7 @@ def tile_moe_bdx_mlp_relu_kernel(tc, dy_words, dy_scales, a, w2, w1, gate, offs,
                     nc.tensor.transpose(bank[:, at : at + P], pairs[:, u * P : (u + 1) * P], ident[:])
 
         def quantise_da(e):
-            mask = placed([P, C, PACK], BF16, f"mask{e}", grouped_at(min(e + 1, E - 1)))
+            mask = placed([P, C, PACK], BF16, f"mask{e}", grouped_at(MASK_ON[e]))
             nc.vector.tensor_scalar(packed_view(mask[:]), planes_view(a_raw[e][:]), 0.0, None, IS_GT)
             da_bf = placed([P, C, PACK], BF16, f"da_bf{e}", da_at(e))
             for half in range(2):
@@ -164,9 +174,9 @@ def tile_moe_bdx_mlp_relu_kernel(tc, dy_words, dy_scales, a, w2, w1, gate, offs,
             nc.vector.quantize_mx(out=da_w[e][:].bitcast(E5M2), scales=da_s[e][:], in_=da_bf[:].rearrange("p n t -> p (n t)"))
 
         def quantise_w1_low(e):
-            w1_bf = placed([P, P, PACK], BF16, f"w1_bf{e}", rounded_at(e, 1))
+            w1_bf = placed([P, P, PACK], BF16, f"w1_bf{e}", rounded_at(*W1_LOW_ON[e]))
             nc.scalar.copy(packed_view(w1_bf[:]), planes_view(w1_raw[e][:, :, 0:P]))
-            w1_w = keep.tile([P, P], U32, name=f"w1_w{e}", align_bytes=64)
+            w1_w = placed([P, P], U32, f"w1_w{e}", LATE_AT if e == E - 1 else SPARE + 29 * KIB + e * KIB // 2)
             w1_s = keep.tile([P, P], U8, name=f"w1_s{e}", align_bytes=64)
             nc.vector.quantize_mx(out=w1_w[:].bitcast(E4M3), scales=w1_s[:], in_=w1_bf[:].rearrange("p k t -> p (k t)"))
             w1_low[e] = (w1_w[:], w1_s[:])
@@ -179,47 +189,61 @@ def tile_moe_bdx_mlp_relu_kernel(tc, dy_words, dy_scales, a, w2, w1, gate, offs,
             nc.scalar.copy(dx[h][:, e * C : (e + 1) * C], bank[:])
 
         gather(0)
-        gather(1)
         quantise_w2(0)
+        gather(1)
+        gather(2)
         for s in range(4):
             first_product(0, s)
         for e in range(E):
             if e + 1 < E:
                 quantise_w2(e + 1)
-            if e + 2 < E:
-                gather(e + 2)
+            if e + 3 < E:
+                gather(e + 3)
             for s in range(4):
                 gate_and_round(e, s)
                 if s % 2 == 1:
                     turn(e, s // 2)
-                if s == 1 and e > 0:
-                    second_product(e - 1, 0, *w1_low[e - 1], sums[1])
                 if e + 1 < E:
                     first_product(e + 1, s)
-            quantise_da(e)
-            quantise_w1_low(e)
-
-        second_product(E - 1, 0, *w1_low[E - 1], sums[0])
-
-        high_bf = placed([P, E * P, PACK], BF16, "high_bf", LAST_ROUNDED_AT[0])
+            if e >= 1:
+                quantise_da(e - 1)
+            if 1 <= e <= 3:
+                quantise_w1_low(e - 1)
+        quantise_w1_low(3)
+        quantise_da(E - 1)
+        quantise_w1_low(4)
         for e in range(E):
-            nc.scalar.copy(packed_view(high_bf[:, e * P : (e + 1) * P, :]), planes_view(w1_raw[e][:, :, P:K]))
+            second_product(e, 0, *w1_low[e], sums[(e + 2) % 4])
+
         high_w = placed([P, E * P], U32, "high_w", da_at(E - 1))
         high_s = placed([P, E * P], U8, "high_s", da_at(E - 1) + 5 * KIB // 2)
-        for cols in (slice(0, 4 * P), slice(4 * P, E * P)):
-            nc.vector.quantize_mx(out=high_w[:, cols].bitcast(E4M3), scales=high_s[:, cols], in_=high_bf[:, cols, :].rearrange("p k t -> p (k t)"))
+        for lo, hi, at in ((0, 2, rounded_at(3, 2)), (2, E, LATE_AT)):
+            high_bf = placed([P, (hi - lo) * P, PACK], BF16, f"high_bf{lo}", at)
+            for e in range(lo, hi):
+                nc.scalar.copy(packed_view(high_bf[:, (e - lo) * P : (e - lo + 1) * P, :]), planes_view(w1_raw[e][:, :, P:K]))
+            for e in range(lo, hi, 2):
+                n = min(2, hi - e) * P
+                cols = slice(e * P, e * P + n)
+                nc.vector.quantize_mx(
+                    out=high_w[:, cols].bitcast(E4M3), scales=high_s[:, cols],
+                    in_=high_bf[:, (e - lo) * P : (e - lo) * P + n, :].rearrange("p k t -> p (k t)"),
+                )
         for e in range(E):
             cols = slice(e * P, (e + 1) * P)
-            second_product(e, 1, high_w[:, cols], high_s[:, cols], sums[(e + 1) % 4])
+            second_product(e, 1, high_w[:, cols], high_s[:, cols], sums[(e + 3) % 4])
 
         for h in range(K // P):
             cuts = TOKEN_CUTS[h]
             for j in range(len(cuts) - 1):
                 lo, hi = cuts[j], cuts[j + 1]
                 first = ring.tile([P, hi - lo], F32, name="first")
-                second = ring.tile([P, hi - lo], F32, name="second")
+                if h == 0:
+                    second = placed([P, hi - lo], F32, f"second_late{j}", LATE_AT - 2 * KIB + j * 5 * KIB // 2)
+                else:
+                    second = ring.tile([P, hi - lo], F32, name="second")
                 total = keep.tile([P, hi - lo], F32, name=f"total{h}_{j}")
                 nc.vector.tensor_copy(first[:], dx[h][:].indirect(pos1_sb[:, lo // LIST : hi // LIST]))
                 nc.vector.tensor_copy(second[:], dx[h][:].indirect(pos2_sb[:, lo // LIST : hi // LIST]))
-                nc.vector.tensor_tensor(total[:], first[:], second[:], ADD)
+                adder = nc.vector if (h, hi) == (K // P - 1, T) else nc.gpsimd
+                adder.tensor_tensor(total[:], first[:], second[:], ADD)
                 nc.sync.dma_start(out[h * P : (h + 1) * P, lo:hi], total[:])

@@ -30,7 +30,7 @@ KIB = 1024
 REGION = 19 * KIB // 2
 ROUNDED_AT = (0, KIB, 2 * KIB, 11 * KIB // 2)
 ROUNDED_REGION = (1, 2, 3, 4, 0)
-MASK_ON = (1, 3, 4, 3, 4)
+MASK_ON = (1, 2, 3, 2, 3)
 W1_LOW_ON = ((0, 0), (1, 0), (2, 0), (4, 0), (4, 1))
 LATE_AT = 3 * REGION + 13 * KIB // 2
 GATHERED_AT = 3 * KIB
@@ -66,7 +66,7 @@ def tile_moe_bdx_mlp_relu_kernel(tc, dy_words, dy_scales, a, w2, w1, gate, offs,
         gate_cols = keep.tile([P, S // P], F32, name="gate_cols")
         ident = keep.tile([P, P], F32, name="ident")
         w2_raw = [placed([P, PACK, H], F32, f"w2_raw{e}", e * REGION) for e in range(E)]
-        w1_raw = [keep.tile([P, PACK, K], F32, name=f"w1_raw{e}") for e in range(E)]
+        w1_raw = [[keep.tile([P, PACK, P], F32, name=f"w1_raw{e}_{h}") for h in range(K // P)] for e in range(E)]
         a_raw = [keep.tile([P, PACK, C], F32, name=f"a_raw{e}") for e in range(E)]
         w2_w = [keep.tile([P, H], U32, name=f"w2_w{e}", align_bytes=64) for e in range(E)]
         w2_s = [keep.tile([P, H], U8, name=f"w2_s{e}", align_bytes=64) for e in range(E)]
@@ -92,15 +92,23 @@ def tile_moe_bdx_mlp_relu_kernel(tc, dy_words, dy_scales, a, w2, w1, gate, offs,
             nc.sync.dma_start(dy_s[32 * q : 32 * q + 4, :].bitcast(I32), dy_scales[0, 4 * q : 4 * q + 4, :].bitcast(I32))
         nc.sync.dma_start(dy_w[:].bitcast(I32), dy_words[0].rearrange("p t d -> p (t d)").bitcast(I32))
         load_w2(nc.sync, 0, slice(H // 2, H))
-        for e in range(E + 1):
-            if e + 1 < E:
-                load_w2(nc.sync, e + 1)
-            if e >= 1:
-                nc.sync.dma_start(w1_raw[e - 1][:], w1[e - 1].rearrange("(p t) k -> p t k", t=PACK))
-            if e < E:
-                nc.sync.dma_start(a_raw[e][:], a_rows[:, :, e * C : (e + 1) * C])
+
+        def load_w1(e, h):
+            nc.sync.dma_start(w1_raw[e][h][:], w1[e].rearrange("(p t) k -> p t k", t=PACK)[:, :, h * P : (h + 1) * P])
+
+        load_w2(nc.sync, 1)
+        for e in range(E):
+            if e + 2 < E:
+                load_w2(nc.sync, e + 2)
+            else:
+                load_w1(e + 2 - E, 0)
+            nc.sync.dma_start(a_raw[e][:], a_rows[:, :, e * C : (e + 1) * C])
+        for e in range(2, E):
+            load_w1(e, 0)
         nc.sync.dma_start(pos1_sb[:], pos1)
         nc.sync.dma_start(pos2_sb[:], pos2)
+        for e in range(E):
+            load_w1(e, 1)
 
         nc.tensor.transpose(turned[3][:, 0:P], gate_rows[:], ident[:])
         nc.vector.tensor_copy(gate_cols[:], turned[3][:, 0 : S // P])
@@ -175,7 +183,7 @@ def tile_moe_bdx_mlp_relu_kernel(tc, dy_words, dy_scales, a, w2, w1, gate, offs,
 
         def quantise_w1_low(e):
             w1_bf = placed([P, P, PACK], BF16, f"w1_bf{e}", rounded_at(*W1_LOW_ON[e]))
-            nc.scalar.copy(packed_view(w1_bf[:]), planes_view(w1_raw[e][:, :, 0:P]))
+            nc.scalar.copy(packed_view(w1_bf[:]), planes_view(w1_raw[e][0][:]))
             w1_w = placed([P, P], U32, f"w1_w{e}", LATE_AT if e == E - 1 else SPARE + 29 * KIB + e * KIB // 2)
             w1_s = keep.tile([P, P], U8, name=f"w1_s{e}", align_bytes=64)
             nc.vector.quantize_mx(out=w1_w[:].bitcast(E4M3), scales=w1_s[:], in_=w1_bf[:].rearrange("p k t -> p (k t)"))
@@ -220,7 +228,7 @@ def tile_moe_bdx_mlp_relu_kernel(tc, dy_words, dy_scales, a, w2, w1, gate, offs,
         for lo, hi, at in ((0, 2, rounded_at(3, 2)), (2, E, LATE_AT)):
             high_bf = placed([P, (hi - lo) * P, PACK], BF16, f"high_bf{lo}", at)
             for e in range(lo, hi):
-                nc.scalar.copy(packed_view(high_bf[:, (e - lo) * P : (e - lo + 1) * P, :]), planes_view(w1_raw[e][:, :, P:K]))
+                nc.scalar.copy(packed_view(high_bf[:, (e - lo) * P : (e - lo + 1) * P, :]), planes_view(w1_raw[e][1][:]))
             for e in range(lo, hi, 2):
                 n = min(2, hi - e) * P
                 cols = slice(e * P, e * P + n)

@@ -30,7 +30,6 @@ KIB = 1024
 REGION = 19 * KIB // 2
 ROUNDED_AT = (0, KIB, 2 * KIB, 11 * KIB // 2)
 ROUNDED_REGION = (1, 2, 3, 4, 0)
-MASK_ON = (1, 2, 3, 2, 3)
 W1_LOW_ON = ((0, 0), (1, 0), (2, 0), (4, 0), (4, 1))
 LATE_AT = 3 * REGION + 13 * KIB // 2
 GATHERED_AT = 3 * KIB
@@ -96,13 +95,18 @@ def tile_moe_bdx_mlp_relu_kernel(tc, dy_words, dy_scales, a, w2, w1, gate, offs,
         def load_w1(e, h):
             nc.sync.dma_start(w1_raw[e][h][:], w1[e].rearrange("(p t) k -> p t k", t=PACK)[:, :, h * P : (h + 1) * P])
 
-        load_w2(nc.sync, 1)
-        for e in range(E):
-            if e + 2 < E:
-                load_w2(nc.sync, e + 2)
-            else:
-                load_w1(e + 2 - E, 0)
+        def load_a(e):
             nc.sync.dma_start(a_raw[e][:], a_rows[:, :, e * C : (e + 1) * C])
+
+        for e in (0, 2):
+            load_w2(nc.sync, e + 1)
+            load_w2(nc.sync, e + 2)
+            load_a(e)
+            if e == 2:
+                load_w1(0, 0)
+            load_a(e + 1)
+        load_w1(1, 0)
+        load_a(E - 1)
         for e in range(2, E):
             load_w1(e, 0)
         nc.sync.dma_start(pos1_sb[:], pos1)
@@ -123,11 +127,16 @@ def tile_moe_bdx_mlp_relu_kernel(tc, dy_words, dy_scales, a, w2, w1, gate, offs,
         def rounded_at(e, s):
             return ROUNDED_REGION[e] * REGION + ROUNDED_AT[s]
 
+        def mask_at(e):
+            if e % 2 == 1:
+                return grouped_at(2) + 2 * KIB
+            return grouped_at(2) - 2 * KIB if e == 0 else grouped_at(4)
+
         def da_at(e):
-            return SPARE + (3 + e % 2) * 4 * KIB
+            return SPARE + 14 * KIB + (e % 2) * 4 * KIB
 
         def gather(e):
-            at = SPARE + 20 * KIB + e * 3 * KIB if e < 3 else (e - 2) * REGION + GATHERED_AT
+            at = SPARE + 22 * KIB + e * 3 * KIB if e < 3 else (e - 2) * REGION + GATHERED_AT
             slots = offs_sb[:, e * C // LIST : (e + 1) * C // LIST]
             g_w = placed([P, C], U32, f"g_w{e}", grouped_at(0) + (e - 1) * 2 * KIB if e in (1, 2) else at)
             g_s = placed([P, C], U8, f"g_s{e}", at + 2 * KIB)
@@ -168,7 +177,7 @@ def tile_moe_bdx_mlp_relu_kernel(tc, dy_words, dy_scales, a, w2, w1, gate, offs,
                     nc.tensor.transpose(bank[:, at : at + P], pairs[:, u * P : (u + 1) * P], ident[:])
 
         def quantise_da(e):
-            mask = placed([P, C, PACK], BF16, f"mask{e}", grouped_at(MASK_ON[e]))
+            mask = placed([P, C, PACK], BF16, f"mask{e}", mask_at(e))
             nc.vector.tensor_scalar(packed_view(mask[:]), planes_view(a_raw[e][:]), 0.0, None, IS_GT)
             da_bf = placed([P, C, PACK], BF16, f"da_bf{e}", da_at(e))
             for half in range(2):
@@ -184,7 +193,7 @@ def tile_moe_bdx_mlp_relu_kernel(tc, dy_words, dy_scales, a, w2, w1, gate, offs,
         def quantise_w1_low(e):
             w1_bf = placed([P, P, PACK], BF16, f"w1_bf{e}", rounded_at(*W1_LOW_ON[e]))
             nc.scalar.copy(packed_view(w1_bf[:]), planes_view(w1_raw[e][0][:]))
-            w1_w = placed([P, P], U32, f"w1_w{e}", LATE_AT if e == E - 1 else SPARE + 29 * KIB + e * KIB // 2)
+            w1_w = placed([P, P], U32, f"w1_w{e}", LATE_AT if e == E - 1 else SPARE + 31 * KIB + e * KIB // 2)
             w1_s = keep.tile([P, P], U8, name=f"w1_s{e}", align_bytes=64)
             nc.vector.quantize_mx(out=w1_w[:].bitcast(E4M3), scales=w1_s[:], in_=w1_bf[:].rearrange("p k t -> p (k t)"))
             w1_low[e] = (w1_w[:], w1_s[:])

@@ -27,14 +27,14 @@ PACK = 4
 LIST = 16
 HALF = C // 2
 KIB = 1024
-REGION = 19 * KIB // 2
-ROUNDED_AT = (0, KIB, 2 * KIB, 11 * KIB // 2)
-ROUNDED_REGION = (1, 2, 3, 4, 0)
-W1_LOW_ON = ((0, 0), (1, 0), (2, 0), (4, 0), (4, 1))
-LATE_AT = 3 * REGION + 13 * KIB // 2
-GATHERED_AT = 3 * KIB
-SPARE = E * REGION
-TOKEN_CUTS = ((0, 640, 1280), (0, 640, 960, 1280))
+
+RAW2_AT = tuple(8 * KIB * e for e in range(E))
+CAST_A = 40 * KIB
+CAST_B = 44 * KIB
+ROUNDED_AT = (48 * KIB, 52 * KIB, 48 * KIB, 56 * KIB, 48 * KIB)
+DA_AT = (60 * KIB, 64 * KIB)
+LAST_RAW_AT = 70 * KIB
+LAST_WORDS_AT = 74 * KIB
 
 
 def planes_view(raw):
@@ -45,121 +45,121 @@ def packed_view(grouped):
     return grouped.rearrange("p (c i) t -> p c t i", i=4)
 
 
+def flat(grouped):
+    return grouped.rearrange("p n t -> p (n t)")
+
+
 def tile_moe_bdx_mlp_relu_kernel(tc, dy_words, dy_scales, a, w2, w1, gate, offs, pos1, pos2, out):
     nc = tc.nc
     with ExitStack() as ctx:
         keep = ctx.enter_context(tc.tile_pool(name="keep", bufs=1))
         arena = ctx.enter_context(tc.tile_pool(name="arena", bufs=1))
-        ring = ctx.enter_context(tc.tile_pool(name="ring", bufs=2))
         psum = ctx.enter_context(tc.psum_pool(name="psum", bufs=1))
 
         def placed(shape, dtype, name, offset):
             return arena.tile(shape, dtype, name=name, offset=offset, align_bytes=64)
 
+        def kept(shape, dtype, name):
+            return keep.tile(shape, dtype, name=name, align_bytes=64)
+
         offs_sb = keep.tile([P, S // LIST], U16, name="offs_sb")
-        pos1_sb = keep.tile([P, T // LIST], U16, name="pos1_sb")
-        pos2_sb = keep.tile([P, T // LIST], U16, name="pos2_sb")
-        dy_w = keep.tile([P, T], U32, name="dy_w", align_bytes=64)
-        dy_s = keep.tile([P, T], U8, name="dy_s", align_bytes=64)
-        gate_rows = keep.tile([P, P], F32, name="gate_rows")
-        gate_cols = keep.tile([P, S // P], F32, name="gate_cols")
-        ident = keep.tile([P, P], F32, name="ident")
-        w2_raw = [placed([P, PACK, H], F32, f"w2_raw{e}", e * REGION) for e in range(E)]
-        w1_raw = [[keep.tile([P, PACK, P], F32, name=f"w1_raw{e}_{h}") for h in range(K // P)] for e in range(E)]
-        a_raw = [keep.tile([P, PACK, C], F32, name=f"a_raw{e}") for e in range(E)]
-        w2_w = [keep.tile([P, H], U32, name=f"w2_w{e}", align_bytes=64) for e in range(E)]
-        w2_s = [keep.tile([P, H], U8, name=f"w2_s{e}", align_bytes=64) for e in range(E)]
-        da_w = [keep.tile([P, C], U32, name=f"da_w{e}", align_bytes=64) for e in range(E)]
-        da_s = [keep.tile([P, C], U8, name=f"da_s{e}", align_bytes=64) for e in range(E)]
-        dx = [keep.tile([P, S], F32, name=f"dx{h}") for h in range(K // P)]
+        pos_sb = [keep.tile([P, T // LIST], U16, name=f"pos{r}_sb") for r in (1, 2)]
+        dy_w = kept([P, T], U32, "dy_w")
+        dy_s = kept([P, T], U8, "dy_s")
+        gate_rows = kept([P, P], F32, "gate_rows")
+        gate_cols = kept([P, S // P], F32, "gate_cols")
+        ident = kept([P, P], F32, "ident")
+        w2_first = [placed([P, PACK, H // 2], F32, f"w2_first{j}", RAW2_AT[0] + j * 4 * KIB) for j in range(2)]
+        w2_raw = {e: placed([P, PACK, H], F32, f"w2_raw{e}", RAW2_AT[e]) for e in range(1, E)}
+        w1_raw = {(e, h): kept([P, PACK, P], F32, f"w1_raw{e}_{h}") for e in range(E) for h in range(2) if (e, h) != (E - 1, 1)}
+        w1_raw[E - 1, 1] = placed([P, PACK, P], F32, "w1_raw_last", LAST_RAW_AT)
+        a_raw = [kept([P, PACK, C], F32, f"a_raw{e}") for e in range(E)]
+        da_w = [kept([P, C], U32, f"da_w{e}") for e in range(E)]
+        da_s = [kept([P, C], U8, f"da_s{e}") for e in range(E)]
+        dx = [kept([P, S], F32, f"dx{h}") for h in range(K // P)]
         sums = [psum.tile([P, C], F32, name=f"sums{b}") for b in range(4)]
         turned = [psum.tile([P, C], F32, name=f"turned{b}") for b in range(4)]
 
         nc.gpsimd.memset(dy_s[:].bitcast(I32), 0)
-        nc.vector.memset(gate_rows[:], 0.0)
+        nc.gpsimd.memset(gate_rows[:], 0.0)
         make_identity(nc, ident[:])
 
         a_rows = a.rearrange("(p t) s -> p t s", t=PACK)
 
-        def load_w2(queue, e, cols=slice(0, H)):
-            queue.dma_start(w2_raw[e][:, :, cols], w2[e].rearrange("(p t) i -> p t i", t=PACK)[:, :, cols])
-
-        load_w2(nc.scalar, 0, slice(0, H // 2))
-        nc.scalar.dma_start(gate_rows[0 : S // P, :], gate[0].rearrange("(c p) -> c p", p=P))
-        nc.sync.dma_start(offs_sb[:], offs)
-        for q in range(4):
-            nc.sync.dma_start(dy_s[32 * q : 32 * q + 4, :].bitcast(I32), dy_scales[0, 4 * q : 4 * q + 4, :].bitcast(I32))
-        nc.sync.dma_start(dy_w[:].bitcast(I32), dy_words[0].rearrange("p t d -> p (t d)").bitcast(I32))
-        load_w2(nc.sync, 0, slice(H // 2, H))
+        def w2_rows(e):
+            return w2[e].rearrange("(p t) i -> p t i", t=PACK)
 
         def load_w1(e, h):
-            nc.sync.dma_start(w1_raw[e][h][:], w1[e].rearrange("(p t) k -> p t k", t=PACK)[:, :, h * P : (h + 1) * P])
+            nc.sync.dma_start(w1_raw[e, h][:], w1[e].rearrange("(p t) k -> p t k", t=PACK)[:, :, h * P : (h + 1) * P])
 
         def load_a(e):
             nc.sync.dma_start(a_raw[e][:], a_rows[:, :, e * C : (e + 1) * C])
 
-        for e in (0, 2):
-            load_w2(nc.sync, e + 1)
-            load_w2(nc.sync, e + 2)
+        nc.scalar.dma_start(gate_rows[0 : S // P, :], gate[0].rearrange("(c p) -> c p", p=P))
+        nc.sync.dma_start(offs_sb[:], offs)
+        for q in range(4):
+            nc.sync.dma_start(dy_s[32 * q : 32 * q + 4, :].bitcast(I32), dy_scales[0, 4 * q : 4 * q + 4, :].bitcast(I32))
+        nc.sync.dma_start(w2_first[0][:], w2_rows(0)[:, :, : H // 2])
+        nc.sync.dma_start(dy_w[:].bitcast(I32), dy_words[0].rearrange("p t d -> p (t d)").bitcast(I32))
+        nc.sync.dma_start(w2_first[1][:], w2_rows(0)[:, :, H // 2 :])
+        for e in (1, 2, 3):
+            nc.sync.dma_start(w2_raw[e][:], w2_rows(e))
+        load_a(0)
+        nc.sync.dma_start(w2_raw[4][:], w2_rows(4))
+        for e in (1, 2, 3):
             load_a(e)
-            if e == 2:
-                load_w1(0, 0)
-            load_a(e + 1)
-        load_w1(1, 0)
-        load_a(E - 1)
-        for e in range(2, E):
+        for e in range(E - 1):
             load_w1(e, 0)
-        nc.sync.dma_start(pos1_sb[:], pos1)
-        nc.sync.dma_start(pos2_sb[:], pos2)
+        load_a(E - 1)
+        load_w1(E - 1, 0)
+        nc.sync.dma_start(pos_sb[0][:], pos1)
+        nc.sync.dma_start(pos_sb[1][:], pos2)
         for e in range(E):
             load_w1(e, 1)
 
         nc.tensor.transpose(turned[3][:, 0:P], gate_rows[:], ident[:])
-        nc.vector.tensor_copy(gate_cols[:], turned[3][:, 0 : S // P])
+        nc.scalar.copy(gate_cols[:], turned[3][:, 0 : S // P])
 
-        gathered = {}
-        rounded = {}
-        w1_low = {}
+        g_w, g_s, w2_bf, w2_q, rounded, mask, da_bf, w1_q = {}, {}, {}, {}, {}, {}, {}, {}
 
-        def grouped_at(e):
-            return SPARE + e * 4 * KIB if e < 3 else rounded_at(e - 3, 3)
+        def slots(e):
+            return offs_sb[:, e * C // LIST : (e + 1) * C // LIST]
 
-        def rounded_at(e, s):
-            return ROUNDED_REGION[e] * REGION + ROUNDED_AT[s]
+        def gather_scales(e, at=None):
+            g_s[e] = kept([P, C], U8, f"g_s{e}") if at is None else placed([P, C], U8, f"g_s{e}", at)
+            nc.vector.tensor_copy(g_s[e][:], dy_s[:].indirect(slots(e)))
 
-        def mask_at(e):
-            if e % 2 == 1:
-                return grouped_at(2) + 2 * KIB
-            return grouped_at(2) - 2 * KIB if e == 0 else grouped_at(4)
+        def gather_words(e, at=None):
+            g_w[e] = kept([P, C], U32, f"g_w{e}") if at is None else placed([P, C], U32, f"g_w{e}", at)
+            nc.vector.tensor_copy(g_w[e][:], dy_w[:].indirect(slots(e)))
 
-        def da_at(e):
-            return SPARE + 14 * KIB + (e % 2) * 4 * KIB
+        def round_w2_on_scalar(e, at):
+            w2_bf[e] = placed([P, H, PACK], BF16, f"w2_bf{e}", at)
+            if e == 0:
+                for j in range(2):
+                    nc.scalar.copy(packed_view(w2_bf[e][:, j * H // 2 : (j + 1) * H // 2, :]), planes_view(w2_first[j][:]))
+            else:
+                nc.scalar.copy(packed_view(w2_bf[e][:]), planes_view(w2_raw[e][:]))
 
-        def gather(e):
-            at = SPARE + 22 * KIB + e * 3 * KIB if e < 3 else (e - 2) * REGION + GATHERED_AT
-            slots = offs_sb[:, e * C // LIST : (e + 1) * C // LIST]
-            g_w = placed([P, C], U32, f"g_w{e}", grouped_at(0) + (e - 1) * 2 * KIB if e in (1, 2) else at)
-            g_s = placed([P, C], U8, f"g_s{e}", at + 2 * KIB)
-            nc.vector.tensor_copy(g_s[:], dy_s[:].indirect(slots))
-            nc.vector.tensor_copy(g_w[:], dy_w[:].indirect(slots))
-            gathered[e] = (g_w, g_s)
+        def round_w2_on_gpsimd(e, at):
+            w2_bf[e] = placed([P, H, PACK], BF16, f"w2_bf{e}", at)
+            nc.gpsimd.tensor_scalar(w2_bf[e][:], w2_raw[e][:].rearrange("p t i -> p i t"), 1.0, 0.0, MULT, ADD)
 
-        def quantise_w2(e):
-            w2_bf = placed([P, H, PACK], BF16, f"w2_bf{e}", grouped_at(e))
-            for cols in (slice(0, H // 2), slice(H // 2, H)) if e == 0 else (slice(0, H),):
-                nc.scalar.copy(packed_view(w2_bf[:, cols, :]), planes_view(w2_raw[e][:, :, cols]))
-            nc.vector.quantize_mx(out=w2_w[e][:].bitcast(E4M3), scales=w2_s[e][:], in_=w2_bf[:].rearrange("p i t -> p (i t)"))
+        def quantise_w2(e, at=None):
+            words = kept([P, H], U32, f"w2_w{e}") if at is None else placed([P, H], U32, f"w2_w{e}", at)
+            scales = kept([P, H], U8, f"w2_s{e}")
+            nc.vector.quantize_mx(out=words[:].bitcast(E4M3), scales=scales[:], in_=flat(w2_bf[e][:]))
+            w2_q[e] = (words, scales)
 
         def first_product(e, s):
-            g_w, g_s = gathered[e]
             cols = slice(s * P, (s + 1) * P)
             nc.tensor.matmul_mx(
-                out=sums[s][:], lhsT=g_w[:, cols].bitcast(E5M2), lhsT_scale=g_s[:, cols],
-                rhs=w2_w[e][:].bitcast(E4M3), rhs_scale=w2_s[e][:], start=True, stop=True,
+                out=sums[s][:], lhsT=g_w[e][:, cols].bitcast(E5M2), lhsT_scale=g_s[e][:, cols],
+                rhs=w2_q[e][0][:].bitcast(E4M3), rhs_scale=w2_q[e][1][:], start=True, stop=True,
             )
 
         def gate_and_round(e, s):
-            dh_bf = placed([P, H], BF16, f"dh_bf{e}_{s}", rounded_at(e, s))
+            dh_bf = placed([P, H], BF16, f"dh_bf{e}_{s}", ROUNDED_AT[e] + s * KIB)
             col = e * (C // P) + s
             nc.scalar.activation(
                 dh_bf[:].rearrange("s (u p x) -> s u p x", u=2, x=2),
@@ -176,91 +176,135 @@ def tile_moe_bdx_mlp_relu_kernel(tc, dy_words, dy_scales, a, w2, w1, gate, offs,
                     at = u * HALF + s * P
                     nc.tensor.transpose(bank[:, at : at + P], pairs[:, u * P : (u + 1) * P], ident[:])
 
-        def quantise_da(e):
-            mask = placed([P, C, PACK], BF16, f"mask{e}", mask_at(e))
-            nc.vector.tensor_scalar(packed_view(mask[:]), planes_view(a_raw[e][:]), 0.0, None, IS_GT)
-            da_bf = placed([P, C, PACK], BF16, f"da_bf{e}", da_at(e))
+        def empty_sums(e, refill):
+            for s in range(4):
+                gate_and_round(e, s)
+                if refill:
+                    first_product(e + 1, s)
+                if s % 2 == 1:
+                    turn(e, s // 2)
+
+        def make_mask(e):
+            mask[e] = placed([P, C, PACK], BF16, f"mask{e}", RAW2_AT[3] if e % 2 == 0 else CAST_A)
+            nc.vector.tensor_scalar(packed_view(mask[e][:]), planes_view(a_raw[e][:]), 0.0, None, IS_GT)
+
+        def apply_mask(e):
+            da_bf[e] = placed([P, C, PACK], BF16, f"da_bf{e}", DA_AT[e % 2])
             for half in range(2):
                 cols = slice(half * HALF, (half + 1) * HALF)
                 nc.vector.tensor_tensor(
-                    da_bf[:, cols, :].rearrange("p n (u x) -> p n u x", u=2),
+                    da_bf[e][:, cols, :].rearrange("p n (u x) -> p n u x", u=2),
                     turned[2 * (e % 2) + half][:].bitcast(BF16).rearrange("p (u n x) -> p n u x", u=2, x=2),
-                    mask[:, cols, :].rearrange("p n (u x) -> p n u x", u=2),
+                    mask[e][:, cols, :].rearrange("p n (u x) -> p n u x", u=2),
                     MULT,
                 )
-            nc.vector.quantize_mx(out=da_w[e][:].bitcast(E5M2), scales=da_s[e][:], in_=da_bf[:].rearrange("p n t -> p (n t)"))
 
-        def quantise_w1_low(e):
-            w1_bf = placed([P, P, PACK], BF16, f"w1_bf{e}", rounded_at(*W1_LOW_ON[e]))
-            nc.scalar.copy(packed_view(w1_bf[:]), planes_view(w1_raw[e][0][:]))
-            w1_w = placed([P, P], U32, f"w1_w{e}", LATE_AT if e == E - 1 else SPARE + 31 * KIB + e * KIB // 2)
-            w1_s = keep.tile([P, P], U8, name=f"w1_s{e}", align_bytes=64)
-            nc.vector.quantize_mx(out=w1_w[:].bitcast(E4M3), scales=w1_s[:], in_=w1_bf[:].rearrange("p k t -> p (k t)"))
-            w1_low[e] = (w1_w[:], w1_s[:])
+        def quantise_da(e, cols=slice(0, C)):
+            nc.vector.quantize_mx(out=da_w[e][:, cols].bitcast(E5M2), scales=da_s[e][:, cols], in_=flat(da_bf[e][:, cols, :]))
 
-        def second_product(e, h, w1_w, w1_s, bank):
+        def round_w1(lo, hi, h, at=None):
+            shape, name = [P, (hi - lo) * P, PACK], f"w1_bf{lo}_{h}"
+            grouped = kept(shape, BF16, name) if at is None else placed(shape, BF16, name, at)
+            for e in range(lo, hi):
+                nc.scalar.copy(packed_view(grouped[:, (e - lo) * P : (e - lo + 1) * P, :]), planes_view(w1_raw[e, h][:]))
+            return grouped
+
+        def quantise_w1(lo, hi, h, grouped, at=None):
+            shape, name = [P, (hi - lo) * P], f"w1_w{lo}_{h}"
+            words = kept(shape, U32, name) if at is None else placed(shape, U32, name, at)
+            scales = kept(shape, U8, f"w1_s{lo}_{h}")
+            nc.vector.quantize_mx(out=words[:].bitcast(E4M3), scales=scales[:], in_=flat(grouped))
+            for e in range(lo, hi):
+                cols = slice((e - lo) * P, (e - lo + 1) * P)
+                w1_q[e, h] = (words[:, cols], scales[:, cols])
+
+        def second_product(e, h):
+            bank = (sums, turned)[h][e % 4]
             nc.tensor.matmul_mx(
-                out=bank[:], lhsT=w1_w.bitcast(E4M3), lhsT_scale=w1_s,
+                out=bank[:], lhsT=w1_q[e, h][0].bitcast(E4M3), lhsT_scale=w1_q[e, h][1],
                 rhs=da_w[e][:].bitcast(E5M2), rhs_scale=da_s[e][:], start=True, stop=True,
             )
             nc.scalar.copy(dx[h][:, e * C : (e + 1) * C], bank[:])
 
-        gather(0)
+        gather_scales(0)
+        gather_scales(1)
+        gather_words(0)
+        gather_words(1)
+        round_w2_on_scalar(0, CAST_A)
         quantise_w2(0)
-        gather(1)
-        gather(2)
+        round_w2_on_gpsimd(1, CAST_A)
+        gather_scales(2, RAW2_AT[0] + 4 * KIB)
+        gather_words(2, RAW2_AT[0] + 5 * KIB)
+        gather_scales(3, RAW2_AT[0] + 7 * KIB)
         for s in range(4):
             first_product(0, s)
+        empty_sums(0, False)
+        round_w2_on_scalar(2, CAST_B)
+        quantise_w2(1)
+        round_w2_on_gpsimd(3, CAST_A)
+        gather_words(3, RAW2_AT[1])
+        gather_scales(4, RAW2_AT[1] + 2 * KIB)
+        gather_words(4, RAW2_AT[1] + 3 * KIB)
+        for s in range(4):
+            first_product(1, s)
+        empty_sums(1, False)
+        quantise_w2(2, RAW2_AT[3] + 4 * KIB)
+        make_mask(0)
+        quantise_w2(3)
+        for s in range(4):
+            first_product(2, s)
+        apply_mask(0)
+        make_mask(1)
+        quantise_da(0)
+        empty_sums(2, True)
+        round_w2_on_scalar(4, ROUNDED_AT[1])
+        apply_mask(1)
+        quantise_w2(4)
+        make_mask(2)
+        quantise_da(1)
+        empty_sums(3, True)
+        apply_mask(2)
+        make_mask(3)
+        quantise_da(2)
+        empty_sums(4, False)
+        low01 = round_w1(0, 2, 0)
+        low23 = round_w1(2, 4, 0)
+        low4 = round_w1(4, 5, 0)
+        apply_mask(3)
+        quantise_w1(0, 2, 0, low01[:])
+        make_mask(4)
+        quantise_da(3)
+        quantise_w1(2, 4, 0, low23[:])
+        apply_mask(4)
+        quantise_da(4, slice(0, HALF))
+        quantise_w1(4, 5, 0, low4[:], LAST_WORDS_AT)
+        quantise_da(4, slice(HALF, C))
         for e in range(E):
-            if e + 1 < E:
-                quantise_w2(e + 1)
-            if e + 3 < E:
-                gather(e + 3)
-            for s in range(4):
-                gate_and_round(e, s)
-                if s % 2 == 1:
-                    turn(e, s // 2)
-                if e + 1 < E:
-                    first_product(e + 1, s)
-            if e >= 1:
-                quantise_da(e - 1)
-            if 1 <= e <= 3:
-                quantise_w1_low(e - 1)
-        quantise_w1_low(3)
-        quantise_da(E - 1)
-        quantise_w1_low(4)
-        for e in range(E):
-            second_product(e, 0, *w1_low[e], sums[(e + 2) % 4])
+            second_product(e, 0)
+        high01 = round_w1(0, 2, 1)
+        quantise_w1(0, 2, 1, high01[:], DA_AT[0])
+        high234 = round_w1(2, 5, 1, LAST_WORDS_AT)
 
-        high_w = placed([P, E * P], U32, "high_w", da_at(E - 1))
-        high_s = placed([P, E * P], U8, "high_s", da_at(E - 1) + 5 * KIB // 2)
-        for lo, hi, at in ((0, 2, rounded_at(3, 2)), (2, E, LATE_AT)):
-            high_bf = placed([P, (hi - lo) * P, PACK], BF16, f"high_bf{lo}", at)
-            for e in range(lo, hi):
-                nc.scalar.copy(packed_view(high_bf[:, (e - lo) * P : (e - lo + 1) * P, :]), planes_view(w1_raw[e][1][:]))
-            for e in range(lo, hi, 2):
-                n = min(2, hi - e) * P
-                cols = slice(e * P, e * P + n)
-                nc.vector.quantize_mx(
-                    out=high_w[:, cols].bitcast(E4M3), scales=high_s[:, cols],
-                    in_=high_bf[:, (e - lo) * P : (e - lo) * P + n, :].rearrange("p k t -> p (k t)"),
-                )
-        for e in range(E):
-            cols = slice(e * P, (e + 1) * P)
-            second_product(e, 1, high_w[:, cols], high_s[:, cols], sums[(e + 3) % 4])
+        def fetch_first(h, lo, hi):
+            first = kept([P, hi - lo], F32, f"first{h}_{lo}")
+            nc.vector.tensor_copy(first[:], dx[h][:].indirect(pos_sb[0][:, lo // LIST : hi // LIST]))
+            return first
 
-        for h in range(K // P):
-            cuts = TOKEN_CUTS[h]
-            for j in range(len(cuts) - 1):
-                lo, hi = cuts[j], cuts[j + 1]
-                first = ring.tile([P, hi - lo], F32, name="first")
-                if h == 0:
-                    second = placed([P, hi - lo], F32, f"second_late{j}", LATE_AT - 2 * KIB + j * 5 * KIB // 2)
-                else:
-                    second = ring.tile([P, hi - lo], F32, name="second")
-                total = keep.tile([P, hi - lo], F32, name=f"total{h}_{j}")
-                nc.vector.tensor_copy(first[:], dx[h][:].indirect(pos1_sb[:, lo // LIST : hi // LIST]))
-                nc.vector.tensor_copy(second[:], dx[h][:].indirect(pos2_sb[:, lo // LIST : hi // LIST]))
-                adder = nc.vector if (h, hi) == (K // P - 1, T) else nc.gpsimd
-                adder.tensor_tensor(total[:], first[:], second[:], ADD)
-                nc.sync.dma_start(out[h * P : (h + 1) * P, lo:hi], total[:])
+        def add_second(h, lo, hi, first, at=None):
+            name = f"total{h}_{lo}"
+            total = kept([P, hi - lo], F32, name) if at is None else placed([P, hi - lo], F32, name, at)
+            nc.vector.tensor_tensor(total[:], dx[h][:].indirect(pos_sb[1][:, lo // LIST : hi // LIST]), first, ADD)
+            nc.sync.dma_start(out[h * P : (h + 1) * P, lo:hi], total[:])
+
+        halves = ((0, T // 2), (T // 2, T))
+        firsts = [fetch_first(0, lo, hi) for lo, hi in halves]
+        quantise_w1(2, 4, 1, high234[:, : 2 * P, :])
+        quantise_w1(4, 5, 1, high234[:, 2 * P :, :])
+        for e in range(E):
+            second_product(e, 1)
+        for j, (lo, hi) in enumerate(halves):
+            add_second(0, lo, hi, firsts[j][:], LAST_RAW_AT + KIB + (j - 1) * T * 2)
+        firsts = [fetch_first(1, lo, hi) for lo, hi in halves]
+        add_second(1, 0, T // 2, firsts[0][:])
+        add_second(1, T // 2, T - 256, firsts[1][:, : T // 2 - 256])
+        add_second(1, T - 256, T, firsts[1][:, T // 2 - 256 :])

@@ -32,9 +32,12 @@ RAW2_AT = tuple(8 * KIB * e for e in range(E))
 CAST_A = 40 * KIB
 CAST_B = 44 * KIB
 ROUNDED_AT = (48 * KIB, 52 * KIB, 48 * KIB, 56 * KIB, 48 * KIB)
-DA_AT = (60 * KIB, 64 * KIB)
-LAST_RAW_AT = 70 * KIB
-LAST_WORDS_AT = 74 * KIB
+DA_AT = tuple(60 * KIB + 4 * KIB * e for e in range(E))
+LAST_RAW_AT = 82 * KIB
+FIRST_A_AT = 86 * KIB
+MASK_AT = (RAW2_AT[2], FIRST_A_AT + 4 * KIB)
+LAST_WORDS_AT = 94 * KIB
+LIFT = 65536.0
 
 
 def planes_view(raw):
@@ -73,7 +76,7 @@ def tile_moe_bdx_mlp_relu_kernel(tc, dy_words, dy_scales, a, w2, w1, gate, offs,
         w2_raw = {e: placed([P, PACK, H], F32, f"w2_raw{e}", RAW2_AT[e]) for e in range(1, E)}
         w1_raw = {(e, h): kept([P, PACK, P], F32, f"w1_raw{e}_{h}") for e in range(E) for h in range(2) if (e, h) != (E - 1, 1)}
         w1_raw[E - 1, 1] = placed([P, PACK, P], F32, "w1_raw_last", LAST_RAW_AT)
-        a_raw = [kept([P, PACK, C], F32, f"a_raw{e}") for e in range(E)]
+        a_raw = [placed([P, PACK, C], F32, "a_raw0", FIRST_A_AT)] + [kept([P, PACK, C], F32, f"a_raw{e}") for e in range(1, E)]
         da_w = [kept([P, C], U32, f"da_w{e}") for e in range(E)]
         da_s = [kept([P, C], U8, f"da_s{e}") for e in range(E)]
         dx = [kept([P, S], F32, f"dx{h}") for h in range(K // P)]
@@ -95,18 +98,19 @@ def tile_moe_bdx_mlp_relu_kernel(tc, dy_words, dy_scales, a, w2, w1, gate, offs,
         def load_a(e):
             nc.sync.dma_start(a_raw[e][:], a_rows[:, :, e * C : (e + 1) * C])
 
-        nc.scalar.dma_start(gate_rows[0 : S // P, :], gate[0].rearrange("(c p) -> c p", p=P))
         nc.sync.dma_start(offs_sb[:], offs)
         for q in range(4):
-            nc.sync.dma_start(dy_s[32 * q : 32 * q + 4, :].bitcast(I32), dy_scales[0, 4 * q : 4 * q + 4, :].bitcast(I32))
+            (nc.scalar, nc.sync)[q % 2].dma_start(dy_s[32 * q : 32 * q + 4, :].bitcast(I32), dy_scales[0, 4 * q : 4 * q + 4, :].bitcast(I32))
+        nc.scalar.dma_start(gate_rows[0 : S // P, :], gate[0].rearrange("(c p) -> c p", p=P))
         nc.sync.dma_start(w2_first[0][:], w2_rows(0)[:, :, : H // 2])
         nc.sync.dma_start(dy_w[:].bitcast(I32), dy_words[0].rearrange("p t d -> p (t d)").bitcast(I32))
         nc.sync.dma_start(w2_first[1][:], w2_rows(0)[:, :, H // 2 :])
-        for e in (1, 2, 3):
+        for e in (1, 2):
             nc.sync.dma_start(w2_raw[e][:], w2_rows(e))
-        load_a(0)
-        nc.sync.dma_start(w2_raw[4][:], w2_rows(4))
-        for e in (1, 2, 3):
+        for e in (0, 1):
+            load_a(e)
+            nc.sync.dma_start(w2_raw[e + 3][:], w2_rows(e + 3))
+        for e in (2, 3):
             load_a(e)
         for e in range(E - 1):
             load_w1(e, 0)
@@ -184,12 +188,20 @@ def tile_moe_bdx_mlp_relu_kernel(tc, dy_words, dy_scales, a, w2, w1, gate, offs,
                 if s % 2 == 1:
                     turn(e, s // 2)
 
-        def make_mask(e):
-            mask[e] = placed([P, C, PACK], BF16, f"mask{e}", RAW2_AT[3] if e % 2 == 0 else CAST_A)
-            nc.vector.tensor_scalar(packed_view(mask[e][:]), planes_view(a_raw[e][:]), 0.0, None, IS_GT)
+        def make_mask(e, lifted=None):
+            mask[e] = placed([P, C, PACK], BF16, f"mask{e}", MASK_AT[e % 2])
+            if lifted is None:
+                nc.vector.tensor_scalar(packed_view(mask[e][:]), planes_view(a_raw[e][:]), 0.0, None, IS_GT)
+            else:
+                nc.vector.tensor_scalar(flat(mask[e][:]), flat(lifted[:]), 0.0, None, IS_GT)
+
+        def lift_on_gpsimd(e, at):
+            lifted = placed([P, C, PACK], BF16, f"lifted{e}", at)
+            nc.gpsimd.tensor_scalar(lifted[:], a_raw[e][:].rearrange("p t n -> p n t"), LIFT, 0.0, MULT, ADD)
+            return lifted
 
         def apply_mask(e):
-            da_bf[e] = placed([P, C, PACK], BF16, f"da_bf{e}", DA_AT[e % 2])
+            da_bf[e] = placed([P, C, PACK], BF16, f"da_bf{e}", DA_AT[e])
             for half in range(2):
                 cols = slice(half * HALF, (half + 1) * HALF)
                 nc.vector.tensor_tensor(
@@ -241,26 +253,27 @@ def tile_moe_bdx_mlp_relu_kernel(tc, dy_words, dy_scales, a, w2, w1, gate, offs,
         empty_sums(0, False)
         round_w2_on_scalar(2, CAST_B)
         quantise_w2(1)
-        round_w2_on_gpsimd(3, CAST_A)
+        lifted = lift_on_gpsimd(0, CAST_A)
         gather_words(3, RAW2_AT[1])
         gather_scales(4, RAW2_AT[1] + 2 * KIB)
         gather_words(4, RAW2_AT[1] + 3 * KIB)
         for s in range(4):
             first_product(1, s)
         empty_sums(1, False)
-        quantise_w2(2, RAW2_AT[3] + 4 * KIB)
-        make_mask(0)
-        quantise_w2(3)
+        round_w2_on_scalar(3, RAW2_AT[0])
+        quantise_w2(2, FIRST_A_AT)
+        make_mask(0, lifted)
+        make_mask(1)
         for s in range(4):
             first_product(2, s)
         apply_mask(0)
-        make_mask(1)
+        quantise_w2(3)
         quantise_da(0)
         empty_sums(2, True)
         round_w2_on_scalar(4, ROUNDED_AT[1])
         apply_mask(1)
-        quantise_w2(4)
         make_mask(2)
+        quantise_w2(4)
         quantise_da(1)
         empty_sums(3, True)
         apply_mask(2)
@@ -282,7 +295,7 @@ def tile_moe_bdx_mlp_relu_kernel(tc, dy_words, dy_scales, a, w2, w1, gate, offs,
         for e in range(E):
             second_product(e, 0)
         high01 = round_w1(0, 2, 1)
-        quantise_w1(0, 2, 1, high01[:], DA_AT[0])
+        quantise_w1(0, 2, 1, high01[:], DA_AT[4])
         high234 = round_w1(2, 5, 1, LAST_WORDS_AT)
 
         def fetch_first(h, lo, hi):

@@ -48,6 +48,10 @@ def packed_view(grouped):
     return grouped.rearrange("p (c i) t -> p c t i", i=4)
 
 
+def pairs_view(raw):
+    return raw.rearrange("p (u x) n -> p u n x", x=2)
+
+
 def flat(grouped):
     return grouped.rearrange("p n t -> p (n t)")
 
@@ -189,25 +193,25 @@ def tile_moe_bdx_mlp_relu_kernel(tc, dy_words, dy_scales, a, w2, w1, gate, offs,
                     turn(e, s // 2)
 
         def make_mask(e, lifted=None):
-            mask[e] = placed([P, C, PACK], BF16, f"mask{e}", MASK_AT[e % 2])
+            mask[e] = placed([P, 2, C, 2], BF16, f"mask{e}", MASK_AT[e % 2])
             if lifted is None:
-                nc.vector.tensor_scalar(packed_view(mask[e][:]), planes_view(a_raw[e][:]), 0.0, None, IS_GT)
+                nc.vector.tensor_scalar(mask[e][:], pairs_view(a_raw[e][:]), 0.0, None, IS_GT)
             else:
-                nc.vector.tensor_scalar(flat(mask[e][:]), flat(lifted[:]), 0.0, None, IS_GT)
+                nc.vector.tensor_scalar(mask[e][:], lifted[:], 0.0, None, IS_GT)
 
         def lift_on_gpsimd(e, at):
-            lifted = placed([P, C, PACK], BF16, f"lifted{e}", at)
-            nc.gpsimd.tensor_scalar(lifted[:], a_raw[e][:].rearrange("p t n -> p n t"), LIFT, 0.0, MULT, ADD)
+            lifted = placed([P, 2, C, 2], BF16, f"lifted{e}", at)
+            nc.gpsimd.tensor_scalar(lifted[:], pairs_view(a_raw[e][:]), LIFT, 0.0, MULT, ADD)
             return lifted
 
         def apply_mask(e):
             da_bf[e] = placed([P, C, PACK], BF16, f"da_bf{e}", DA_AT[e])
-            for half in range(2):
+            for half in (1, 0):
                 cols = slice(half * HALF, (half + 1) * HALF)
                 nc.vector.tensor_tensor(
                     da_bf[e][:, cols, :].rearrange("p n (u x) -> p n u x", u=2),
                     turned[2 * (e % 2) + half][:].bitcast(BF16).rearrange("p (u n x) -> p n u x", u=2, x=2),
-                    mask[e][:, cols, :].rearrange("p n (u x) -> p n u x", u=2),
+                    mask[e][:, :, cols, :].rearrange("p u n x -> p n u x"),
                     MULT,
                 )
 
@@ -289,9 +293,9 @@ def tile_moe_bdx_mlp_relu_kernel(tc, dy_words, dy_scales, a, w2, w1, gate, offs,
         quantise_da(3)
         quantise_w1(2, 4, 0, low23[:])
         apply_mask(4)
-        quantise_da(4, slice(0, HALF))
-        quantise_w1(4, 5, 0, low4[:], LAST_WORDS_AT)
         quantise_da(4, slice(HALF, C))
+        quantise_w1(4, 5, 0, low4[:], LAST_WORDS_AT)
+        quantise_da(4, slice(0, HALF))
         for e in range(E):
             second_product(e, 0)
         high01 = round_w1(0, 2, 1)

@@ -34,9 +34,10 @@ CAST_B = 44 * KIB
 ROUNDED_AT = (48 * KIB, 52 * KIB, 48 * KIB, 56 * KIB, 48 * KIB)
 DA_AT = tuple(60 * KIB + 4 * KIB * e for e in range(E))
 LAST_RAW_AT = 82 * KIB
-FIRST_A_AT = 86 * KIB
-MASK_AT = (RAW2_AT[2], FIRST_A_AT + 4 * KIB)
-LAST_WORDS_AT = 94 * KIB
+LAST_WORDS_AT = 86 * KIB
+A_AT = tuple(90 * KIB + 8 * KIB * e for e in range(E))
+MASK_AT = (RAW2_AT[2], A_AT[0] + 4 * KIB)
+W1_RAW_AT = {(4, 1): LAST_RAW_AT}
 LIFT = 65536.0
 
 
@@ -78,9 +79,10 @@ def tile_moe_bdx_mlp_relu_kernel(tc, dy_words, dy_scales, a, w2, w1, gate, offs,
         ident = kept([P, P], F32, "ident")
         w2_first = [placed([P, PACK, H // 2], F32, f"w2_first{j}", RAW2_AT[0] + j * 4 * KIB) for j in range(2)]
         w2_raw = {e: placed([P, PACK, H], F32, f"w2_raw{e}", RAW2_AT[e]) for e in range(1, E)}
-        w1_raw = {(e, h): kept([P, PACK, P], F32, f"w1_raw{e}_{h}") for e in range(E) for h in range(2) if (e, h) != (E - 1, 1)}
-        w1_raw[E - 1, 1] = placed([P, PACK, P], F32, "w1_raw_last", LAST_RAW_AT)
-        a_raw = [placed([P, PACK, C], F32, "a_raw0", FIRST_A_AT)] + [kept([P, PACK, C], F32, f"a_raw{e}") for e in range(1, E)]
+        w1_raw = {(e, h): kept([P, PACK, P], F32, f"w1_raw{e}_{h}") for e in range(E) for h in range(2) if (e, h) not in W1_RAW_AT}
+        for (e, h), at in W1_RAW_AT.items():
+            w1_raw[e, h] = placed([P, PACK, P], F32, f"w1_raw{e}_{h}", at)
+        a_raw = [placed([P, PACK, C], F32, f"a_raw{e}", A_AT[e]) for e in range(E)]
         da_w = [kept([P, C], U32, f"da_w{e}") for e in range(E)]
         da_s = [kept([P, C], U8, f"da_s{e}") for e in range(E)]
         dx = [kept([P, S], F32, f"dx{h}") for h in range(K // P)]
@@ -111,15 +113,17 @@ def tile_moe_bdx_mlp_relu_kernel(tc, dy_words, dy_scales, a, w2, w1, gate, offs,
         nc.sync.dma_start(w2_first[1][:], w2_rows(0)[:, :, H // 2 :])
         for e in (1, 2):
             nc.sync.dma_start(w2_raw[e][:], w2_rows(e))
-        for e in (0, 1):
-            load_a(e)
-            nc.sync.dma_start(w2_raw[e + 3][:], w2_rows(e + 3))
-        for e in (2, 3):
-            load_a(e)
-        for e in range(E - 1):
+        load_a(0)
+        nc.sync.dma_start(w2_raw[3][:], w2_rows(3))
+        load_a(1)
+        nc.sync.dma_start(w2_raw[4][:], w2_rows(4))
+        for e in range(2):
             load_w1(e, 0)
-        load_a(E - 1)
-        load_w1(E - 1, 0)
+            load_a(e + 2)
+        for e in (2, 3):
+            load_w1(e, 0)
+        load_a(4)
+        load_w1(4, 0)
         nc.sync.dma_start(pos_sb[0][:], pos1)
         nc.sync.dma_start(pos_sb[1][:], pos2)
         for e in range(E):
@@ -193,36 +197,44 @@ def tile_moe_bdx_mlp_relu_kernel(tc, dy_words, dy_scales, a, w2, w1, gate, offs,
                     turn(e, s // 2)
 
         def make_mask(e, lifted=None):
-            mask[e] = placed([P, 2, C, 2], BF16, f"mask{e}", MASK_AT[e % 2])
-            if lifted is None:
-                nc.vector.tensor_scalar(mask[e][:], pairs_view(a_raw[e][:]), 0.0, None, IS_GT)
-            else:
-                nc.vector.tensor_scalar(mask[e][:], lifted[:], 0.0, None, IS_GT)
+            for half in range(2):
+                cols = slice(half * HALF, (half + 1) * HALF)
+                mask[e, half] = placed([P, 2, HALF, 2], BF16, f"mask{e}_{half}", MASK_AT[e % 2] + half * 2 * KIB)
+                source = pairs_view(a_raw[e][:, :, cols]) if lifted is None else lifted[:, half]
+                nc.vector.tensor_scalar(mask[e, half][:], source, 0.0, None, IS_GT)
 
         def lift_on_gpsimd(e, at):
-            lifted = placed([P, 2, C, 2], BF16, f"lifted{e}", at)
-            nc.gpsimd.tensor_scalar(lifted[:], pairs_view(a_raw[e][:]), LIFT, 0.0, MULT, ADD)
+            lifted = placed([P, 2, 2, HALF, 2], BF16, f"lifted{e}", at)
+            for half in range(2):
+                cols = slice(half * HALF, (half + 1) * HALF)
+                nc.gpsimd.tensor_scalar(lifted[:, half], pairs_view(a_raw[e][:, :, cols]), LIFT, 0.0, MULT, ADD)
             return lifted
 
         def apply_mask(e):
-            da_bf[e] = placed([P, C, PACK], BF16, f"da_bf{e}", DA_AT[e])
-            for half in (1, 0):
-                cols = slice(half * HALF, (half + 1) * HALF)
+            for half in range(2):
+                da_bf[e, half] = placed([P, HALF, PACK], BF16, f"da_bf{e}_{half}", DA_AT[e] + half * 2 * KIB)
                 nc.vector.tensor_tensor(
-                    da_bf[e][:, cols, :].rearrange("p n (u x) -> p n u x", u=2),
+                    da_bf[e, half][:].rearrange("p n (u x) -> p n u x", u=2),
                     turned[2 * (e % 2) + half][:].bitcast(BF16).rearrange("p (u n x) -> p n u x", u=2, x=2),
-                    mask[e][:, :, cols, :].rearrange("p u n x -> p n u x"),
+                    mask[e, half][:].rearrange("p u n x -> p n u x"),
                     MULT,
                 )
 
-        def quantise_da(e, cols=slice(0, C)):
-            nc.vector.quantize_mx(out=da_w[e][:, cols].bitcast(E5M2), scales=da_s[e][:, cols], in_=flat(da_bf[e][:, cols, :]))
+        def quantise_da(e):
+            for half in range(2):
+                cols = slice(half * HALF, (half + 1) * HALF)
+                nc.vector.quantize_mx(out=da_w[e][:, cols].bitcast(E5M2), scales=da_s[e][:, cols], in_=flat(da_bf[e, half][:]))
 
         def round_w1(lo, hi, h, at=None):
             shape, name = [P, (hi - lo) * P, PACK], f"w1_bf{lo}_{h}"
             grouped = kept(shape, BF16, name) if at is None else placed(shape, BF16, name, at)
             for e in range(lo, hi):
                 nc.scalar.copy(packed_view(grouped[:, (e - lo) * P : (e - lo + 1) * P, :]), planes_view(w1_raw[e, h][:]))
+            return grouped
+
+        def round_w1_on_gpsimd(e, at):
+            grouped = placed([P, P, PACK], BF16, f"w1_bf{e}_0", at)
+            nc.gpsimd.tensor_scalar(grouped[:], w1_raw[e, 0][:].rearrange("p t k -> p k t"), 1.0, 0.0, MULT, ADD)
             return grouped
 
         def quantise_w1(lo, hi, h, grouped, at=None):
@@ -265,37 +277,40 @@ def tile_moe_bdx_mlp_relu_kernel(tc, dy_words, dy_scales, a, w2, w1, gate, offs,
             first_product(1, s)
         empty_sums(1, False)
         round_w2_on_scalar(3, RAW2_AT[0])
-        quantise_w2(2, FIRST_A_AT)
         make_mask(0, lifted)
-        make_mask(1)
+        quantise_w2(2, A_AT[0])
         for s in range(4):
             first_product(2, s)
         apply_mask(0)
-        quantise_w2(3)
         quantise_da(0)
+        quantise_w2(3)
         empty_sums(2, True)
         round_w2_on_scalar(4, ROUNDED_AT[1])
+        make_mask(1)
+        low0 = round_w1_on_gpsimd(0, A_AT[1])
         apply_mask(1)
-        make_mask(2)
-        quantise_w2(4)
         quantise_da(1)
-        empty_sums(3, True)
+        quantise_w1(0, 1, 0, low0[:])
+        make_mask(2)
+        low1 = round_w1_on_gpsimd(1, A_AT[2])
         apply_mask(2)
-        make_mask(3)
+        quantise_w2(4, MASK_AT[0])
+        empty_sums(3, True)
         quantise_da(2)
+        quantise_w1(1, 2, 0, low1[:])
         empty_sums(4, False)
-        low01 = round_w1(0, 2, 0)
-        low23 = round_w1(2, 4, 0)
-        low4 = round_w1(4, 5, 0)
+        low3 = round_w1(3, 4, 0)
+        make_mask(3)
+        low2 = round_w1_on_gpsimd(2, A_AT[3])
         apply_mask(3)
-        quantise_w1(0, 2, 0, low01[:])
-        make_mask(4)
         quantise_da(3)
-        quantise_w1(2, 4, 0, low23[:])
+        quantise_w1(2, 3, 0, low2[:])
+        quantise_w1(3, 4, 0, low3[:])
+        make_mask(4)
+        low4 = round_w1_on_gpsimd(4, A_AT[4])
         apply_mask(4)
-        quantise_da(4, slice(HALF, C))
+        quantise_da(4)
         quantise_w1(4, 5, 0, low4[:], LAST_WORDS_AT)
-        quantise_da(4, slice(0, HALF))
         for e in range(E):
             second_product(e, 0)
         high01 = round_w1(0, 2, 1)

@@ -31,13 +31,16 @@ KIB = 1024
 RAW2_AT = tuple(8 * KIB * e for e in range(E))
 CAST_A = 40 * KIB
 CAST_B = 44 * KIB
-ROUNDED_AT = (48 * KIB, 52 * KIB, 48 * KIB, 56 * KIB, 48 * KIB)
+ROUNDED_AT = (48 * KIB, 52 * KIB, 48 * KIB, 131 * KIB, 48 * KIB)
 DA_AT = tuple(60 * KIB + 4 * KIB * e for e in range(E))
-LAST_RAW_AT = 82 * KIB
+LAST_RAW_AT = 83 * KIB
 LAST_WORDS_AT = 86 * KIB
-A_AT = tuple(90 * KIB + 8 * KIB * e for e in range(E))
+A_AT = tuple(91 * KIB + 8 * KIB * e for e in range(E))
 MASK_AT = (RAW2_AT[2], A_AT[0] + 4 * KIB)
-W1_RAW_AT = {(4, 1): LAST_RAW_AT}
+MIDDLE_RAW_AT = 56 * KIB
+W1_RAW_AT = {(2, 1): MIDDLE_RAW_AT, (4, 1): LAST_RAW_AT}
+FIRST_ON_SCALAR = 304
+EARLY_TOKENS = 832
 LIFT = 65536.0
 
 
@@ -77,8 +80,7 @@ def tile_moe_bdx_mlp_relu_kernel(tc, dy_words, dy_scales, a, w2, w1, gate, offs,
         gate_rows = kept([P, P], F32, "gate_rows")
         gate_cols = kept([P, S // P], F32, "gate_cols")
         ident = kept([P, P], F32, "ident")
-        w2_first = [placed([P, PACK, H // 2], F32, f"w2_first{j}", RAW2_AT[0] + j * 4 * KIB) for j in range(2)]
-        w2_raw = {e: placed([P, PACK, H], F32, f"w2_raw{e}", RAW2_AT[e]) for e in range(1, E)}
+        w2_raw = [placed([P, PACK, H], F32, f"w2_raw{e}", RAW2_AT[e]) for e in range(E)]
         w1_raw = {(e, h): kept([P, PACK, P], F32, f"w1_raw{e}_{h}") for e in range(E) for h in range(2) if (e, h) not in W1_RAW_AT}
         for (e, h), at in W1_RAW_AT.items():
             w1_raw[e, h] = placed([P, PACK, P], F32, f"w1_raw{e}_{h}", at)
@@ -108,22 +110,18 @@ def tile_moe_bdx_mlp_relu_kernel(tc, dy_words, dy_scales, a, w2, w1, gate, offs,
         for q in range(4):
             (nc.scalar, nc.sync)[q % 2].dma_start(dy_s[32 * q : 32 * q + 4, :].bitcast(I32), dy_scales[0, 4 * q : 4 * q + 4, :].bitcast(I32))
         nc.scalar.dma_start(gate_rows[0 : S // P, :], gate[0].rearrange("(c p) -> c p", p=P))
-        nc.sync.dma_start(w2_first[0][:], w2_rows(0)[:, :, : H // 2])
         nc.sync.dma_start(dy_w[:].bitcast(I32), dy_words[0].rearrange("p t d -> p (t d)").bitcast(I32))
-        nc.sync.dma_start(w2_first[1][:], w2_rows(0)[:, :, H // 2 :])
-        for e in (1, 2):
+        for e in (0, 1, 2):
             nc.sync.dma_start(w2_raw[e][:], w2_rows(e))
         load_a(0)
         nc.sync.dma_start(w2_raw[3][:], w2_rows(3))
         load_a(1)
         nc.sync.dma_start(w2_raw[4][:], w2_rows(4))
-        for e in range(2):
+        for e in range(3):
             load_w1(e, 0)
             load_a(e + 2)
-        for e in (2, 3):
+        for e in (3, 4):
             load_w1(e, 0)
-        load_a(4)
-        load_w1(4, 0)
         nc.sync.dma_start(pos_sb[0][:], pos1)
         nc.sync.dma_start(pos_sb[1][:], pos2)
         for e in range(E):
@@ -145,17 +143,13 @@ def tile_moe_bdx_mlp_relu_kernel(tc, dy_words, dy_scales, a, w2, w1, gate, offs,
             g_w[e] = kept([P, C], U32, f"g_w{e}") if at is None else placed([P, C], U32, f"g_w{e}", at)
             nc.vector.tensor_copy(g_w[e][:], dy_w[:].indirect(slots(e)))
 
-        def round_w2_on_scalar(e, at):
+        def round_w2(e, at, on_scalar):
             w2_bf[e] = placed([P, H, PACK], BF16, f"w2_bf{e}", at)
-            if e == 0:
-                for j in range(2):
-                    nc.scalar.copy(packed_view(w2_bf[e][:, j * H // 2 : (j + 1) * H // 2, :]), planes_view(w2_first[j][:]))
-            else:
-                nc.scalar.copy(packed_view(w2_bf[e][:]), planes_view(w2_raw[e][:]))
-
-        def round_w2_on_gpsimd(e, at):
-            w2_bf[e] = placed([P, H, PACK], BF16, f"w2_bf{e}", at)
-            nc.gpsimd.tensor_scalar(w2_bf[e][:], w2_raw[e][:].rearrange("p t i -> p i t"), 1.0, 0.0, MULT, ADD)
+            if on_scalar > 0:
+                nc.scalar.copy(packed_view(w2_bf[e][:, :on_scalar, :]), planes_view(w2_raw[e][:, :, :on_scalar]))
+            if on_scalar < H:
+                rest = w2_raw[e][:, :, on_scalar:].rearrange("p t i -> p i t")
+                nc.gpsimd.tensor_scalar(w2_bf[e][:, on_scalar:, :], rest, 1.0, 0.0, MULT, ADD)
 
         def quantise_w2(e, at=None):
             words = kept([P, H], U32, f"w2_w{e}") if at is None else placed([P, H], U32, f"w2_w{e}", at)
@@ -258,16 +252,16 @@ def tile_moe_bdx_mlp_relu_kernel(tc, dy_words, dy_scales, a, w2, w1, gate, offs,
         gather_scales(1)
         gather_words(0)
         gather_words(1)
-        round_w2_on_scalar(0, CAST_A)
+        round_w2(0, CAST_A, FIRST_ON_SCALAR)
         quantise_w2(0)
-        round_w2_on_gpsimd(1, CAST_A)
+        round_w2(1, CAST_A, 0)
         gather_scales(2, RAW2_AT[0] + 4 * KIB)
         gather_words(2, RAW2_AT[0] + 5 * KIB)
         gather_scales(3, RAW2_AT[0] + 7 * KIB)
         for s in range(4):
             first_product(0, s)
         empty_sums(0, False)
-        round_w2_on_scalar(2, CAST_B)
+        round_w2(2, CAST_B, H)
         quantise_w2(1)
         lifted = lift_on_gpsimd(0, CAST_A)
         gather_words(3, RAW2_AT[1])
@@ -276,7 +270,7 @@ def tile_moe_bdx_mlp_relu_kernel(tc, dy_words, dy_scales, a, w2, w1, gate, offs,
         for s in range(4):
             first_product(1, s)
         empty_sums(1, False)
-        round_w2_on_scalar(3, RAW2_AT[0])
+        round_w2(3, RAW2_AT[0], H)
         make_mask(0, lifted)
         quantise_w2(2, A_AT[0])
         for s in range(4):
@@ -285,7 +279,7 @@ def tile_moe_bdx_mlp_relu_kernel(tc, dy_words, dy_scales, a, w2, w1, gate, offs,
         quantise_da(0)
         quantise_w2(3)
         empty_sums(2, True)
-        round_w2_on_scalar(4, ROUNDED_AT[1])
+        round_w2(4, ROUNDED_AT[1], H)
         make_mask(1)
         low0 = round_w1_on_gpsimd(0, A_AT[1])
         apply_mask(1)
@@ -299,26 +293,25 @@ def tile_moe_bdx_mlp_relu_kernel(tc, dy_words, dy_scales, a, w2, w1, gate, offs,
         quantise_da(2)
         quantise_w1(1, 2, 0, low1[:])
         empty_sums(4, False)
-        low3 = round_w1(3, 4, 0)
         make_mask(3)
         low2 = round_w1_on_gpsimd(2, A_AT[3])
         apply_mask(3)
         quantise_da(3)
         quantise_w1(2, 3, 0, low2[:])
-        quantise_w1(3, 4, 0, low3[:])
         make_mask(4)
-        low4 = round_w1_on_gpsimd(4, A_AT[4])
+        low3 = round_w1_on_gpsimd(3, A_AT[4])
+        low4 = round_w1(4, 5, 0)
         apply_mask(4)
+        quantise_w1(3, 4, 0, low3[:])
         quantise_da(4)
         quantise_w1(4, 5, 0, low4[:], LAST_WORDS_AT)
         for e in range(E):
             second_product(e, 0)
-        high01 = round_w1(0, 2, 1)
-        quantise_w1(0, 2, 1, high01[:], DA_AT[4])
-        high234 = round_w1(2, 5, 1, LAST_WORDS_AT)
+        high = round_w1(0, E, 1, LAST_WORDS_AT)
 
-        def fetch_first(h, lo, hi):
-            first = kept([P, hi - lo], F32, f"first{h}_{lo}")
+        def fetch_first(h, lo, hi, at=None):
+            name = f"first{h}_{lo}"
+            first = kept([P, hi - lo], F32, name) if at is None else placed([P, hi - lo], F32, name, at)
             nc.vector.tensor_copy(first[:], dx[h][:].indirect(pos_sb[0][:, lo // LIST : hi // LIST]))
             return first
 
@@ -328,14 +321,16 @@ def tile_moe_bdx_mlp_relu_kernel(tc, dy_words, dy_scales, a, w2, w1, gate, offs,
             nc.vector.tensor_tensor(total[:], dx[h][:].indirect(pos_sb[1][:, lo // LIST : hi // LIST]), first, ADD)
             nc.sync.dma_start(out[h * P : (h + 1) * P, lo:hi], total[:])
 
-        halves = ((0, T // 2), (T // 2, T))
-        firsts = [fetch_first(0, lo, hi) for lo, hi in halves]
-        quantise_w1(2, 4, 1, high234[:, : 2 * P, :])
-        quantise_w1(4, 5, 1, high234[:, 2 * P :, :])
+        early = fetch_first(0, 0, EARLY_TOKENS)
+        quantise_w1(0, 2, 1, high[:, : 2 * P, :])
+        quantise_w1(2, 3, 1, high[:, 2 * P : 3 * P, :])
+        late = fetch_first(0, EARLY_TOKENS, T, MIDDLE_RAW_AT)
+        quantise_w1(3, 5, 1, high[:, 3 * P :, :])
         for e in range(E):
             second_product(e, 1)
-        for j, (lo, hi) in enumerate(halves):
-            add_second(0, lo, hi, firsts[j][:], LAST_RAW_AT + KIB + (j - 1) * T * 2)
+        add_second(0, 0, EARLY_TOKENS, early[:], LAST_RAW_AT + KIB - 4 * EARLY_TOKENS)
+        add_second(0, EARLY_TOKENS, T, late[:], LAST_RAW_AT + KIB)
+        halves = ((0, T // 2), (T // 2, T))
         firsts = [fetch_first(1, lo, hi) for lo, hi in halves]
         add_second(1, 0, T // 2, firsts[0][:])
         add_second(1, T // 2, T - 256, firsts[1][:, : T // 2 - 256])

@@ -33,14 +33,14 @@ CAST_A = 40 * KIB
 CAST_B = 44 * KIB
 ROUNDED_AT = (48 * KIB, 52 * KIB, 48 * KIB, 131 * KIB, 48 * KIB)
 DA_AT = tuple(60 * KIB + 4 * KIB * e for e in range(E))
-LAST_RAW_AT = 83 * KIB
+LAST_RAW_AT = 82 * KIB
 LAST_WORDS_AT = 86 * KIB
 A_AT = tuple(91 * KIB + 8 * KIB * e for e in range(E))
 MASK_AT = (RAW2_AT[2], A_AT[0] + 4 * KIB)
-MIDDLE_RAW_AT = 56 * KIB
-W1_RAW_AT = {(2, 1): MIDDLE_RAW_AT, (4, 1): LAST_RAW_AT}
+W1_RAW_AT = {(4, 1): LAST_RAW_AT}
 FIRST_ON_SCALAR = 304
-EARLY_TOKENS = 832
+LAST_TOKENS = 256
+WINDOW = 1408
 LIFT = 65536.0
 
 
@@ -75,8 +75,8 @@ def tile_moe_bdx_mlp_relu_kernel(tc, dy_words, dy_scales, a, w2, w1, gate, offs,
 
         offs_sb = keep.tile([P, S // LIST], U16, name="offs_sb")
         pos_sb = [keep.tile([P, T // LIST], U16, name=f"pos{r}_sb") for r in (1, 2)]
-        dy_w = kept([P, T], U32, "dy_w")
-        dy_s = kept([P, T], U8, "dy_s")
+        dy_w = kept([P, WINDOW], U32, "dy_w")
+        dy_s = kept([P, WINDOW], U8, "dy_s")
         gate_rows = kept([P, P], F32, "gate_rows")
         gate_cols = kept([P, S // P], F32, "gate_cols")
         ident = kept([P, P], F32, "ident")
@@ -93,6 +93,7 @@ def tile_moe_bdx_mlp_relu_kernel(tc, dy_words, dy_scales, a, w2, w1, gate, offs,
 
         nc.gpsimd.memset(dy_s[:].bitcast(I32), 0)
         nc.gpsimd.memset(gate_rows[:], 0.0)
+        nc.gpsimd.memset(dy_w[:, T:].bitcast(I32), 0)
         make_identity(nc, ident[:])
 
         a_rows = a.rearrange("(p t) s -> p t s", t=PACK)
@@ -108,20 +109,19 @@ def tile_moe_bdx_mlp_relu_kernel(tc, dy_words, dy_scales, a, w2, w1, gate, offs,
 
         nc.sync.dma_start(offs_sb[:], offs)
         for q in range(4):
-            (nc.scalar, nc.sync)[q % 2].dma_start(dy_s[32 * q : 32 * q + 4, :].bitcast(I32), dy_scales[0, 4 * q : 4 * q + 4, :].bitcast(I32))
+            (nc.scalar, nc.sync)[q % 2].dma_start(dy_s[32 * q : 32 * q + 4, :T].bitcast(I32), dy_scales[0, 4 * q : 4 * q + 4, :].bitcast(I32))
         nc.scalar.dma_start(gate_rows[0 : S // P, :], gate[0].rearrange("(c p) -> c p", p=P))
-        nc.sync.dma_start(dy_w[:].bitcast(I32), dy_words[0].rearrange("p t d -> p (t d)").bitcast(I32))
+        nc.sync.dma_start(dy_w[:, :T].bitcast(I32), dy_words[0].rearrange("p t d -> p (t d)").bitcast(I32))
         for e in (0, 1, 2):
             nc.sync.dma_start(w2_raw[e][:], w2_rows(e))
         load_a(0)
         nc.sync.dma_start(w2_raw[3][:], w2_rows(3))
-        load_a(1)
-        nc.sync.dma_start(w2_raw[4][:], w2_rows(4))
-        for e in range(3):
+        for e in range(E):
             load_w1(e, 0)
-            load_a(e + 2)
-        for e in (3, 4):
-            load_w1(e, 0)
+            if e + 1 < E:
+                load_a(e + 1)
+            if e == 0:
+                nc.sync.dma_start(w2_raw[4][:], w2_rows(4))
         nc.sync.dma_start(pos_sb[0][:], pos1)
         nc.sync.dma_start(pos_sb[1][:], pos2)
         for e in range(E):
@@ -132,16 +132,12 @@ def tile_moe_bdx_mlp_relu_kernel(tc, dy_words, dy_scales, a, w2, w1, gate, offs,
 
         g_w, g_s, w2_bf, w2_q, rounded, mask, da_bf, w1_q = {}, {}, {}, {}, {}, {}, {}, {}
 
-        def slots(e):
-            return offs_sb[:, e * C // LIST : (e + 1) * C // LIST]
-
-        def gather_scales(e, at=None):
-            g_s[e] = kept([P, C], U8, f"g_s{e}") if at is None else placed([P, C], U8, f"g_s{e}", at)
-            nc.vector.tensor_copy(g_s[e][:], dy_s[:].indirect(slots(e)))
-
-        def gather_words(e, at=None):
-            g_w[e] = kept([P, C], U32, f"g_w{e}") if at is None else placed([P, C], U32, f"g_w{e}", at)
-            nc.vector.tensor_copy(g_w[e][:], dy_w[:].indirect(slots(e)))
+        def gather(window, dtype, into, lo, hi, at=None):
+            shape, name = [P, (hi - lo) * C], f"gathered{len(g_w) + len(g_s)}"
+            picked = kept(shape, dtype, name) if at is None else placed(shape, dtype, name, at)
+            nc.vector.tensor_copy(picked[:], window[:].indirect(offs_sb[:, lo * C // LIST : hi * C // LIST]))
+            for e in range(lo, hi):
+                into[e] = picked[:, (e - lo) * C : (e - lo + 1) * C]
 
         def round_w2(e, at, on_scalar):
             w2_bf[e] = placed([P, H, PACK], BF16, f"w2_bf{e}", at)
@@ -248,25 +244,21 @@ def tile_moe_bdx_mlp_relu_kernel(tc, dy_words, dy_scales, a, w2, w1, gate, offs,
             )
             nc.scalar.copy(dx[h][:, e * C : (e + 1) * C], bank[:])
 
-        gather_scales(0)
-        gather_scales(1)
-        gather_words(0)
-        gather_words(1)
+        gather(dy_s, U8, g_s, 0, 2)
+        gather(dy_w, U32, g_w, 0, 2)
         round_w2(0, CAST_A, FIRST_ON_SCALAR)
         quantise_w2(0)
         round_w2(1, CAST_A, 0)
-        gather_scales(2, RAW2_AT[0] + 4 * KIB)
-        gather_words(2, RAW2_AT[0] + 5 * KIB)
-        gather_scales(3, RAW2_AT[0] + 7 * KIB)
+        gather(dy_s, U8, g_s, 2, 4, RAW2_AT[0] + 4 * KIB)
+        gather(dy_w, U32, g_w, 2, 3, RAW2_AT[0] + 5 * KIB)
         for s in range(4):
             first_product(0, s)
         empty_sums(0, False)
         round_w2(2, CAST_B, H)
         quantise_w2(1)
         lifted = lift_on_gpsimd(0, CAST_A)
-        gather_words(3, RAW2_AT[1])
-        gather_scales(4, RAW2_AT[1] + 2 * KIB)
-        gather_words(4, RAW2_AT[1] + 3 * KIB)
+        gather(dy_w, U32, g_w, 3, 5, RAW2_AT[1])
+        gather(dy_s, U8, g_s, 4, 5, RAW2_AT[1] + 4 * KIB)
         for s in range(4):
             first_product(1, s)
         empty_sums(1, False)
@@ -275,43 +267,31 @@ def tile_moe_bdx_mlp_relu_kernel(tc, dy_words, dy_scales, a, w2, w1, gate, offs,
         quantise_w2(2, A_AT[0])
         for s in range(4):
             first_product(2, s)
-        apply_mask(0)
-        quantise_da(0)
-        quantise_w2(3)
-        empty_sums(2, True)
-        round_w2(4, ROUNDED_AT[1], H)
-        make_mask(1)
-        low0 = round_w1_on_gpsimd(0, A_AT[1])
-        apply_mask(1)
-        quantise_da(1)
-        quantise_w1(0, 1, 0, low0[:])
-        make_mask(2)
-        low1 = round_w1_on_gpsimd(1, A_AT[2])
-        apply_mask(2)
-        quantise_w2(4, MASK_AT[0])
-        empty_sums(3, True)
-        quantise_da(2)
-        quantise_w1(1, 2, 0, low1[:])
-        empty_sums(4, False)
-        make_mask(3)
-        low2 = round_w1_on_gpsimd(2, A_AT[3])
-        apply_mask(3)
-        quantise_da(3)
-        quantise_w1(2, 3, 0, low2[:])
-        make_mask(4)
-        low3 = round_w1_on_gpsimd(3, A_AT[4])
-        low4 = round_w1(4, 5, 0)
-        apply_mask(4)
-        quantise_w1(3, 4, 0, low3[:])
-        quantise_da(4)
-        quantise_w1(4, 5, 0, low4[:], LAST_WORDS_AT)
+        for e in range(E):
+            if e > 0:
+                make_mask(e)
+            low = round_w1_on_gpsimd(e, A_AT[e] if e > 0 else CAST_B)
+            apply_mask(e)
+            if e == 2:
+                quantise_w2(4, MASK_AT[0])
+                empty_sums(3, True)
+            quantise_da(e)
+            quantise_w1(e, e + 1, 0, low[:], LAST_WORDS_AT if e == E - 1 else None)
+            if e == 0:
+                quantise_w2(3)
+                empty_sums(2, True)
+                round_w2(4, ROUNDED_AT[1], H)
+            if e == 2:
+                empty_sums(4, False)
         for e in range(E):
             second_product(e, 0)
-        high = round_w1(0, E, 1, LAST_WORDS_AT)
+        early = round_w1(0, 3, 1)
+        quantise_w1(0, 2, 1, early[:, : 2 * P, :], DA_AT[4])
+        quantise_w1(2, 3, 1, early[:, 2 * P :, :], DA_AT[4] + KIB)
+        late = round_w1(3, 5, 1, LAST_WORDS_AT)
 
-        def fetch_first(h, lo, hi, at=None):
-            name = f"first{h}_{lo}"
-            first = kept([P, hi - lo], F32, name) if at is None else placed([P, hi - lo], F32, name, at)
+        def fetch_first(h, lo, hi):
+            first = kept([P, hi - lo], F32, f"first{h}_{lo}")
             nc.vector.tensor_copy(first[:], dx[h][:].indirect(pos_sb[0][:, lo // LIST : hi // LIST]))
             return first
 
@@ -321,17 +301,12 @@ def tile_moe_bdx_mlp_relu_kernel(tc, dy_words, dy_scales, a, w2, w1, gate, offs,
             nc.vector.tensor_tensor(total[:], dx[h][:].indirect(pos_sb[1][:, lo // LIST : hi // LIST]), first, ADD)
             nc.sync.dma_start(out[h * P : (h + 1) * P, lo:hi], total[:])
 
-        early = fetch_first(0, 0, EARLY_TOKENS)
-        quantise_w1(0, 2, 1, high[:, : 2 * P, :])
-        quantise_w1(2, 3, 1, high[:, 2 * P : 3 * P, :])
-        late = fetch_first(0, EARLY_TOKENS, T, MIDDLE_RAW_AT)
-        quantise_w1(3, 5, 1, high[:, 3 * P :, :])
+        first = fetch_first(0, 0, T)
+        quantise_w1(3, 5, 1, late[:])
         for e in range(E):
             second_product(e, 1)
-        add_second(0, 0, EARLY_TOKENS, early[:], LAST_RAW_AT + KIB - 4 * EARLY_TOKENS)
-        add_second(0, EARLY_TOKENS, T, late[:], LAST_RAW_AT + KIB)
-        halves = ((0, T // 2), (T // 2, T))
-        firsts = [fetch_first(1, lo, hi) for lo, hi in halves]
+        add_second(0, 0, T, first[:], LAST_RAW_AT - 2 * KIB)
+        firsts = [fetch_first(1, lo, lo + T // 2) for lo in (0, T // 2)]
         add_second(1, 0, T // 2, firsts[0][:])
-        add_second(1, T // 2, T - 256, firsts[1][:, : T // 2 - 256])
-        add_second(1, T - 256, T, firsts[1][:, T // 2 - 256 :])
+        add_second(1, T // 2, T - LAST_TOKENS, firsts[1][:, : T // 2 - LAST_TOKENS])
+        add_second(1, T - LAST_TOKENS, T, firsts[1][:, T // 2 - LAST_TOKENS :])

@@ -36,7 +36,7 @@ DA_AT = tuple(60 * KIB + 4 * KIB * e for e in range(E))
 LAST_RAW_AT = 82 * KIB
 LAST_WORDS_AT = 86 * KIB
 A_AT = tuple(91 * KIB + 8 * KIB * e for e in range(E))
-MASK_AT = (RAW2_AT[2], A_AT[0] + 4 * KIB)
+MASK_AT = (RAW2_AT[2], A_AT[0])
 W1_RAW_AT = {(4, 1): LAST_RAW_AT}
 FIRST_ON_SCALAR = 304
 LAST_TOKENS = 256
@@ -84,7 +84,8 @@ def tile_moe_bdx_mlp_relu_kernel(tc, dy_words, dy_scales, a, w2, w1, gate, offs,
         w1_raw = {(e, h): kept([P, PACK, P], F32, f"w1_raw{e}_{h}") for e in range(E) for h in range(2) if (e, h) not in W1_RAW_AT}
         for (e, h), at in W1_RAW_AT.items():
             w1_raw[e, h] = placed([P, PACK, P], F32, f"w1_raw{e}_{h}", at)
-        a_raw = [placed([P, PACK, C], F32, f"a_raw{e}", A_AT[e]) for e in range(E)]
+        a_first = [placed([P, PACK, HALF], F32, f"a_first{j}", A_AT[0] + j * 4 * KIB) for j in range(2)]
+        a_raw = {e: placed([P, PACK, C], F32, f"a_raw{e}", A_AT[e]) for e in range(1, E)}
         da_w = [kept([P, C], U32, f"da_w{e}") for e in range(E)]
         da_s = [kept([P, C], U8, f"da_s{e}") for e in range(E)]
         dx = [kept([P, S], F32, f"dx{h}") for h in range(K // P)]
@@ -114,7 +115,8 @@ def tile_moe_bdx_mlp_relu_kernel(tc, dy_words, dy_scales, a, w2, w1, gate, offs,
         nc.sync.dma_start(dy_w[:, :T].bitcast(I32), dy_words[0].rearrange("p t d -> p (t d)").bitcast(I32))
         for e in (0, 1, 2):
             nc.sync.dma_start(w2_raw[e][:], w2_rows(e))
-        load_a(0)
+        for j in range(2):
+            nc.sync.dma_start(a_first[j][:], a_rows[:, :, j * HALF : (j + 1) * HALF])
         nc.sync.dma_start(w2_raw[3][:], w2_rows(3))
         for e in range(E):
             load_w1(e, 0)
@@ -196,8 +198,7 @@ def tile_moe_bdx_mlp_relu_kernel(tc, dy_words, dy_scales, a, w2, w1, gate, offs,
         def lift_on_gpsimd(e, at):
             lifted = placed([P, 2, 2, HALF, 2], BF16, f"lifted{e}", at)
             for half in range(2):
-                cols = slice(half * HALF, (half + 1) * HALF)
-                nc.gpsimd.tensor_scalar(lifted[:, half], pairs_view(a_raw[e][:, :, cols]), LIFT, 0.0, MULT, ADD)
+                nc.gpsimd.tensor_scalar(lifted[:, half], pairs_view(a_first[half][:]), LIFT, 0.0, MULT, ADD)
             return lifted
 
         def apply_mask(e):
@@ -264,7 +265,7 @@ def tile_moe_bdx_mlp_relu_kernel(tc, dy_words, dy_scales, a, w2, w1, gate, offs,
         empty_sums(1, False)
         round_w2(3, RAW2_AT[0], H)
         make_mask(0, lifted)
-        quantise_w2(2, A_AT[0])
+        quantise_w2(2, A_AT[0] + 4 * KIB)
         for s in range(4):
             first_product(2, s)
         for e in range(E):

@@ -31,14 +31,15 @@ KIB = 1024
 RAW2_AT = tuple(8 * KIB * e for e in range(E))
 CAST_A = 40 * KIB
 CAST_B = 44 * KIB
-ROUNDED_AT = (48 * KIB, 52 * KIB, 48 * KIB, 131 * KIB, 48 * KIB)
+ROUNDED_AT = (48 * KIB, 52 * KIB, RAW2_AT[3], RAW2_AT[4], 48 * KIB)
 DA_AT = tuple(60 * KIB + 4 * KIB * e for e in range(E))
 LAST_RAW_AT = 82 * KIB
 LAST_WORDS_AT = 86 * KIB
 A_AT = tuple(91 * KIB + 8 * KIB * e for e in range(E))
 MASK_AT = (RAW2_AT[2], A_AT[0])
-W1_RAW_AT = {(4, 1): LAST_RAW_AT}
+W1_RAW_AT = {(4, 1): LAST_RAW_AT, (1, 1): 56 * KIB}
 FIRST_ON_SCALAR = 304
+BESIDE_PRODUCT = 192
 LAST_TOKENS = 256
 WINDOW = 1408
 LIFT = 65536.0
@@ -84,8 +85,8 @@ def tile_moe_bdx_mlp_relu_kernel(tc, dy_words, dy_scales, a, w2, w1, gate, offs,
         w1_raw = {(e, h): kept([P, PACK, P], F32, f"w1_raw{e}_{h}") for e in range(E) for h in range(2) if (e, h) not in W1_RAW_AT}
         for (e, h), at in W1_RAW_AT.items():
             w1_raw[e, h] = placed([P, PACK, P], F32, f"w1_raw{e}_{h}", at)
-        a_first = [placed([P, PACK, HALF], F32, f"a_first{j}", A_AT[0] + j * 4 * KIB) for j in range(2)]
-        a_raw = {e: placed([P, PACK, C], F32, f"a_raw{e}", A_AT[e]) for e in range(1, E)}
+        a_pair = {(e, u): placed([P, 2, C], F32, f"a_pair{e}_{u}", A_AT[e] + u * 4 * KIB) for e in (0, E - 1) for u in range(2)}
+        a_raw = {e: placed([P, PACK, C], F32, f"a_raw{e}", A_AT[e]) for e in range(1, E - 1)}
         da_w = [kept([P, C], U32, f"da_w{e}") for e in range(E)]
         da_s = [kept([P, C], U8, f"da_s{e}") for e in range(E)]
         dx = [kept([P, S], F32, f"dx{h}") for h in range(K // P)]
@@ -108,6 +109,10 @@ def tile_moe_bdx_mlp_relu_kernel(tc, dy_words, dy_scales, a, w2, w1, gate, offs,
         def load_a(e):
             nc.sync.dma_start(a_raw[e][:], a_rows[:, :, e * C : (e + 1) * C])
 
+        def load_a_pairs(e):
+            for u in range(2):
+                nc.sync.dma_start(a_pair[e, u][:], a_rows[:, 2 * u : 2 * u + 2, e * C : (e + 1) * C])
+
         nc.sync.dma_start(offs_sb[:], offs)
         for q in range(4):
             (nc.scalar, nc.sync)[q % 2].dma_start(dy_s[32 * q : 32 * q + 4, :T].bitcast(I32), dy_scales[0, 4 * q : 4 * q + 4, :].bitcast(I32))
@@ -115,15 +120,17 @@ def tile_moe_bdx_mlp_relu_kernel(tc, dy_words, dy_scales, a, w2, w1, gate, offs,
         nc.sync.dma_start(dy_w[:, :T].bitcast(I32), dy_words[0].rearrange("p t d -> p (t d)").bitcast(I32))
         for e in (0, 1, 2):
             nc.sync.dma_start(w2_raw[e][:], w2_rows(e))
-        for j in range(2):
-            nc.sync.dma_start(a_first[j][:], a_rows[:, :, j * HALF : (j + 1) * HALF])
+        load_a_pairs(0)
         nc.sync.dma_start(w2_raw[3][:], w2_rows(3))
-        for e in range(E):
+        load_a(1)
+        nc.sync.dma_start(w2_raw[4][:], w2_rows(4))
+        load_a(2)
+        load_a(3)
+        for e in (3, 0, 1):
             load_w1(e, 0)
-            if e + 1 < E:
-                load_a(e + 1)
-            if e == 0:
-                nc.sync.dma_start(w2_raw[4][:], w2_rows(4))
+        load_a_pairs(4)
+        for e in (2, 4):
+            load_w1(e, 0)
         nc.sync.dma_start(pos_sb[0][:], pos1)
         nc.sync.dma_start(pos_sb[1][:], pos2)
         for e in range(E):
@@ -135,11 +142,11 @@ def tile_moe_bdx_mlp_relu_kernel(tc, dy_words, dy_scales, a, w2, w1, gate, offs,
         g_w, g_s, w2_bf, w2_q, rounded, mask, da_bf, w1_q = {}, {}, {}, {}, {}, {}, {}, {}
 
         def gather(window, dtype, into, lo, hi, at=None):
-            shape, name = [P, (hi - lo) * C], f"gathered{len(g_w) + len(g_s)}"
+            shape, name = [P, (hi - lo) * P], f"gathered{len(g_w) + len(g_s)}"
             picked = kept(shape, dtype, name) if at is None else placed(shape, dtype, name, at)
-            nc.vector.tensor_copy(picked[:], window[:].indirect(offs_sb[:, lo * C // LIST : hi * C // LIST]))
-            for e in range(lo, hi):
-                into[e] = picked[:, (e - lo) * C : (e - lo + 1) * C]
+            nc.vector.tensor_copy(picked[:], window[:].indirect(offs_sb[:, lo * P // LIST : hi * P // LIST]))
+            for b in range(lo, hi):
+                into[b] = picked[:, (b - lo) * P : (b - lo + 1) * P]
 
         def round_w2(e, at, on_scalar):
             w2_bf[e] = placed([P, H, PACK], BF16, f"w2_bf{e}", at)
@@ -149,6 +156,24 @@ def tile_moe_bdx_mlp_relu_kernel(tc, dy_words, dy_scales, a, w2, w1, gate, offs,
                 rest = w2_raw[e][:, :, on_scalar:].rearrange("p t i -> p i t")
                 nc.gpsimd.tensor_scalar(w2_bf[e][:, on_scalar:, :], rest, 1.0, 0.0, MULT, ADD)
 
+        def round_w2_in_halves(e, first_at, second_at):
+            half, cut = H // 2, H - BESIDE_PRODUCT
+            first = placed([P, half, PACK], BF16, f"w2_first{e}", first_at)
+            second = placed([P, half, PACK], BF16, f"w2_second{e}", second_at)
+            nc.scalar.copy(packed_view(first[:]), planes_view(w2_raw[e][:, :, :half]))
+            nc.scalar.copy(packed_view(second[:, : cut - half, :]), planes_view(w2_raw[e][:, :, half:cut]))
+            rest = w2_raw[e][:, :, cut:].rearrange("p t i -> p i t")
+            nc.gpsimd.tensor_scalar(second[:, cut - half :, :], rest, 1.0, 0.0, MULT, ADD)
+            return first, second
+
+        def quantise_w2_halves(e, halves):
+            words = kept([P, H], U32, f"w2_w{e}")
+            scales = kept([P, H], U8, f"w2_s{e}")
+            for j, part in enumerate(halves):
+                cols = slice(j * H // 2, (j + 1) * H // 2)
+                nc.vector.quantize_mx(out=words[:, cols].bitcast(E4M3), scales=scales[:, cols], in_=flat(part[:]))
+            w2_q[e] = (words, scales)
+
         def quantise_w2(e, at=None):
             words = kept([P, H], U32, f"w2_w{e}") if at is None else placed([P, H], U32, f"w2_w{e}", at)
             scales = kept([P, H], U8, f"w2_s{e}")
@@ -156,9 +181,9 @@ def tile_moe_bdx_mlp_relu_kernel(tc, dy_words, dy_scales, a, w2, w1, gate, offs,
             w2_q[e] = (words, scales)
 
         def first_product(e, s):
-            cols = slice(s * P, (s + 1) * P)
+            b = e * (C // P) + s
             nc.tensor.matmul_mx(
-                out=sums[s][:], lhsT=g_w[e][:, cols].bitcast(E5M2), lhsT_scale=g_s[e][:, cols],
+                out=sums[s][:], lhsT=g_w[b].bitcast(E5M2), lhsT_scale=g_s[b],
                 rhs=w2_q[e][0][:].bitcast(E4M3), rhs_scale=w2_q[e][1][:], start=True, stop=True,
             )
 
@@ -192,13 +217,21 @@ def tile_moe_bdx_mlp_relu_kernel(tc, dy_words, dy_scales, a, w2, w1, gate, offs,
             for half in range(2):
                 cols = slice(half * HALF, (half + 1) * HALF)
                 mask[e, half] = placed([P, 2, HALF, 2], BF16, f"mask{e}_{half}", MASK_AT[e % 2] + half * 2 * KIB)
-                source = pairs_view(a_raw[e][:, :, cols]) if lifted is None else lifted[:, half]
+                source = pairs_view(a_raw[e][:, :, cols]) if lifted is None else lifted[:, :, cols, :]
                 nc.vector.tensor_scalar(mask[e, half][:], source, 0.0, None, IS_GT)
 
-        def lift_on_gpsimd(e, at):
-            lifted = placed([P, 2, 2, HALF, 2], BF16, f"lifted{e}", at)
+        def make_mask_by_pairs(e):
             for half in range(2):
-                nc.gpsimd.tensor_scalar(lifted[:, half], pairs_view(a_first[half][:]), LIFT, 0.0, MULT, ADD)
+                mask[e, half] = placed([P, 2, HALF, 2], BF16, f"mask{e}_{half}", MASK_AT[e % 2] + half * 2 * KIB)
+            for u in range(2):
+                for half in range(2):
+                    source = a_pair[e, u][:, :, half * HALF : (half + 1) * HALF].rearrange("p x n -> p n x")
+                    nc.vector.tensor_scalar(mask[e, half][:, u], source, 0.0, None, IS_GT)
+
+        def lift_on_gpsimd(e, at):
+            lifted = placed([P, 2, C, 2], BF16, f"lifted{e}", at)
+            for u in range(2):
+                nc.gpsimd.tensor_scalar(lifted[:, u], a_pair[e, u][:].rearrange("p x n -> p n x"), LIFT, 0.0, MULT, ADD)
             return lifted
 
         def apply_mask(e):
@@ -245,54 +278,68 @@ def tile_moe_bdx_mlp_relu_kernel(tc, dy_words, dy_scales, a, w2, w1, gate, offs,
             )
             nc.scalar.copy(dx[h][:, e * C : (e + 1) * C], bank[:])
 
-        gather(dy_s, U8, g_s, 0, 2)
-        gather(dy_w, U32, g_w, 0, 2)
+        gather(dy_s, U8, g_s, 0, 8)
+        gather(dy_s, U8, g_s, 8, 10)
+        gather(dy_w, U32, g_w, 0, 8)
         round_w2(0, CAST_A, FIRST_ON_SCALAR)
         quantise_w2(0)
         round_w2(1, CAST_A, 0)
-        gather(dy_s, U8, g_s, 2, 4, RAW2_AT[0] + 4 * KIB)
-        gather(dy_w, U32, g_w, 2, 3, RAW2_AT[0] + 5 * KIB)
+        gather(dy_w, U32, g_w, 8, 15, RAW2_AT[0] + 4 * KIB)
+        gather(dy_s, U8, g_s, 10, 14, RAW2_AT[0] + 4 * KIB + 7 * 512)
         for s in range(4):
             first_product(0, s)
         empty_sums(0, False)
         round_w2(2, CAST_B, H)
         quantise_w2(1)
         lifted = lift_on_gpsimd(0, CAST_A)
-        gather(dy_w, U32, g_w, 3, 5, RAW2_AT[1])
-        gather(dy_s, U8, g_s, 4, 5, RAW2_AT[1] + 4 * KIB)
+        gather(dy_w, U32, g_w, 15, 20, RAW2_AT[1])
+        gather(dy_s, U8, g_s, 14, 20, RAW2_AT[1] + 4 * KIB)
         for s in range(4):
             first_product(1, s)
         empty_sums(1, False)
-        round_w2(3, RAW2_AT[0], H)
-        make_mask(0, lifted)
         quantise_w2(2, A_AT[0] + 4 * KIB)
+        make_mask(0, lifted)
+        halves = round_w2_in_halves(3, RAW2_AT[0], CAST_A)
         for s in range(4):
             first_product(2, s)
-        for e in range(E):
+        for e in range(3):
+            if e == 2:
+                quantise_w2_halves(4, halves)
+                empty_sums(3, True)
             if e > 0:
                 make_mask(e)
-            low = round_w1_on_gpsimd(e, A_AT[e] if e > 0 else CAST_B)
+            if e == 1:
+                halves = round_w2_in_halves(4, ROUNDED_AT[1], A_AT[1])
             apply_mask(e)
-            if e == 2:
-                quantise_w2(4, MASK_AT[0])
-                empty_sums(3, True)
             quantise_da(e)
-            quantise_w1(e, e + 1, 0, low[:], LAST_WORDS_AT if e == E - 1 else None)
             if e == 0:
-                quantise_w2(3)
+                quantise_w2_halves(3, halves)
                 empty_sums(2, True)
-                round_w2(4, ROUNDED_AT[1], H)
             if e == 2:
                 empty_sums(4, False)
-        for e in range(E):
+        make_mask(3)
+        low3 = round_w1_on_gpsimd(3, A_AT[3])
+        apply_mask(3)
+        quantise_da(3)
+        quantise_w1(3, 4, 0, low3[:])
+        low01 = round_w1(0, 2, 0)
+        quantise_w1(0, 2, 0, low01[:])
+        for e in (3, 0, 1):
             second_product(e, 0)
-        early = round_w1(0, 3, 1)
-        quantise_w1(0, 2, 1, early[:, : 2 * P, :], DA_AT[4])
-        quantise_w1(2, 3, 1, early[:, 2 * P :, :], DA_AT[4] + KIB)
-        late = round_w1(3, 5, 1, LAST_WORDS_AT)
+        make_mask_by_pairs(4)
+        low2 = round_w1_on_gpsimd(2, A_AT[4] + 4 * KIB)
+        apply_mask(4)
+        quantise_w1(2, 3, 0, low2[:])
+        quantise_da(4)
+        low4 = round_w1(4, 5, 0)
+        quantise_w1(4, 5, 0, low4[:], LAST_WORDS_AT)
+        second_product(2, 0)
+        second_product(4, 0)
+        upper = round_w1(0, 5, 1, LAST_WORDS_AT)
 
-        def fetch_first(h, lo, hi):
-            first = kept([P, hi - lo], F32, f"first{h}_{lo}")
+        def fetch_first(h, lo, hi, at=None):
+            name = f"first{h}_{lo}"
+            first = kept([P, hi - lo], F32, name) if at is None else placed([P, hi - lo], F32, name, at)
             nc.vector.tensor_copy(first[:], dx[h][:].indirect(pos_sb[0][:, lo // LIST : hi // LIST]))
             return first
 
@@ -302,11 +349,15 @@ def tile_moe_bdx_mlp_relu_kernel(tc, dy_words, dy_scales, a, w2, w1, gate, offs,
             nc.vector.tensor_tensor(total[:], dx[h][:].indirect(pos_sb[1][:, lo // LIST : hi // LIST]), first, ADD)
             nc.sync.dma_start(out[h * P : (h + 1) * P, lo:hi], total[:])
 
-        first = fetch_first(0, 0, T)
-        quantise_w1(3, 5, 1, late[:])
+        first_a = fetch_first(0, 0, T // 2)
+        quantise_w1(0, 2, 1, upper[:, : 2 * P, :])
+        first_b = fetch_first(0, T // 2, T, W1_RAW_AT[1, 1])
+        quantise_w1(2, 4, 1, upper[:, 2 * P : 4 * P, :])
+        quantise_w1(4, 5, 1, upper[:, 4 * P :, :])
         for e in range(E):
             second_product(e, 1)
-        add_second(0, 0, T, first[:], LAST_RAW_AT - 2 * KIB)
+        add_second(0, 0, T // 2, first_a[:], LAST_RAW_AT - 2 * KIB)
+        add_second(0, T // 2, T, first_b[:], LAST_RAW_AT + KIB // 2)
         firsts = [fetch_first(1, lo, lo + T // 2) for lo in (0, T // 2)]
         add_second(1, 0, T // 2, firsts[0][:])
         add_second(1, T // 2, T - LAST_TOKENS, firsts[1][:, : T // 2 - LAST_TOKENS])

@@ -39,7 +39,7 @@ A_AT = tuple(91 * KIB + 8 * KIB * e for e in range(E))
 MASK_AT = (RAW2_AT[2], A_AT[0])
 W1_RAW_AT = {(4, 1): LAST_RAW_AT, (1, 1): 56 * KIB}
 FIRST_ON_SCALAR = 304
-BESIDE_PRODUCT = 192
+BESIDE_PRODUCT = 128
 LAST_TOKENS = 256
 WINDOW = 1408
 LIFT = 65536.0
@@ -117,8 +117,9 @@ def tile_moe_bdx_mlp_relu_kernel(tc, dy_words, dy_scales, a, w2, w1, gate, offs,
         for q in range(4):
             (nc.scalar, nc.sync)[q % 2].dma_start(dy_s[32 * q : 32 * q + 4, :T].bitcast(I32), dy_scales[0, 4 * q : 4 * q + 4, :].bitcast(I32))
         nc.scalar.dma_start(gate_rows[0 : S // P, :], gate[0].rearrange("(c p) -> c p", p=P))
+        nc.sync.dma_start(w2_raw[0][:], w2_rows(0))
         nc.sync.dma_start(dy_w[:, :T].bitcast(I32), dy_words[0].rearrange("p t d -> p (t d)").bitcast(I32))
-        for e in (0, 1, 2):
+        for e in (1, 2):
             nc.sync.dma_start(w2_raw[e][:], w2_rows(e))
         load_a_pairs(0)
         nc.sync.dma_start(w2_raw[3][:], w2_rows(3))
@@ -279,27 +280,27 @@ def tile_moe_bdx_mlp_relu_kernel(tc, dy_words, dy_scales, a, w2, w1, gate, offs,
             nc.scalar.copy(dx[h][:, e * C : (e + 1) * C], bank[:])
 
         gather(dy_s, U8, g_s, 0, 8)
-        gather(dy_s, U8, g_s, 8, 10)
-        gather(dy_w, U32, g_w, 0, 8)
+        gather(dy_s, U8, g_s, 8, 14)
         round_w2(0, CAST_A, FIRST_ON_SCALAR)
         quantise_w2(0)
         round_w2(1, CAST_A, 0)
-        gather(dy_w, U32, g_w, 8, 15, RAW2_AT[0] + 4 * KIB)
-        gather(dy_s, U8, g_s, 10, 14, RAW2_AT[0] + 4 * KIB + 7 * 512)
+        gather(dy_w, U32, g_w, 0, 4, RAW2_AT[0] + 2 * KIB)
+        gather(dy_w, U32, g_w, 4, 12, RAW2_AT[0] + 4 * KIB)
+        gather(dy_s, U8, g_s, 14, 16, RAW2_AT[0] + 2 * KIB - 512)
         for s in range(4):
             first_product(0, s)
         empty_sums(0, False)
         round_w2(2, CAST_B, H)
         quantise_w2(1)
         lifted = lift_on_gpsimd(0, CAST_A)
-        gather(dy_w, U32, g_w, 15, 20, RAW2_AT[1])
-        gather(dy_s, U8, g_s, 14, 20, RAW2_AT[1] + 4 * KIB)
+        gather(dy_w, U32, g_w, 12, 20, RAW2_AT[1])
+        gather(dy_s, U8, g_s, 16, 20, RAW2_AT[1] + 4 * KIB)
         for s in range(4):
             first_product(1, s)
         empty_sums(1, False)
         quantise_w2(2, A_AT[0] + 4 * KIB)
         make_mask(0, lifted)
-        halves = round_w2_in_halves(3, RAW2_AT[0], CAST_A)
+        halves = round_w2_in_halves(3, RAW2_AT[1] + 6 * KIB, CAST_A)
         for s in range(4):
             first_product(2, s)
         for e in range(3):

@@ -37,8 +37,10 @@ LAST_RAW_AT = 82 * KIB
 LAST_WORDS_AT = 86 * KIB
 A_AT = tuple(91 * KIB + 8 * KIB * e for e in range(E))
 MASK_AT = (RAW2_AT[2], A_AT[0])
-W1_RAW_AT = {(4, 1): LAST_RAW_AT, (1, 1): 56 * KIB}
+W1_RAW_AT = {(4, 1): LAST_RAW_AT}
 FIRST_ON_SCALAR = 304
+SECOND_ON_SCALAR = 240
+THIRD_ON_SCALAR = 384
 BESIDE_PRODUCT = 128
 LAST_TOKENS = 256
 WINDOW = 1408
@@ -126,15 +128,17 @@ def tile_moe_bdx_mlp_relu_kernel(tc, dy_words, dy_scales, a, w2, w1, gate, offs,
         load_a(1)
         nc.sync.dma_start(w2_raw[4][:], w2_rows(4))
         load_a(2)
+        load_w1(0, 0)
         load_a(3)
-        for e in (3, 0, 1):
+        for e in (1, 2, 3):
             load_w1(e, 0)
         load_a_pairs(4)
-        for e in (2, 4):
-            load_w1(e, 0)
+        load_w1(4, 0)
         nc.sync.dma_start(pos_sb[0][:], pos1)
+        for e in range(3):
+            load_w1(e, 1)
         nc.sync.dma_start(pos_sb[1][:], pos2)
-        for e in range(E):
+        for e in range(3, E):
             load_w1(e, 1)
 
         nc.tensor.transpose(turned[3][:, 0:P], gate_rows[:], ident[:])
@@ -245,8 +249,8 @@ def tile_moe_bdx_mlp_relu_kernel(tc, dy_words, dy_scales, a, w2, w1, gate, offs,
                     MULT,
                 )
 
-        def quantise_da(e):
-            for half in range(2):
+        def quantise_da(e, halves=(0, 1)):
+            for half in halves:
                 cols = slice(half * HALF, (half + 1) * HALF)
                 nc.vector.quantize_mx(out=da_w[e][:, cols].bitcast(E5M2), scales=da_s[e][:, cols], in_=flat(da_bf[e, half][:]))
 
@@ -283,18 +287,18 @@ def tile_moe_bdx_mlp_relu_kernel(tc, dy_words, dy_scales, a, w2, w1, gate, offs,
         gather(dy_s, U8, g_s, 8, 14)
         round_w2(0, CAST_A, FIRST_ON_SCALAR)
         quantise_w2(0)
-        round_w2(1, CAST_A, 0)
+        round_w2(1, CAST_B, SECOND_ON_SCALAR)
         gather(dy_w, U32, g_w, 0, 4, RAW2_AT[0] + 2 * KIB)
-        gather(dy_w, U32, g_w, 4, 12, RAW2_AT[0] + 4 * KIB)
-        gather(dy_s, U8, g_s, 14, 16, RAW2_AT[0] + 2 * KIB - 512)
+        gather(dy_w, U32, g_w, 4, 11, RAW2_AT[0] + 4 * KIB)
         for s in range(4):
             first_product(0, s)
         empty_sums(0, False)
-        round_w2(2, CAST_B, H)
         quantise_w2(1)
+        round_w2(2, CAST_B, THIRD_ON_SCALAR)
         lifted = lift_on_gpsimd(0, CAST_A)
-        gather(dy_w, U32, g_w, 12, 20, RAW2_AT[1])
-        gather(dy_s, U8, g_s, 16, 20, RAW2_AT[1] + 4 * KIB)
+        gather(dy_w, U32, g_w, 11, 16, RAW2_AT[1])
+        gather(dy_w, U32, g_w, 16, 20, RAW2_AT[1] + 5 * 512)
+        gather(dy_s, U8, g_s, 14, 20, RAW2_AT[1] + 9 * 512)
         for s in range(4):
             first_product(1, s)
         empty_sums(1, False)
@@ -311,6 +315,8 @@ def tile_moe_bdx_mlp_relu_kernel(tc, dy_words, dy_scales, a, w2, w1, gate, offs,
                 make_mask(e)
             if e == 1:
                 halves = round_w2_in_halves(4, ROUNDED_AT[1], A_AT[1])
+            if e == 2:
+                low0 = round_w1_on_gpsimd(0, A_AT[2])
             apply_mask(e)
             quantise_da(e)
             if e == 0:
@@ -318,25 +324,27 @@ def tile_moe_bdx_mlp_relu_kernel(tc, dy_words, dy_scales, a, w2, w1, gate, offs,
                 empty_sums(2, True)
             if e == 2:
                 empty_sums(4, False)
+        quantise_w1(0, 1, 0, low0[:])
         make_mask(3)
-        low3 = round_w1_on_gpsimd(3, A_AT[3])
+        low1 = round_w1_on_gpsimd(1, A_AT[3])
+        low23 = round_w1(2, 4, 0)
         apply_mask(3)
         quantise_da(3)
-        quantise_w1(3, 4, 0, low3[:])
-        low01 = round_w1(0, 2, 0)
-        quantise_w1(0, 2, 0, low01[:])
-        for e in (3, 0, 1):
+        quantise_w1(1, 2, 0, low1[:])
+        quantise_w1(2, 4, 0, low23[:])
+        for e in range(4):
             second_product(e, 0)
         make_mask_by_pairs(4)
-        low2 = round_w1_on_gpsimd(2, A_AT[4] + 4 * KIB)
+        low4 = round_w1_on_gpsimd(4, A_AT[4] + 4 * KIB)
         apply_mask(4)
-        quantise_w1(2, 3, 0, low2[:])
-        quantise_da(4)
-        low4 = round_w1(4, 5, 0)
+        quantise_da(4, (0,))
         quantise_w1(4, 5, 0, low4[:], LAST_WORDS_AT)
-        second_product(2, 0)
+        quantise_da(4, (1,))
+        early = round_w1(0, 3, 1)
         second_product(4, 0)
-        upper = round_w1(0, 5, 1, LAST_WORDS_AT)
+        quantise_w1(0, 2, 1, early[:, : 2 * P, :], DA_AT[4])
+        quantise_w1(2, 3, 1, early[:, 2 * P :, :], DA_AT[4] + KIB)
+        late = round_w1(3, 5, 1, LAST_WORDS_AT)
 
         def fetch_first(h, lo, hi, at=None):
             name = f"first{h}_{lo}"
@@ -350,15 +358,11 @@ def tile_moe_bdx_mlp_relu_kernel(tc, dy_words, dy_scales, a, w2, w1, gate, offs,
             nc.vector.tensor_tensor(total[:], dx[h][:].indirect(pos_sb[1][:, lo // LIST : hi // LIST]), first, ADD)
             nc.sync.dma_start(out[h * P : (h + 1) * P, lo:hi], total[:])
 
-        first_a = fetch_first(0, 0, T // 2)
-        quantise_w1(0, 2, 1, upper[:, : 2 * P, :])
-        first_b = fetch_first(0, T // 2, T, W1_RAW_AT[1, 1])
-        quantise_w1(2, 4, 1, upper[:, 2 * P : 4 * P, :])
-        quantise_w1(4, 5, 1, upper[:, 4 * P :, :])
+        first = fetch_first(0, 0, T)
+        quantise_w1(3, 5, 1, late[:])
         for e in range(E):
             second_product(e, 1)
-        add_second(0, 0, T // 2, first_a[:], LAST_RAW_AT - 2 * KIB)
-        add_second(0, T // 2, T, first_b[:], LAST_RAW_AT + KIB // 2)
+        add_second(0, 0, T, first[:], LAST_RAW_AT - 2 * KIB)
         firsts = [fetch_first(1, lo, lo + T // 2) for lo in (0, T // 2)]
         add_second(1, 0, T // 2, firsts[0][:])
         add_second(1, T // 2, T - LAST_TOKENS, firsts[1][:, : T // 2 - LAST_TOKENS])

@@ -40,9 +40,9 @@ MASK_AT = (RAW2_AT[2], A_AT[0])
 W1_RAW_AT = {(4, 1): LAST_RAW_AT}
 FIRST_ON_SCALAR = 304
 SECOND_ON_SCALAR = 240
-THIRD_ON_SCALAR = 384
-BESIDE_PRODUCT = 128
-LAST_TOKENS = 256
+THIRD_ON_SCALAR = 352
+BESIDE_PRODUCT = 160
+LAST_TOKENS = 192
 WINDOW = 1408
 LIFT = 65536.0
 
@@ -78,7 +78,7 @@ def tile_moe_bdx_mlp_relu_kernel(tc, dy_words, dy_scales, a, w2, w1, gate, offs,
 
         offs_sb = keep.tile([P, S // LIST], U16, name="offs_sb")
         pos_sb = [keep.tile([P, T // LIST], U16, name=f"pos{r}_sb") for r in (1, 2)]
-        dy_w = kept([P, WINDOW], U32, "dy_w")
+        dy_w = kept([P, T], U32, "dy_w")
         dy_s = kept([P, WINDOW], U8, "dy_s")
         gate_rows = kept([P, P], F32, "gate_rows")
         gate_cols = kept([P, S // P], F32, "gate_cols")
@@ -97,7 +97,6 @@ def tile_moe_bdx_mlp_relu_kernel(tc, dy_words, dy_scales, a, w2, w1, gate, offs,
 
         nc.gpsimd.memset(dy_s[:].bitcast(I32), 0)
         nc.gpsimd.memset(gate_rows[:], 0.0)
-        nc.gpsimd.memset(dy_w[:, T:].bitcast(I32), 0)
         make_identity(nc, ident[:])
 
         a_rows = a.rearrange("(p t) s -> p t s", t=PACK)
@@ -120,7 +119,7 @@ def tile_moe_bdx_mlp_relu_kernel(tc, dy_words, dy_scales, a, w2, w1, gate, offs,
             (nc.scalar, nc.sync)[q % 2].dma_start(dy_s[32 * q : 32 * q + 4, :T].bitcast(I32), dy_scales[0, 4 * q : 4 * q + 4, :].bitcast(I32))
         nc.scalar.dma_start(gate_rows[0 : S // P, :], gate[0].rearrange("(c p) -> c p", p=P))
         nc.sync.dma_start(w2_raw[0][:], w2_rows(0))
-        nc.sync.dma_start(dy_w[:, :T].bitcast(I32), dy_words[0].rearrange("p t d -> p (t d)").bitcast(I32))
+        nc.sync.dma_start(dy_w[:].bitcast(I32), dy_words[0].rearrange("p t d -> p (t d)").bitcast(I32))
         for e in (1, 2):
             nc.sync.dma_start(w2_raw[e][:], w2_rows(e))
         load_a_pairs(0)
@@ -134,9 +133,10 @@ def tile_moe_bdx_mlp_relu_kernel(tc, dy_words, dy_scales, a, w2, w1, gate, offs,
             load_w1(e, 0)
         load_a_pairs(4)
         load_w1(4, 0)
-        nc.sync.dma_start(pos_sb[0][:], pos1)
-        for e in range(3):
+        for e in range(2):
             load_w1(e, 1)
+        nc.sync.dma_start(pos_sb[0][:], pos1)
+        load_w1(2, 1)
         nc.sync.dma_start(pos_sb[1][:], pos2)
         for e in range(3, E):
             load_w1(e, 1)

@@ -29,22 +29,22 @@ HALF = C // 2
 KIB = 1024
 
 RAW2_AT = tuple(8 * KIB * e for e in range(E))
-CAST_A = 40 * KIB
-CAST_B = 44 * KIB
-ROUNDED_AT = (48 * KIB, 52 * KIB, RAW2_AT[3], RAW2_AT[4], 48 * KIB)
-DA_AT = tuple(60 * KIB + 4 * KIB * e for e in range(E))
-LAST_RAW_AT = 82 * KIB
-LAST_WORDS_AT = 86 * KIB
-A_AT = tuple(91 * KIB + 8 * KIB * e for e in range(E))
-MASK_AT = (RAW2_AT[2], A_AT[0])
-W1_RAW_AT = {(4, 1): LAST_RAW_AT}
+A_AT = tuple(40 * KIB + 8 * KIB * e for e in range(E))
+CAST_A = 80 * KIB
+CAST_B = 84 * KIB
+SPARE = tuple(88 * KIB + 4 * KIB * j for j in range(4))
+DA_AT = tuple(104 * KIB + 4 * KIB * e for e in range(E))
+ROUNDED_AT = (SPARE[0], SPARE[1], SPARE[0], RAW2_AT[4], SPARE[1])
+MASK_AT = (RAW2_AT[3], RAW2_AT[3] + 4 * KIB, SPARE[2], SPARE[3], CAST_B)
+W1_WORDS_AT = (MASK_AT[2] + 2 * KIB, MASK_AT[2] + 3 * KIB, MASK_AT[3] + 2 * KIB, A_AT[4] + 4 * KIB, A_AT[4] + 5 * KIB)
 FIRST_ON_SCALAR = 304
-SECOND_ON_SCALAR = 240
-THIRD_ON_SCALAR = 352
-BESIDE_PRODUCT = 160
-LAST_TOKENS = 192
+W2_ON_SCALAR = (192, 96, 128)
+WORD_CUTS = (4, 10, 16, 20)
+SCALE_CUTS = (13, 16, 20)
+BESIDE_PRODUCT = 192
 WINDOW = 1408
-LIFT = 65536.0
+FIRST_RUN = 256
+RUN = 320
 
 
 def planes_view(raw):
@@ -84,11 +84,13 @@ def tile_moe_bdx_mlp_relu_kernel(tc, dy_words, dy_scales, a, w2, w1, gate, offs,
         gate_cols = kept([P, S // P], F32, "gate_cols")
         ident = kept([P, P], F32, "ident")
         w2_raw = [placed([P, PACK, H], F32, f"w2_raw{e}", RAW2_AT[e]) for e in range(E)]
-        w1_raw = {(e, h): kept([P, PACK, P], F32, f"w1_raw{e}_{h}") for e in range(E) for h in range(2) if (e, h) not in W1_RAW_AT}
-        for (e, h), at in W1_RAW_AT.items():
-            w1_raw[e, h] = placed([P, PACK, P], F32, f"w1_raw{e}_{h}", at)
-        a_pair = {(e, u): placed([P, 2, C], F32, f"a_pair{e}_{u}", A_AT[e] + u * 4 * KIB) for e in (0, E - 1) for u in range(2)}
-        a_raw = {e: placed([P, PACK, C], F32, f"a_raw{e}", A_AT[e]) for e in range(1, E - 1)}
+        w1_raw = [kept([P, PACK, K], F32, f"w1_raw{e}") for e in range(E)]
+        a_raw = [placed([P, PACK, C], F32, f"a_raw{e}", A_AT[e]) for e in range(E - 1)]
+        a_pair = [placed([P, 2, C], F32, f"a_pair{u}", A_AT[E - 1] + u * 4 * KIB) for u in range(2)]
+        w2_w = [kept([P, H], U32, f"w2_w{e}") for e in range(E)]
+        w2_s = [kept([P, H], U8, f"w2_s{e}") for e in range(E)]
+        w1_w = {}
+        w1_s = [kept([P, K], U8, f"w1_s{e}") for e in range(E)]
         da_w = [kept([P, C], U32, f"da_w{e}") for e in range(E)]
         da_s = [kept([P, C], U8, f"da_s{e}") for e in range(E)]
         dx = [kept([P, S], F32, f"dx{h}") for h in range(K // P)]
@@ -101,50 +103,43 @@ def tile_moe_bdx_mlp_relu_kernel(tc, dy_words, dy_scales, a, w2, w1, gate, offs,
 
         a_rows = a.rearrange("(p t) s -> p t s", t=PACK)
 
-        def w2_rows(e):
-            return w2[e].rearrange("(p t) i -> p t i", t=PACK)
+        def load_w2(e):
+            nc.sync.dma_start(w2_raw[e][:], w2[e].rearrange("(p t) i -> p t i", t=PACK))
 
-        def load_w1(e, h):
-            nc.sync.dma_start(w1_raw[e, h][:], w1[e].rearrange("(p t) k -> p t k", t=PACK)[:, :, h * P : (h + 1) * P])
+        def load_w1(e):
+            nc.sync.dma_start(w1_raw[e][:], w1[e].rearrange("(p t) k -> p t k", t=PACK))
 
         def load_a(e):
             nc.sync.dma_start(a_raw[e][:], a_rows[:, :, e * C : (e + 1) * C])
-
-        def load_a_pairs(e):
-            for u in range(2):
-                nc.sync.dma_start(a_pair[e, u][:], a_rows[:, 2 * u : 2 * u + 2, e * C : (e + 1) * C])
 
         nc.sync.dma_start(offs_sb[:], offs)
         for q in range(4):
             (nc.scalar, nc.sync)[q % 2].dma_start(dy_s[32 * q : 32 * q + 4, :T].bitcast(I32), dy_scales[0, 4 * q : 4 * q + 4, :].bitcast(I32))
         nc.scalar.dma_start(gate_rows[0 : S // P, :], gate[0].rearrange("(c p) -> c p", p=P))
-        nc.sync.dma_start(w2_raw[0][:], w2_rows(0))
+        load_w2(0)
         nc.sync.dma_start(dy_w[:].bitcast(I32), dy_words[0].rearrange("p t d -> p (t d)").bitcast(I32))
-        for e in (1, 2):
-            nc.sync.dma_start(w2_raw[e][:], w2_rows(e))
-        load_a_pairs(0)
-        nc.sync.dma_start(w2_raw[3][:], w2_rows(3))
+        load_w2(1)
+        load_w2(2)
+        load_w2(3)
+        load_a(0)
+        load_w2(4)
         load_a(1)
-        nc.sync.dma_start(w2_raw[4][:], w2_rows(4))
+        load_w1(0)
         load_a(2)
-        load_w1(0, 0)
+        load_w1(1)
         load_a(3)
-        for e in (1, 2, 3):
-            load_w1(e, 0)
-        load_a_pairs(4)
-        load_w1(4, 0)
-        for e in range(2):
-            load_w1(e, 1)
+        load_w1(2)
+        load_w1(3)
+        for u in range(2):
+            nc.sync.dma_start(a_pair[u][:], a_rows[:, 2 * u : 2 * u + 2, (E - 1) * C :])
+        load_w1(4)
         nc.sync.dma_start(pos_sb[0][:], pos1)
-        load_w1(2, 1)
         nc.sync.dma_start(pos_sb[1][:], pos2)
-        for e in range(3, E):
-            load_w1(e, 1)
 
         nc.tensor.transpose(turned[3][:, 0:P], gate_rows[:], ident[:])
         nc.scalar.copy(gate_cols[:], turned[3][:, 0 : S // P])
 
-        g_w, g_s, w2_bf, w2_q, rounded, mask, da_bf, w1_q = {}, {}, {}, {}, {}, {}, {}, {}
+        g_w, g_s, rounded, mask, da_bf = {}, {}, {}, {}, {}
 
         def gather(window, dtype, into, lo, hi, at=None):
             shape, name = [P, (hi - lo) * P], f"gathered{len(g_w) + len(g_s)}"
@@ -153,54 +148,36 @@ def tile_moe_bdx_mlp_relu_kernel(tc, dy_words, dy_scales, a, w2, w1, gate, offs,
             for b in range(lo, hi):
                 into[b] = picked[:, (b - lo) * P : (b - lo + 1) * P]
 
-        def round_w2(e, at, on_scalar):
-            w2_bf[e] = placed([P, H, PACK], BF16, f"w2_bf{e}", at)
-            if on_scalar > 0:
-                nc.scalar.copy(packed_view(w2_bf[e][:, :on_scalar, :]), planes_view(w2_raw[e][:, :, :on_scalar]))
-            if on_scalar < H:
-                rest = w2_raw[e][:, :, on_scalar:].rearrange("p t i -> p i t")
-                nc.gpsimd.tensor_scalar(w2_bf[e][:, on_scalar:, :], rest, 1.0, 0.0, MULT, ADD)
+        def round_columns(raw, lo, cut, hi, name, at=None):
+            shape = [P, hi - lo, PACK]
+            grouped = kept(shape, BF16, name) if at is None else placed(shape, BF16, name, at)
+            if cut > lo:
+                nc.scalar.copy(packed_view(grouped[:, : cut - lo, :]), planes_view(raw[:, :, lo:cut]))
+            if hi > cut:
+                nc.gpsimd.tensor_scalar(grouped[:, cut - lo :, :], raw[:, :, cut:hi].rearrange("p t i -> p i t"), 1.0, 0.0, MULT, ADD)
+            return grouped
 
-        def round_w2_in_halves(e, first_at, second_at):
-            half, cut = H // 2, H - BESIDE_PRODUCT
-            first = placed([P, half, PACK], BF16, f"w2_first{e}", first_at)
-            second = placed([P, half, PACK], BF16, f"w2_second{e}", second_at)
-            nc.scalar.copy(packed_view(first[:]), planes_view(w2_raw[e][:, :, :half]))
-            nc.scalar.copy(packed_view(second[:, : cut - half, :]), planes_view(w2_raw[e][:, :, half:cut]))
-            rest = w2_raw[e][:, :, cut:].rearrange("p t i -> p i t")
-            nc.gpsimd.tensor_scalar(second[:, cut - half :, :], rest, 1.0, 0.0, MULT, ADD)
-            return first, second
+        def quantise(words, scales, lo, hi, grouped, fmt):
+            nc.vector.quantize_mx(out=words[:, lo:hi].bitcast(fmt), scales=scales[:, lo:hi], in_=flat(grouped[:]))
 
-        def quantise_w2_halves(e, halves):
-            words = kept([P, H], U32, f"w2_w{e}")
-            scales = kept([P, H], U8, f"w2_s{e}")
-            for j, part in enumerate(halves):
-                cols = slice(j * H // 2, (j + 1) * H // 2)
-                nc.vector.quantize_mx(out=words[:, cols].bitcast(E4M3), scales=scales[:, cols], in_=flat(part[:]))
-            w2_q[e] = (words, scales)
-
-        def quantise_w2(e, at=None):
-            words = kept([P, H], U32, f"w2_w{e}") if at is None else placed([P, H], U32, f"w2_w{e}", at)
-            scales = kept([P, H], U8, f"w2_s{e}")
-            nc.vector.quantize_mx(out=words[:].bitcast(E4M3), scales=scales[:], in_=flat(w2_bf[e][:]))
-            w2_q[e] = (words, scales)
-
-        def first_product(e, s):
-            b = e * (C // P) + s
-            nc.tensor.matmul_mx(
-                out=sums[s][:], lhsT=g_w[b].bitcast(E5M2), lhsT_scale=g_s[b],
-                rhs=w2_q[e][0][:].bitcast(E4M3), rhs_scale=w2_q[e][1][:], start=True, stop=True,
-            )
-
-        def gate_and_round(e, s):
-            dh_bf = placed([P, H], BF16, f"dh_bf{e}_{s}", ROUNDED_AT[e] + s * KIB)
-            col = e * (C // P) + s
-            nc.scalar.activation(
-                dh_bf[:].rearrange("s (u p x) -> s u p x", u=2, x=2),
-                sums[s][:].rearrange("s (p u x) -> s u p x", u=2, x=2),
-                COPY, scale=gate_cols[:, col : col + 1],
-            )
-            rounded[e, s] = dh_bf
+        def first_products(e):
+            for s in range(4):
+                b = e * (C // P) + s
+                nc.tensor.matmul_mx(
+                    out=sums[s][:], lhsT=g_w[b].bitcast(E5M2), lhsT_scale=g_s[b],
+                    rhs=w2_w[e][:].bitcast(E4M3), rhs_scale=w2_s[e][:], start=True, stop=True,
+                )
+            for s in range(4):
+                dh_bf = placed([P, H], BF16, f"dh_bf{e}_{s}", ROUNDED_AT[e] + s * KIB)
+                col = e * (C // P) + s
+                nc.scalar.activation(
+                    dh_bf[:].rearrange("s (u p x) -> s u p x", u=2, x=2),
+                    sums[s][:].rearrange("s (p u x) -> s u p x", u=2, x=2),
+                    COPY, scale=gate_cols[:, col : col + 1],
+                )
+                rounded[e, s] = dh_bf
+                if s % 2 == 1 and e < 2:
+                    turn(e, s // 2)
 
         def turn(e, half):
             bank = turned[2 * (e % 2) + half]
@@ -210,34 +187,21 @@ def tile_moe_bdx_mlp_relu_kernel(tc, dy_words, dy_scales, a, w2, w1, gate, offs,
                     at = u * HALF + s * P
                     nc.tensor.transpose(bank[:, at : at + P], pairs[:, u * P : (u + 1) * P], ident[:])
 
-        def empty_sums(e, refill):
-            for s in range(4):
-                gate_and_round(e, s)
-                if refill:
-                    first_product(e + 1, s)
-                if s % 2 == 1:
-                    turn(e, s // 2)
-
-        def make_mask(e, lifted=None):
+        def mask_tiles(e):
             for half in range(2):
-                cols = slice(half * HALF, (half + 1) * HALF)
-                mask[e, half] = placed([P, 2, HALF, 2], BF16, f"mask{e}_{half}", MASK_AT[e % 2] + half * 2 * KIB)
-                source = pairs_view(a_raw[e][:, :, cols]) if lifted is None else lifted[:, :, cols, :]
-                nc.vector.tensor_scalar(mask[e, half][:], source, 0.0, None, IS_GT)
+                mask[e, half] = placed([P, 2, HALF, 2], BF16, f"mask{e}_{half}", MASK_AT[e] + half * 2 * KIB)
 
-        def make_mask_by_pairs(e):
+        def make_mask(e, source):
+            mask_tiles(e)
             for half in range(2):
-                mask[e, half] = placed([P, 2, HALF, 2], BF16, f"mask{e}_{half}", MASK_AT[e % 2] + half * 2 * KIB)
+                nc.vector.tensor_scalar(mask[e, half][:], source[:, :, half * HALF : (half + 1) * HALF, :], 0.0, None, IS_GT)
+
+        def make_last_mask():
+            mask_tiles(E - 1)
             for u in range(2):
                 for half in range(2):
-                    source = a_pair[e, u][:, :, half * HALF : (half + 1) * HALF].rearrange("p x n -> p n x")
-                    nc.vector.tensor_scalar(mask[e, half][:, u], source, 0.0, None, IS_GT)
-
-        def lift_on_gpsimd(e, at):
-            lifted = placed([P, 2, C, 2], BF16, f"lifted{e}", at)
-            for u in range(2):
-                nc.gpsimd.tensor_scalar(lifted[:, u], a_pair[e, u][:].rearrange("p x n -> p n x"), LIFT, 0.0, MULT, ADD)
-            return lifted
+                    source = a_pair[u][:, :, half * HALF : (half + 1) * HALF].rearrange("p x n -> p n x")
+                    nc.vector.tensor_scalar(mask[E - 1, half][:, u], source, 0.0, None, IS_GT)
 
         def apply_mask(e):
             for half in range(2):
@@ -248,122 +212,88 @@ def tile_moe_bdx_mlp_relu_kernel(tc, dy_words, dy_scales, a, w2, w1, gate, offs,
                     mask[e, half][:].rearrange("p u n x -> p n u x"),
                     MULT,
                 )
+                if e + 2 < E:
+                    turn(e + 2, half)
 
-        def quantise_da(e, halves=(0, 1)):
-            for half in halves:
-                cols = slice(half * HALF, (half + 1) * HALF)
-                nc.vector.quantize_mx(out=da_w[e][:, cols].bitcast(E5M2), scales=da_s[e][:, cols], in_=flat(da_bf[e, half][:]))
+        def quantise_da(e, half):
+            quantise(da_w[e], da_s[e], half * HALF, (half + 1) * HALF, da_bf[e, half], E5M2)
 
-        def round_w1(lo, hi, h, at=None):
-            shape, name = [P, (hi - lo) * P, PACK], f"w1_bf{lo}_{h}"
-            grouped = kept(shape, BF16, name) if at is None else placed(shape, BF16, name, at)
-            for e in range(lo, hi):
-                nc.scalar.copy(packed_view(grouped[:, (e - lo) * P : (e - lo + 1) * P, :]), planes_view(w1_raw[e, h][:]))
-            return grouped
-
-        def round_w1_on_gpsimd(e, at):
-            grouped = placed([P, P, PACK], BF16, f"w1_bf{e}_0", at)
-            nc.gpsimd.tensor_scalar(grouped[:], w1_raw[e, 0][:].rearrange("p t k -> p k t"), 1.0, 0.0, MULT, ADD)
-            return grouped
-
-        def quantise_w1(lo, hi, h, grouped, at=None):
-            shape, name = [P, (hi - lo) * P], f"w1_w{lo}_{h}"
-            words = kept(shape, U32, name) if at is None else placed(shape, U32, name, at)
-            scales = kept(shape, U8, f"w1_s{lo}_{h}")
-            nc.vector.quantize_mx(out=words[:].bitcast(E4M3), scales=scales[:], in_=flat(grouped))
-            for e in range(lo, hi):
-                cols = slice((e - lo) * P, (e - lo + 1) * P)
-                w1_q[e, h] = (words[:, cols], scales[:, cols])
-
-        def second_product(e, h):
-            bank = (sums, turned)[h][e % 4]
+        def second_product(e, h, lo, hi, bank, copy):
             nc.tensor.matmul_mx(
-                out=bank[:], lhsT=w1_q[e, h][0].bitcast(E4M3), lhsT_scale=w1_q[e, h][1],
-                rhs=da_w[e][:].bitcast(E5M2), rhs_scale=da_s[e][:], start=True, stop=True,
+                out=bank[:, : hi - lo], lhsT=w1_w[e][:, h * P : (h + 1) * P].bitcast(E4M3), lhsT_scale=w1_s[e][:, h * P : (h + 1) * P],
+                rhs=da_w[e][:, lo:hi].bitcast(E5M2), rhs_scale=da_s[e][:, lo:hi], start=True, stop=True,
             )
-            nc.scalar.copy(dx[h][:, e * C : (e + 1) * C], bank[:])
+            copy(dx[h][:, e * C + lo : e * C + hi], bank[:, : hi - lo])
+
+        def second_products(e):
+            for h in range(2):
+                second_product(e, h, 0, C, sums[2 * ((e + 1) % 2) + h], nc.scalar.copy)
+
+        def quantise_w1(e):
+            w1_w[e] = placed([P, K], U32, f"w1_w{e}", W1_WORDS_AT[e])
+            quantise(w1_w[e], w1_s[e], 0, K, w1_bf[e], E4M3)
+            if e < E - 1:
+                second_products(e)
 
         gather(dy_s, U8, g_s, 0, 8)
-        gather(dy_s, U8, g_s, 8, 14)
-        round_w2(0, CAST_A, FIRST_ON_SCALAR)
-        quantise_w2(0)
-        round_w2(1, CAST_B, SECOND_ON_SCALAR)
-        gather(dy_w, U32, g_w, 0, 4, RAW2_AT[0] + 2 * KIB)
-        gather(dy_w, U32, g_w, 4, 11, RAW2_AT[0] + 4 * KIB)
-        for s in range(4):
-            first_product(0, s)
-        empty_sums(0, False)
-        quantise_w2(1)
-        round_w2(2, CAST_B, THIRD_ON_SCALAR)
-        lifted = lift_on_gpsimd(0, CAST_A)
-        gather(dy_w, U32, g_w, 11, 16, RAW2_AT[1])
-        gather(dy_w, U32, g_w, 16, 20, RAW2_AT[1] + 5 * 512)
-        gather(dy_s, U8, g_s, 14, 20, RAW2_AT[1] + 9 * 512)
-        for s in range(4):
-            first_product(1, s)
-        empty_sums(1, False)
-        quantise_w2(2, A_AT[0] + 4 * KIB)
-        make_mask(0, lifted)
-        halves = round_w2_in_halves(3, RAW2_AT[1] + 6 * KIB, CAST_A)
-        for s in range(4):
-            first_product(2, s)
-        for e in range(3):
-            if e == 2:
-                quantise_w2_halves(4, halves)
-                empty_sums(3, True)
-            if e > 0:
-                make_mask(e)
+        gather(dy_s, U8, g_s, 8, SCALE_CUTS[0])
+        part = round_columns(w2_raw[0], 0, FIRST_ON_SCALAR, H, "w2_bf0", CAST_A)
+        quantise(w2_w[0], w2_s[0], 0, H, part, E4M3)
+        gather(dy_w, U32, g_w, 0, 4, RAW2_AT[0] + 4 * KIB)
+        for e in (1, 2, 3):
+            part = round_columns(w2_raw[e], 0, W2_ON_SCALAR[e - 1], H, f"w2_bf{e}", CAST_A)
             if e == 1:
-                halves = round_w2_in_halves(4, ROUNDED_AT[1], A_AT[1])
-            if e == 2:
-                low0 = round_w1_on_gpsimd(0, A_AT[2])
+                first_products(0)
+            gather(dy_w, U32, g_w, WORD_CUTS[e - 1], WORD_CUTS[e], RAW2_AT[e - 1])
+            if e > 1:
+                gather(dy_s, U8, g_s, SCALE_CUTS[e - 2], SCALE_CUTS[e - 1], RAW2_AT[e - 1] + 4 * KIB)
+            quantise(w2_w[e], w2_s[e], 0, H, part, E4M3)
+            if e < 3:
+                first_products(e)
+
+        make_mask(0, pairs_view(a_raw[0][:]))
+        part = round_columns(w2_raw[4], 0, H - BESIDE_PRODUCT, H, "w2_bf4", A_AT[0])
+        first_products(3)
+        apply_mask(0)
+        for half in range(2):
+            quantise_da(0, half)
+        quantise(w2_w[4], w2_s[4], 0, H, part, E4M3)
+        first_products(4)
+
+        w1_bf = {}
+        for e in (1, 2, 3):
+            make_mask(e, pairs_view(a_raw[e][:]))
+            w1_bf[e - 1] = round_columns(w1_raw[e - 1], 0, K - BESIDE_PRODUCT, K, f"w1_bf{e - 1}", A_AT[e])
             apply_mask(e)
-            quantise_da(e)
-            if e == 0:
-                quantise_w2_halves(3, halves)
-                empty_sums(2, True)
-            if e == 2:
-                empty_sums(4, False)
-        quantise_w1(0, 1, 0, low0[:])
-        make_mask(3)
-        low1 = round_w1_on_gpsimd(1, A_AT[3])
-        low23 = round_w1(2, 4, 0)
-        apply_mask(3)
-        quantise_da(3)
-        quantise_w1(1, 2, 0, low1[:])
-        quantise_w1(2, 4, 0, low23[:])
-        for e in range(4):
-            second_product(e, 0)
-        make_mask_by_pairs(4)
-        low4 = round_w1_on_gpsimd(4, A_AT[4] + 4 * KIB)
+            for half in range(2):
+                quantise_da(e, half)
+            for d in ((), (0, 1), (2,))[e - 1]:
+                quantise_w1(d)
+        w1_bf[3] = round_columns(w1_raw[3], 0, K, K, "w1_bf3", CAST_A)
+
+        make_last_mask()
+        quantise_w1(3)
+        w1_bf[4] = placed([P, K, PACK], BF16, "w1_bf4", CAST_A)
+        nc.gpsimd.tensor_scalar(w1_bf[4][:, :BESIDE_PRODUCT, :], w1_raw[4][:, :, :BESIDE_PRODUCT].rearrange("p t i -> p i t"), 1.0, 0.0, MULT, ADD)
         apply_mask(4)
-        quantise_da(4, (0,))
-        quantise_w1(4, 5, 0, low4[:], LAST_WORDS_AT)
-        quantise_da(4, (1,))
-        early = round_w1(0, 3, 1)
-        second_product(4, 0)
-        quantise_w1(0, 2, 1, early[:, : 2 * P, :], DA_AT[4])
-        quantise_w1(2, 3, 1, early[:, 2 * P :, :], DA_AT[4] + KIB)
-        late = round_w1(3, 5, 1, LAST_WORDS_AT)
+        nc.vector.tensor_copy(packed_view(w1_bf[4][:, BESIDE_PRODUCT:, :]), planes_view(w1_raw[4][:, :, BESIDE_PRODUCT:]))
+        quantise_da(4, 0)
+        quantise_w1(4)
+        quantise_da(4, 1)
+        for half in range(2):
+            second_product(4, 0, half * HALF, (half + 1) * HALF, turned[2 + half], nc.scalar.copy)
+        second_product(4, 1, 0, C, sums[2], nc.vector.tensor_copy)
 
-        def fetch_first(h, lo, hi, at=None):
-            name = f"first{h}_{lo}"
-            first = kept([P, hi - lo], F32, name) if at is None else placed([P, hi - lo], F32, name, at)
-            nc.vector.tensor_copy(first[:], dx[h][:].indirect(pos_sb[0][:, lo // LIST : hi // LIST]))
-            return first
-
-        def add_second(h, lo, hi, first, at=None):
-            name = f"total{h}_{lo}"
-            total = kept([P, hi - lo], F32, name) if at is None else placed([P, hi - lo], F32, name, at)
-            nc.vector.tensor_tensor(total[:], dx[h][:].indirect(pos_sb[1][:, lo // LIST : hi // LIST]), first, ADD)
+        def bring_back(h, lo, hi):
+            first = kept([P, hi - lo], F32, f"first{h}_{lo}")
+            total = kept([P, hi - lo], F32, f"total{h}_{lo}")
+            nc.scalar.activation(first[:], dx[h][:].indirect(pos_sb[0][:, lo // LIST : hi // LIST]), COPY)
+            nc.vector.tensor_tensor(total[:], dx[h][:].indirect(pos_sb[1][:, lo // LIST : hi // LIST]), first[:], ADD)
             nc.sync.dma_start(out[h * P : (h + 1) * P, lo:hi], total[:])
 
-        first = fetch_first(0, 0, T)
-        quantise_w1(3, 5, 1, late[:])
-        for e in range(E):
-            second_product(e, 1)
-        add_second(0, 0, T, first[:], LAST_RAW_AT - 2 * KIB)
-        firsts = [fetch_first(1, lo, lo + T // 2) for lo in (0, T // 2)]
-        add_second(1, 0, T // 2, firsts[0][:])
-        add_second(1, T // 2, T - LAST_TOKENS, firsts[1][:, : T // 2 - LAST_TOKENS])
-        add_second(1, T - LAST_TOKENS, T, firsts[1][:, T // 2 - LAST_TOKENS :])
+        cuts = (0, FIRST_RUN, FIRST_RUN + RUN, FIRST_RUN + 2 * RUN, T)
+        for lo, hi in zip(cuts, cuts[1:]):
+            bring_back(0, lo, hi)
+        cuts = (0, 512, 1024, T)
+        for lo, hi in zip(cuts, cuts[1:]):
+            bring_back(1, lo, hi)

@@ -36,15 +36,15 @@ SPARE = tuple(88 * KIB + 4 * KIB * j for j in range(4))
 DA_AT = tuple(104 * KIB + 4 * KIB * e for e in range(E))
 ROUNDED_AT = (SPARE[0], SPARE[1], SPARE[0], RAW2_AT[4], SPARE[1])
 MASK_AT = (RAW2_AT[3], RAW2_AT[3] + 4 * KIB, SPARE[2], SPARE[3], CAST_B)
-W1_WORDS_AT = (MASK_AT[2] + 2 * KIB, MASK_AT[2] + 3 * KIB, MASK_AT[3] + 2 * KIB, A_AT[4] + 4 * KIB, A_AT[4] + 5 * KIB)
+RAW1_AT = tuple(124 * KIB + 4 * KIB * e for e in range(E))
+W1_WORDS_AT = (MASK_AT[1] + 2 * KIB, MASK_AT[2] + 2 * KIB, MASK_AT[3] + 2 * KIB, MASK_AT[3], A_AT[4] + KIB)
 FIRST_ON_SCALAR = 304
-W2_ON_SCALAR = (192, 96, 128)
+W2_ON_SCALAR = (192, 128, 160)
 WORD_CUTS = (4, 10, 16, 20)
 SCALE_CUTS = (13, 16, 20)
-BESIDE_PRODUCT = 192
+BESIDE_PRODUCT = 160
 WINDOW = 1408
-FIRST_RUN = 256
-RUN = 320
+RUNS = ((0, 0, 256), (0, 256, 576), (0, 576, 896), (1, 0, 256), (0, 896, T), (1, 256, 576), (1, 576, 896), (1, 896, 1152), (1, 1152, T))
 
 
 def planes_view(raw):
@@ -84,7 +84,7 @@ def tile_moe_bdx_mlp_relu_kernel(tc, dy_words, dy_scales, a, w2, w1, gate, offs,
         gate_cols = kept([P, S // P], F32, "gate_cols")
         ident = kept([P, P], F32, "ident")
         w2_raw = [placed([P, PACK, H], F32, f"w2_raw{e}", RAW2_AT[e]) for e in range(E)]
-        w1_raw = [kept([P, PACK, K], F32, f"w1_raw{e}") for e in range(E)]
+        w1_raw = [placed([P, PACK, K], F32, f"w1_raw{e}", RAW1_AT[e]) for e in range(E)]
         a_raw = [placed([P, PACK, C], F32, f"a_raw{e}", A_AT[e]) for e in range(E - 1)]
         a_pair = [placed([P, 2, C], F32, f"a_pair{u}", A_AT[E - 1] + u * 4 * KIB) for u in range(2)]
         w2_w = [kept([P, H], U32, f"w2_w{e}") for e in range(E)]
@@ -196,12 +196,10 @@ def tile_moe_bdx_mlp_relu_kernel(tc, dy_words, dy_scales, a, w2, w1, gate, offs,
             for half in range(2):
                 nc.vector.tensor_scalar(mask[e, half][:], source[:, :, half * HALF : (half + 1) * HALF, :], 0.0, None, IS_GT)
 
-        def make_last_mask():
-            mask_tiles(E - 1)
-            for u in range(2):
-                for half in range(2):
-                    source = a_pair[u][:, :, half * HALF : (half + 1) * HALF].rearrange("p x n -> p n x")
-                    nc.vector.tensor_scalar(mask[E - 1, half][:, u], source, 0.0, None, IS_GT)
+        def make_last_mask(u):
+            for half in range(2):
+                source = a_pair[u][:, :, half * HALF : (half + 1) * HALF].rearrange("p x n -> p n x")
+                nc.vector.tensor_scalar(mask[E - 1, half][:, u], source, 0.0, None, IS_GT)
 
         def apply_mask(e):
             for half in range(2):
@@ -227,11 +225,13 @@ def tile_moe_bdx_mlp_relu_kernel(tc, dy_words, dy_scales, a, w2, w1, gate, offs,
 
         def second_products(e):
             for h in range(2):
-                second_product(e, h, 0, C, sums[2 * ((e + 1) % 2) + h], nc.scalar.copy)
+                second_product(e, h, 0, C, sums[2 * (e % 2) + h], nc.scalar.copy)
 
         def quantise_w1(e):
             w1_w[e] = placed([P, K], U32, f"w1_w{e}", W1_WORDS_AT[e])
-            quantise(w1_w[e], w1_s[e], 0, K, w1_bf[e], E4M3)
+            width = K // len(w1_bf[e])
+            for j, grouped in enumerate(w1_bf[e]):
+                quantise(w1_w[e], w1_s[e], j * width, (j + 1) * width, grouped, E4M3)
             if e < E - 1:
                 second_products(e)
 
@@ -251,49 +251,58 @@ def tile_moe_bdx_mlp_relu_kernel(tc, dy_words, dy_scales, a, w2, w1, gate, offs,
             if e < 3:
                 first_products(e)
 
+        early = round_columns(w2_raw[4], 0, H - P, H - P, "w2_bf4a", CAST_B)
         make_mask(0, pairs_view(a_raw[0][:]))
-        part = round_columns(w2_raw[4], 0, H - BESIDE_PRODUCT, H, "w2_bf4", A_AT[0])
+        late = round_columns(w2_raw[4], H - P, H - P, H, "w2_bf4b", A_AT[0])
         first_products(3)
         apply_mask(0)
         for half in range(2):
             quantise_da(0, half)
-        quantise(w2_w[4], w2_s[4], 0, H, part, E4M3)
+        quantise(w2_w[4], w2_s[4], H - P, H, late, E4M3)
+        quantise(w2_w[4], w2_s[4], 0, H - P, early, E4M3)
+        w1_bf = {0: [round_columns(w1_raw[0], P, K, K, "w1_high0")]}
         first_products(4)
 
-        w1_bf = {}
         for e in (1, 2, 3):
             make_mask(e, pairs_view(a_raw[e][:]))
-            w1_bf[e - 1] = round_columns(w1_raw[e - 1], 0, K - BESIDE_PRODUCT, K, f"w1_bf{e - 1}", A_AT[e])
+            w1_bf[e - 1] = [round_columns(w1_raw[e - 1], 0, 0, P, f"w1_low{e - 1}", A_AT[e])] + w1_bf[e - 1]
             apply_mask(e)
+            if e == 3:
+                quantise_w1(2)
             for half in range(2):
                 quantise_da(e, half)
-            for d in ((), (0, 1), (2,))[e - 1]:
-                quantise_w1(d)
-        w1_bf[3] = round_columns(w1_raw[3], 0, K, K, "w1_bf3", CAST_A)
-
-        make_last_mask()
+            if e < 3:
+                quantise_w1(e - 1)
+                w1_bf[e] = [round_columns(w1_raw[e], P, K, K, f"w1_high{e}")]
+            if e == 2:
+                w1_bf[3] = [round_columns(w1_raw[3], 0, K, K, "w1_bf3", CAST_A)]
         quantise_w1(3)
-        w1_bf[4] = placed([P, K, PACK], BF16, "w1_bf4", CAST_A)
-        nc.gpsimd.tensor_scalar(w1_bf[4][:, :BESIDE_PRODUCT, :], w1_raw[4][:, :, :BESIDE_PRODUCT].rearrange("p t i -> p i t"), 1.0, 0.0, MULT, ADD)
+
+        mask_tiles(E - 1)
+        for u in range(2):
+            make_last_mask(u)
+        last = placed([P, K, PACK], BF16, "w1_bf4", A_AT[4] + 4 * KIB)
+        w1_bf[4] = [last]
+        nc.gpsimd.tensor_scalar(last[:, :BESIDE_PRODUCT, :], w1_raw[4][:, :, :BESIDE_PRODUCT].rearrange("p t i -> p i t"), 1.0, 0.0, MULT, ADD)
         apply_mask(4)
-        nc.vector.tensor_copy(packed_view(w1_bf[4][:, BESIDE_PRODUCT:, :]), planes_view(w1_raw[4][:, :, BESIDE_PRODUCT:]))
+        nc.vector.tensor_copy(packed_view(last[:, BESIDE_PRODUCT:, :]), planes_view(w1_raw[4][:, :, BESIDE_PRODUCT:]))
         quantise_da(4, 0)
         quantise_w1(4)
         quantise_da(4, 1)
         for half in range(2):
             second_product(4, 0, half * HALF, (half + 1) * HALF, turned[2 + half], nc.scalar.copy)
-        second_product(4, 1, 0, C, sums[2], nc.vector.tensor_copy)
+        second_product(4, 1, 0, C, sums[0], nc.vector.tensor_copy)
 
-        def bring_back(h, lo, hi):
+        def bring_back(h, lo, hi, on_vector):
             first = kept([P, hi - lo], F32, f"first{h}_{lo}")
             total = kept([P, hi - lo], F32, f"total{h}_{lo}")
-            nc.scalar.activation(first[:], dx[h][:].indirect(pos_sb[0][:, lo // LIST : hi // LIST]), COPY)
+            picked = dx[h][:].indirect(pos_sb[0][:, lo // LIST : hi // LIST])
+            if on_vector:
+                nc.vector.tensor_copy(first[:], picked)
+            else:
+                nc.scalar.activation(first[:], picked, COPY)
             nc.vector.tensor_tensor(total[:], dx[h][:].indirect(pos_sb[1][:, lo // LIST : hi // LIST]), first[:], ADD)
             nc.sync.dma_start(out[h * P : (h + 1) * P, lo:hi], total[:])
 
-        cuts = (0, FIRST_RUN, FIRST_RUN + RUN, FIRST_RUN + 2 * RUN, T)
-        for lo, hi in zip(cuts, cuts[1:]):
-            bring_back(0, lo, hi)
-        cuts = (0, 512, 1024, T)
-        for lo, hi in zip(cuts, cuts[1:]):
-            bring_back(1, lo, hi)
+        for h, lo, hi in RUNS:
+            bring_back(h, lo, hi, lo == 0)

@@ -37,14 +37,15 @@ DA_AT = tuple(104 * KIB + 4 * KIB * e for e in range(E))
 ROUNDED_AT = (SPARE[0], SPARE[1], SPARE[0], RAW2_AT[4], SPARE[1])
 MASK_AT = (RAW2_AT[3], RAW2_AT[3] + 4 * KIB, SPARE[2], SPARE[3], CAST_B)
 RAW1_AT = tuple(124 * KIB + 4 * KIB * e for e in range(E))
-W1_WORDS_AT = (MASK_AT[1] + 2 * KIB, MASK_AT[2] + 2 * KIB, MASK_AT[3] + 2 * KIB, MASK_AT[3], A_AT[4] + KIB)
+W1_WORDS_AT = (MASK_AT[1] + 2 * KIB, MASK_AT[2] + 2 * KIB, MASK_AT[3] + 2 * KIB, A_AT[4] + 4 * KIB, A_AT[4] + KIB)
 FIRST_ON_SCALAR = 304
 W2_ON_SCALAR = (192, 128, 160)
 WORD_CUTS = (4, 10, 16, 20)
 SCALE_CUTS = (13, 16, 20)
 BESIDE_PRODUCT = 160
 WINDOW = 1408
-RUNS = ((0, 0, 256), (0, 256, 576), (0, 576, 896), (1, 0, 256), (0, 896, T), (1, 256, 576), (1, 576, 896), (1, 896, 1152), (1, 1152, T))
+LOW_CUTS = (0, 256, 576, 928, T)
+HIGH_CUTS = (0, 384, 768, 1120, T)
 
 
 def planes_view(raw):
@@ -91,7 +92,7 @@ def tile_moe_bdx_mlp_relu_kernel(tc, dy_words, dy_scales, a, w2, w1, gate, offs,
         w2_s = [kept([P, H], U8, f"w2_s{e}") for e in range(E)]
         w1_w = {}
         w1_s = [kept([P, K], U8, f"w1_s{e}") for e in range(E)]
-        da_w = [kept([P, C], U32, f"da_w{e}") for e in range(E)]
+        da_w = [kept([P, C], U32, f"da_w{e}") for e in range(E - 1)]
         da_s = [kept([P, C], U8, f"da_s{e}") for e in range(E)]
         dx = [kept([P, S], F32, f"dx{h}") for h in range(K // P)]
         sums = [psum.tile([P, C], F32, name=f"sums{b}") for b in range(4)]
@@ -129,9 +130,9 @@ def tile_moe_bdx_mlp_relu_kernel(tc, dy_words, dy_scales, a, w2, w1, gate, offs,
         load_w1(1)
         load_a(3)
         load_w1(2)
-        load_w1(3)
         for u in range(2):
             nc.sync.dma_start(a_pair[u][:], a_rows[:, 2 * u : 2 * u + 2, (E - 1) * C :])
+        load_w1(3)
         load_w1(4)
         nc.sync.dma_start(pos_sb[0][:], pos1)
         nc.sync.dma_start(pos_sb[1][:], pos2)
@@ -139,7 +140,7 @@ def tile_moe_bdx_mlp_relu_kernel(tc, dy_words, dy_scales, a, w2, w1, gate, offs,
         nc.tensor.transpose(turned[3][:, 0:P], gate_rows[:], ident[:])
         nc.scalar.copy(gate_cols[:], turned[3][:, 0 : S // P])
 
-        g_w, g_s, rounded, mask, da_bf = {}, {}, {}, {}, {}
+        g_w, g_s, rounded, mask, da_bf, last_w = {}, {}, {}, {}, {}, {}
 
         def gather(window, dtype, into, lo, hi, at=None):
             shape, name = [P, (hi - lo) * P], f"gathered{len(g_w) + len(g_s)}"
@@ -218,7 +219,7 @@ def tile_moe_bdx_mlp_relu_kernel(tc, dy_words, dy_scales, a, w2, w1, gate, offs,
 
         def second_product(e, h, lo, hi, bank, copy):
             nc.tensor.matmul_mx(
-                out=bank[:, : hi - lo], lhsT=w1_w[e][:, h * P : (h + 1) * P].bitcast(E4M3), lhsT_scale=w1_s[e][:, h * P : (h + 1) * P],
+                out=bank[:, : hi - lo], lhsT=w1_w[e, h].bitcast(E4M3), lhsT_scale=w1_s[e][:, h * P : (h + 1) * P],
                 rhs=da_w[e][:, lo:hi].bitcast(E5M2), rhs_scale=da_s[e][:, lo:hi], start=True, stop=True,
             )
             copy(dx[h][:, e * C + lo : e * C + hi], bank[:, : hi - lo])
@@ -228,12 +229,31 @@ def tile_moe_bdx_mlp_relu_kernel(tc, dy_words, dy_scales, a, w2, w1, gate, offs,
                 second_product(e, h, 0, C, sums[2 * (e % 2) + h], nc.scalar.copy)
 
         def quantise_w1(e):
-            w1_w[e] = placed([P, K], U32, f"w1_w{e}", W1_WORDS_AT[e])
+            words = placed([P, K], U32, f"w1_w{e}", W1_WORDS_AT[e])
             width = K // len(w1_bf[e])
             for j, grouped in enumerate(w1_bf[e]):
-                quantise(w1_w[e], w1_s[e], j * width, (j + 1) * width, grouped, E4M3)
-            if e < E - 1:
+                quantise(words, w1_s[e], j * width, (j + 1) * width, grouped, E4M3)
+            for h in range(2):
+                w1_w[e, h] = words[:, h * P : (h + 1) * P]
+            if e < 3:
                 second_products(e)
+
+        def quantise_w1_half(e, h, at):
+            words = placed([P, P], U32, f"w1_w{e}_{h}", at)
+            cols = slice(h * P, (h + 1) * P)
+            nc.vector.quantize_mx(out=words[:].bitcast(E4M3), scales=w1_s[e][:, cols], in_=flat(w1_bf[e][0][:, cols, :]))
+            w1_w[e, h] = words[:]
+
+        def quantise_last_da(half, at):
+            last_w[half] = placed([P, HALF], U32, f"last_w{half}", at)
+            cols = slice(half * HALF, (half + 1) * HALF)
+            nc.vector.quantize_mx(out=last_w[half][:].bitcast(E5M2), scales=da_s[4][:, cols], in_=flat(da_bf[4, half][:]))
+
+        def last_product(h, half, bank):
+            nc.tensor.matmul_mx(
+                out=bank, lhsT=w1_w[4, h].bitcast(E4M3), lhsT_scale=w1_s[4][:, h * P : (h + 1) * P],
+                rhs=last_w[half][:].bitcast(E5M2), rhs_scale=da_s[4][:, half * HALF : (half + 1) * HALF], start=True, stop=True,
+            )
 
         gather(dy_s, U8, g_s, 0, 8)
         gather(dy_s, U8, g_s, 8, SCALE_CUTS[0])
@@ -274,35 +294,31 @@ def tile_moe_bdx_mlp_relu_kernel(tc, dy_words, dy_scales, a, w2, w1, gate, offs,
             if e < 3:
                 quantise_w1(e - 1)
                 w1_bf[e] = [round_columns(w1_raw[e], P, K, K, f"w1_high{e}")]
-            if e == 2:
-                w1_bf[3] = [round_columns(w1_raw[3], 0, K, K, "w1_bf3", CAST_A)]
-        quantise_w1(3)
+        w1_bf[3] = [round_columns(w1_raw[3], 0, K, K, "w1_bf3", CAST_A)]
 
         mask_tiles(E - 1)
         for u in range(2):
             make_last_mask(u)
-        last = placed([P, K, PACK], BF16, "w1_bf4", A_AT[4] + 4 * KIB)
-        w1_bf[4] = [last]
-        nc.gpsimd.tensor_scalar(last[:, :BESIDE_PRODUCT, :], w1_raw[4][:, :, :BESIDE_PRODUCT].rearrange("p t i -> p i t"), 1.0, 0.0, MULT, ADD)
+        w1_bf[4] = [round_columns(w1_raw[4], 0, K - BESIDE_PRODUCT, K, "w1_bf4", A_AT[4] + 4 * KIB)]
         apply_mask(4)
-        nc.vector.tensor_copy(packed_view(last[:, BESIDE_PRODUCT:, :]), planes_view(w1_raw[4][:, :, BESIDE_PRODUCT:]))
-        quantise_da(4, 0)
+        quantise_w1_half(3, 0, MASK_AT[4] + 2 * KIB)
+        second_product(3, 0, 0, C, sums[2], nc.scalar.copy)
+        quantise_last_da(0, MASK_AT[4])
         quantise_w1(4)
-        quantise_da(4, 1)
+        quantise_last_da(1, RAW1_AT[4])
+        quantise_w1_half(3, 1, RAW1_AT[4] + KIB)
         for half in range(2):
-            second_product(4, 0, half * HALF, (half + 1) * HALF, turned[2 + half], nc.scalar.copy)
-        second_product(4, 1, 0, C, sums[0], nc.vector.tensor_copy)
+            last_product(0, half, turned[2 + half][:, :HALF])
+            nc.scalar.copy(dx[0][:, 4 * C + half * HALF : 4 * C + (half + 1) * HALF], turned[2 + half][:, :HALF])
+        second_product(3, 1, 0, C, sums[3], nc.vector.tensor_copy)
+        for half in range(2):
+            last_product(1, half, sums[0][:, half * HALF : (half + 1) * HALF])
+        nc.vector.tensor_copy(dx[1][:, 4 * C :], sums[0][:])
 
-        def bring_back(h, lo, hi, on_vector):
-            first = kept([P, hi - lo], F32, f"first{h}_{lo}")
-            total = kept([P, hi - lo], F32, f"total{h}_{lo}")
-            picked = dx[h][:].indirect(pos_sb[0][:, lo // LIST : hi // LIST])
-            if on_vector:
-                nc.vector.tensor_copy(first[:], picked)
-            else:
-                nc.scalar.activation(first[:], picked, COPY)
-            nc.vector.tensor_tensor(total[:], dx[h][:].indirect(pos_sb[1][:, lo // LIST : hi // LIST]), first[:], ADD)
-            nc.sync.dma_start(out[h * P : (h + 1) * P, lo:hi], total[:])
-
-        for h, lo, hi in RUNS:
-            bring_back(h, lo, hi, lo == 0)
+        for h, cuts in enumerate((LOW_CUTS, HIGH_CUTS)):
+            for lo, hi in zip(cuts, cuts[1:]):
+                first = kept([P, hi - lo], F32, f"first{h}_{lo}")
+                total = kept([P, hi - lo], F32, f"total{h}_{lo}")
+                nc.scalar.activation(first[:], dx[h][:].indirect(pos_sb[0][:, lo // LIST : hi // LIST]), COPY)
+                nc.vector.tensor_tensor(total[:], dx[h][:].indirect(pos_sb[1][:, lo // LIST : hi // LIST]), first[:], ADD)
+                nc.sync.dma_start(out[h * P : (h + 1) * P, lo:hi], total[:])

@@ -37,13 +37,11 @@ DA_AT = tuple(104 * KIB + 4 * KIB * e for e in range(E))
 ROUNDED_AT = (SPARE[0], SPARE[1], SPARE[0], RAW2_AT[4], SPARE[1])
 MASK_AT = (RAW2_AT[3], RAW2_AT[3] + 4 * KIB, SPARE[2], SPARE[3], CAST_B)
 RAW1_AT = tuple(124 * KIB + 4 * KIB * e for e in range(E))
-W1_WORDS_AT = (MASK_AT[1] + 2 * KIB, MASK_AT[2] + 2 * KIB, MASK_AT[3] + 2 * KIB, A_AT[4] + 4 * KIB, A_AT[4] + KIB)
+W1_WORDS_AT = (MASK_AT[1] + 2 * KIB, MASK_AT[2] + 2 * KIB, MASK_AT[3] + 2 * KIB)
 FIRST_ON_SCALAR = 304
 W2_ON_SCALAR = (192, 128, 160)
 WORD_CUTS = (4, 10, 16, 20)
 SCALE_CUTS = (13, 16, 20)
-BESIDE_PRODUCT = 160
-WINDOW = 1408
 LOW_CUTS = (0, 256, 576, 928, T)
 HIGH_CUTS = (0, 384, 768, 1120, T)
 
@@ -80,12 +78,13 @@ def tile_moe_bdx_mlp_relu_kernel(tc, dy_words, dy_scales, a, w2, w1, gate, offs,
         offs_sb = keep.tile([P, S // LIST], U16, name="offs_sb")
         pos_sb = [keep.tile([P, T // LIST], U16, name=f"pos{r}_sb") for r in (1, 2)]
         dy_w = kept([P, T], U32, "dy_w")
-        dy_s = kept([P, WINDOW], U8, "dy_s")
+        dy_s = kept([P, T], U8, "dy_s")
         gate_rows = kept([P, P], F32, "gate_rows")
         gate_cols = kept([P, S // P], F32, "gate_cols")
         ident = kept([P, P], F32, "ident")
         w2_raw = [placed([P, PACK, H], F32, f"w2_raw{e}", RAW2_AT[e]) for e in range(E)]
-        w1_raw = [placed([P, PACK, K], F32, f"w1_raw{e}", RAW1_AT[e]) for e in range(E)]
+        w1_raw = [placed([P, PACK, K], F32, f"w1_raw{e}", RAW1_AT[e]) for e in range(3)]
+        w1_half = {(e, h): placed([P, PACK, P], F32, f"w1_half{e}_{h}", RAW1_AT[e] + 2 * KIB * h) for e in (3, 4) for h in range(2)}
         a_raw = [placed([P, PACK, C], F32, f"a_raw{e}", A_AT[e]) for e in range(E - 1)]
         a_pair = [placed([P, 2, C], F32, f"a_pair{u}", A_AT[E - 1] + u * 4 * KIB) for u in range(2)]
         w2_w = [kept([P, H], U32, f"w2_w{e}") for e in range(E)]
@@ -98,7 +97,6 @@ def tile_moe_bdx_mlp_relu_kernel(tc, dy_words, dy_scales, a, w2, w1, gate, offs,
         sums = [psum.tile([P, C], F32, name=f"sums{b}") for b in range(4)]
         turned = [psum.tile([P, C], F32, name=f"turned{b}") for b in range(4)]
 
-        nc.gpsimd.memset(dy_s[:].bitcast(I32), 0)
         nc.gpsimd.memset(gate_rows[:], 0.0)
         make_identity(nc, ident[:])
 
@@ -110,12 +108,16 @@ def tile_moe_bdx_mlp_relu_kernel(tc, dy_words, dy_scales, a, w2, w1, gate, offs,
         def load_w1(e):
             nc.sync.dma_start(w1_raw[e][:], w1[e].rearrange("(p t) k -> p t k", t=PACK))
 
+        def load_w1_half(e, h):
+            nc.sync.dma_start(w1_half[e, h][:], w1[e].rearrange("(p t) k -> p t k", t=PACK)[:, :, h * P : (h + 1) * P])
+
         def load_a(e):
             nc.sync.dma_start(a_raw[e][:], a_rows[:, :, e * C : (e + 1) * C])
 
         nc.sync.dma_start(offs_sb[:], offs)
         for q in range(4):
-            (nc.scalar, nc.sync)[q % 2].dma_start(dy_s[32 * q : 32 * q + 4, :T].bitcast(I32), dy_scales[0, 4 * q : 4 * q + 4, :].bitcast(I32))
+            rows = dy_scales[0, 4 * q : 4 * q + 4, :].bitcast(I32).unsqueeze(0).to_broadcast([8, 4, T // 4])
+            (nc.scalar, nc.sync)[q % 2].dma_start(dy_s[32 * q : 32 * q + 32, :].bitcast(I32), rows)
         nc.scalar.dma_start(gate_rows[0 : S // P, :], gate[0].rearrange("(c p) -> c p", p=P))
         load_w2(0)
         nc.sync.dma_start(dy_w[:].bitcast(I32), dy_words[0].rearrange("p t d -> p (t d)").bitcast(I32))
@@ -132,10 +134,12 @@ def tile_moe_bdx_mlp_relu_kernel(tc, dy_words, dy_scales, a, w2, w1, gate, offs,
         load_w1(2)
         for u in range(2):
             nc.sync.dma_start(a_pair[u][:], a_rows[:, 2 * u : 2 * u + 2, (E - 1) * C :])
-        load_w1(3)
-        load_w1(4)
+        for e in (3, 4):
+            load_w1_half(e, 0)
         nc.sync.dma_start(pos_sb[0][:], pos1)
         nc.sync.dma_start(pos_sb[1][:], pos2)
+        for e in (3, 4):
+            load_w1_half(e, 1)
 
         nc.tensor.transpose(turned[3][:, 0:P], gate_rows[:], ident[:])
         nc.scalar.copy(gate_cols[:], turned[3][:, 0 : S // P])
@@ -235,13 +239,12 @@ def tile_moe_bdx_mlp_relu_kernel(tc, dy_words, dy_scales, a, w2, w1, gate, offs,
                 quantise(words, w1_s[e], j * width, (j + 1) * width, grouped, E4M3)
             for h in range(2):
                 w1_w[e, h] = words[:, h * P : (h + 1) * P]
-            if e < 3:
-                second_products(e)
+            second_products(e)
 
-        def quantise_w1_half(e, h, at):
+        def quantise_w1_half(e, h, grouped, at):
             words = placed([P, P], U32, f"w1_w{e}_{h}", at)
             cols = slice(h * P, (h + 1) * P)
-            nc.vector.quantize_mx(out=words[:].bitcast(E4M3), scales=w1_s[e][:, cols], in_=flat(w1_bf[e][0][:, cols, :]))
+            nc.vector.quantize_mx(out=words[:].bitcast(E4M3), scales=w1_s[e][:, cols], in_=flat(grouped[:]))
             w1_w[e, h] = words[:]
 
         def quantise_last_da(half, at):
@@ -255,8 +258,8 @@ def tile_moe_bdx_mlp_relu_kernel(tc, dy_words, dy_scales, a, w2, w1, gate, offs,
                 rhs=last_w[half][:].bitcast(E5M2), rhs_scale=da_s[4][:, half * HALF : (half + 1) * HALF], start=True, stop=True,
             )
 
-        gather(dy_s, U8, g_s, 0, 8)
-        gather(dy_s, U8, g_s, 8, SCALE_CUTS[0])
+        gather(dy_s, U8, g_s, 0, 7)
+        gather(dy_s, U8, g_s, 7, SCALE_CUTS[0])
         part = round_columns(w2_raw[0], 0, FIRST_ON_SCALAR, H, "w2_bf0", CAST_A)
         quantise(w2_w[0], w2_s[0], 0, H, part, E4M3)
         gather(dy_w, U32, g_w, 0, 4, RAW2_AT[0] + 4 * KIB)
@@ -294,19 +297,23 @@ def tile_moe_bdx_mlp_relu_kernel(tc, dy_words, dy_scales, a, w2, w1, gate, offs,
             if e < 3:
                 quantise_w1(e - 1)
                 w1_bf[e] = [round_columns(w1_raw[e], P, K, K, f"w1_high{e}")]
-        w1_bf[3] = [round_columns(w1_raw[3], 0, K, K, "w1_bf3", CAST_A)]
+        low = {e: round_columns(w1_half[e, 0], 0, P, P, f"w1_low{e}") for e in (3, 4)}
 
         mask_tiles(E - 1)
         for u in range(2):
             make_last_mask(u)
-        w1_bf[4] = [round_columns(w1_raw[4], 0, K - BESIDE_PRODUCT, K, "w1_bf4", A_AT[4] + 4 * KIB)]
         apply_mask(4)
-        quantise_w1_half(3, 0, MASK_AT[4] + 2 * KIB)
+        quantise_w1_half(3, 0, low[3], MASK_AT[4] + 2 * KIB)
         second_product(3, 0, 0, C, sums[2], nc.scalar.copy)
         quantise_last_da(0, MASK_AT[4])
-        quantise_w1(4)
+        quantise_w1_half(4, 0, low[4], A_AT[4])
         quantise_last_da(1, RAW1_AT[4])
-        quantise_w1_half(3, 1, RAW1_AT[4] + KIB)
+        high = {}
+        for e in (3, 4):
+            high[e] = kept([P, P, PACK], BF16, f"w1_high{e}")
+            nc.vector.tensor_copy(packed_view(high[e][:]), planes_view(w1_half[e, 1][:]))
+        for e in (3, 4):
+            quantise_w1_half(e, 1, high[e], A_AT[4] + e * KIB)
         for half in range(2):
             last_product(0, half, turned[2 + half][:, :HALF])
             nc.scalar.copy(dx[0][:, 4 * C + half * HALF : 4 * C + (half + 1) * HALF], turned[2 + half][:, :HALF])

@@ -39,11 +39,11 @@ MASK_AT = (RAW2_AT[3], RAW2_AT[3] + 4 * KIB, SPARE[2], SPARE[3], CAST_B)
 RAW1_AT = tuple(124 * KIB + 4 * KIB * e for e in range(E))
 W1_WORDS_AT = (MASK_AT[1] + 2 * KIB, MASK_AT[2] + 2 * KIB, MASK_AT[3] + 2 * KIB)
 FIRST_ON_SCALAR = 304
-W2_ON_SCALAR = (192, 128, 160)
-WORD_CUTS = (4, 10, 16, 20)
+W2_ON_SCALAR = (224, 128, 160)
+WORD_CUTS = (4, 11, 16, 20)
 SCALE_CUTS = (13, 16, 20)
-LOW_CUTS = (0, 256, 576, 928, T)
-HIGH_CUTS = (0, 384, 768, 1120, T)
+LOW_CUTS = (320, 800, T)
+HIGH_CUTS = (0, 448, 800, 1056)
 
 
 def planes_view(raw):
@@ -136,10 +136,10 @@ def tile_moe_bdx_mlp_relu_kernel(tc, dy_words, dy_scales, a, w2, w1, gate, offs,
             nc.sync.dma_start(a_pair[u][:], a_rows[:, 2 * u : 2 * u + 2, (E - 1) * C :])
         for e in (3, 4):
             load_w1_half(e, 0)
-        nc.sync.dma_start(pos_sb[0][:], pos1)
-        nc.sync.dma_start(pos_sb[1][:], pos2)
         for e in (3, 4):
             load_w1_half(e, 1)
+        nc.sync.dma_start(pos_sb[0][:], pos1)
+        nc.sync.dma_start(pos_sb[1][:], pos2)
 
         nc.tensor.transpose(turned[3][:, 0:P], gate_rows[:], ident[:])
         nc.scalar.copy(gate_cols[:], turned[3][:, 0 : S // P])
@@ -265,14 +265,11 @@ def tile_moe_bdx_mlp_relu_kernel(tc, dy_words, dy_scales, a, w2, w1, gate, offs,
         gather(dy_w, U32, g_w, 0, 4, RAW2_AT[0] + 4 * KIB)
         for e in (1, 2, 3):
             part = round_columns(w2_raw[e], 0, W2_ON_SCALAR[e - 1], H, f"w2_bf{e}", CAST_A)
-            if e == 1:
-                first_products(0)
+            first_products(e - 1)
             gather(dy_w, U32, g_w, WORD_CUTS[e - 1], WORD_CUTS[e], RAW2_AT[e - 1])
             if e > 1:
                 gather(dy_s, U8, g_s, SCALE_CUTS[e - 2], SCALE_CUTS[e - 1], RAW2_AT[e - 1] + 4 * KIB)
             quantise(w2_w[e], w2_s[e], 0, H, part, E4M3)
-            if e < 3:
-                first_products(e)
 
         early = round_columns(w2_raw[4], 0, H - P, H - P, "w2_bf4a", CAST_B)
         make_mask(0, pairs_view(a_raw[0][:]))
@@ -290,12 +287,10 @@ def tile_moe_bdx_mlp_relu_kernel(tc, dy_words, dy_scales, a, w2, w1, gate, offs,
             make_mask(e, pairs_view(a_raw[e][:]))
             w1_bf[e - 1] = [round_columns(w1_raw[e - 1], 0, 0, P, f"w1_low{e - 1}", A_AT[e])] + w1_bf[e - 1]
             apply_mask(e)
-            if e == 3:
-                quantise_w1(2)
             for half in range(2):
                 quantise_da(e, half)
+            quantise_w1(e - 1)
             if e < 3:
-                quantise_w1(e - 1)
                 w1_bf[e] = [round_columns(w1_raw[e], P, K, K, f"w1_high{e}")]
         low = {e: round_columns(w1_half[e, 0], 0, P, P, f"w1_low{e}") for e in (3, 4)}
 
@@ -317,15 +312,31 @@ def tile_moe_bdx_mlp_relu_kernel(tc, dy_words, dy_scales, a, w2, w1, gate, offs,
         for half in range(2):
             last_product(0, half, turned[2 + half][:, :HALF])
             nc.scalar.copy(dx[0][:, 4 * C + half * HALF : 4 * C + (half + 1) * HALF], turned[2 + half][:, :HALF])
+
+        def picked(h, r, lo, hi):
+            return dx[h][:].indirect(pos_sb[r][:, lo // LIST : hi // LIST])
+
+        def gather_on_scalar(h, r, lo, hi):
+            values = kept([P, hi - lo], F32, f"values{h}_{r}_{lo}")
+            nc.scalar.activation(values[:], picked(h, r, lo, hi), COPY)
+            return values[:]
+
+        def add_and_store(h, lo, hi, second, first):
+            total = kept([P, hi - lo], F32, f"total{h}_{lo}")
+            nc.vector.tensor_tensor(total[:], second, first, ADD)
+            nc.sync.dma_start(out[h * P : (h + 1) * P, lo:hi], total[:])
+
+        opening = LOW_CUTS[0]
+        first = gather_on_scalar(0, 0, 0, opening)
+        second = kept([P, opening], F32, "second")
+        nc.vector.tensor_copy(second[:], picked(0, 1, 0, opening))
         second_product(3, 1, 0, C, sums[3], nc.vector.tensor_copy)
+        add_and_store(0, 0, opening, second[:], first)
         for half in range(2):
             last_product(1, half, sums[0][:, half * HALF : (half + 1) * HALF])
         nc.vector.tensor_copy(dx[1][:, 4 * C :], sums[0][:])
-
         for h, cuts in enumerate((LOW_CUTS, HIGH_CUTS)):
             for lo, hi in zip(cuts, cuts[1:]):
-                first = kept([P, hi - lo], F32, f"first{h}_{lo}")
-                total = kept([P, hi - lo], F32, f"total{h}_{lo}")
-                nc.scalar.activation(first[:], dx[h][:].indirect(pos_sb[0][:, lo // LIST : hi // LIST]), COPY)
-                nc.vector.tensor_tensor(total[:], dx[h][:].indirect(pos_sb[1][:, lo // LIST : hi // LIST]), first[:], ADD)
-                nc.sync.dma_start(out[h * P : (h + 1) * P, lo:hi], total[:])
+                add_and_store(h, lo, hi, picked(h, 1, lo, hi), gather_on_scalar(h, 0, lo, hi))
+        closing = HIGH_CUTS[-1]
+        add_and_store(1, closing, T, gather_on_scalar(1, 1, closing, T), gather_on_scalar(1, 0, closing, T))

@@ -85,8 +85,8 @@ def tile_moe_bdx_mlp_relu_kernel(tc, dy_words, dy_scales, a, w2, w1, gate, offs,
         w2_raw = [placed([P, PACK, H], F32, f"w2_raw{e}", RAW2_AT[e]) for e in range(E)]
         w1_raw = [placed([P, PACK, K], F32, f"w1_raw{e}", RAW1_AT[e]) for e in range(3)]
         w1_half = {(e, h): placed([P, PACK, P], F32, f"w1_half{e}_{h}", RAW1_AT[e] + 2 * KIB * h) for e in (3, 4) for h in range(2)}
-        a_raw = [placed([P, PACK, C], F32, f"a_raw{e}", A_AT[e]) for e in range(E - 1)]
-        a_pair = [placed([P, 2, C], F32, f"a_pair{u}", A_AT[E - 1] + u * 4 * KIB) for u in range(2)]
+        a_raw = [placed([P, PACK, C], F32, f"a_raw{e}", A_AT[e]) for e in range(3)]
+        a_pair = {(e, u): placed([P, 2, C], F32, f"a_pair{e}_{u}", A_AT[e] + u * 4 * KIB) for e in (3, 4) for u in range(2)}
         w2_w = [kept([P, H], U32, f"w2_w{e}") for e in range(E)]
         w2_s = [kept([P, H], U8, f"w2_s{e}") for e in range(E)]
         w1_w = {}
@@ -114,6 +114,10 @@ def tile_moe_bdx_mlp_relu_kernel(tc, dy_words, dy_scales, a, w2, w1, gate, offs,
         def load_a(e):
             nc.sync.dma_start(a_raw[e][:], a_rows[:, :, e * C : (e + 1) * C])
 
+        def load_a_pairs(e):
+            for u in range(2):
+                nc.sync.dma_start(a_pair[e, u][:], a_rows[:, 2 * u : 2 * u + 2, e * C : (e + 1) * C])
+
         nc.sync.dma_start(offs_sb[:], offs)
         for q in range(4):
             rows = dy_scales[0, 4 * q : 4 * q + 4, :].bitcast(I32).unsqueeze(0).to_broadcast([8, 4, T // 4])
@@ -130,16 +134,15 @@ def tile_moe_bdx_mlp_relu_kernel(tc, dy_words, dy_scales, a, w2, w1, gate, offs,
         load_w1(0)
         load_a(2)
         load_w1(1)
-        load_a(3)
+        load_a_pairs(3)
         load_w1(2)
-        for u in range(2):
-            nc.sync.dma_start(a_pair[u][:], a_rows[:, 2 * u : 2 * u + 2, (E - 1) * C :])
+        load_a_pairs(4)
         for e in (3, 4):
             load_w1_half(e, 0)
-        for e in (3, 4):
-            load_w1_half(e, 1)
         nc.sync.dma_start(pos_sb[0][:], pos1)
         nc.sync.dma_start(pos_sb[1][:], pos2)
+        for e in (3, 4):
+            load_w1_half(e, 1)
 
         nc.tensor.transpose(turned[3][:, 0:P], gate_rows[:], ident[:])
         nc.scalar.copy(gate_cols[:], turned[3][:, 0 : S // P])
@@ -201,10 +204,12 @@ def tile_moe_bdx_mlp_relu_kernel(tc, dy_words, dy_scales, a, w2, w1, gate, offs,
             for half in range(2):
                 nc.vector.tensor_scalar(mask[e, half][:], source[:, :, half * HALF : (half + 1) * HALF, :], 0.0, None, IS_GT)
 
-        def make_last_mask(u):
-            for half in range(2):
-                source = a_pair[u][:, :, half * HALF : (half + 1) * HALF].rearrange("p x n -> p n x")
-                nc.vector.tensor_scalar(mask[E - 1, half][:, u], source, 0.0, None, IS_GT)
+        def make_mask_by_pairs(e):
+            mask_tiles(e)
+            for u in range(2):
+                for half in range(2):
+                    source = a_pair[e, u][:, :, half * HALF : (half + 1) * HALF].rearrange("p x n -> p n x")
+                    nc.vector.tensor_scalar(mask[e, half][:, u], source, 0.0, None, IS_GT)
 
         def apply_mask(e):
             for half in range(2):
@@ -284,8 +289,11 @@ def tile_moe_bdx_mlp_relu_kernel(tc, dy_words, dy_scales, a, w2, w1, gate, offs,
         first_products(4)
 
         for e in (1, 2, 3):
-            make_mask(e, pairs_view(a_raw[e][:]))
-            w1_bf[e - 1] = [round_columns(w1_raw[e - 1], 0, 0, P, f"w1_low{e - 1}", A_AT[e])] + w1_bf[e - 1]
+            if e < 3:
+                make_mask(e, pairs_view(a_raw[e][:]))
+            else:
+                make_mask_by_pairs(e)
+            w1_bf[e - 1] = [round_columns(w1_raw[e - 1], 0, 0, P, f"w1_low{e - 1}", A_AT[e] + 4 * KIB)] + w1_bf[e - 1]
             apply_mask(e)
             for half in range(2):
                 quantise_da(e, half)
@@ -294,9 +302,7 @@ def tile_moe_bdx_mlp_relu_kernel(tc, dy_words, dy_scales, a, w2, w1, gate, offs,
                 w1_bf[e] = [round_columns(w1_raw[e], P, K, K, f"w1_high{e}")]
         low = {e: round_columns(w1_half[e, 0], 0, P, P, f"w1_low{e}") for e in (3, 4)}
 
-        mask_tiles(E - 1)
-        for u in range(2):
-            make_last_mask(u)
+        make_mask_by_pairs(4)
         apply_mask(4)
         quantise_w1_half(3, 0, low[3], MASK_AT[4] + 2 * KIB)
         second_product(3, 0, 0, C, sums[2], nc.scalar.copy)

@@ -252,6 +252,12 @@ def tile_moe_bdx_mlp_relu_kernel(tc, dy_words, dy_scales, a, w2, w1, gate, offs,
             nc.vector.quantize_mx(out=words[:].bitcast(E4M3), scales=w1_s[e][:, cols], in_=flat(grouped[:]))
             w1_w[e, h] = words[:]
 
+        def warm_up(bank):
+            nc.tensor.matmul_mx(
+                out=bank[:], lhsT=w1_w[2, 0].bitcast(E4M3), lhsT_scale=w1_s[2][:, :P],
+                rhs=da_w[2][:].bitcast(E5M2), rhs_scale=da_s[2][:], start=True, stop=True,
+            )
+
         def quantise_last_da(half, at):
             last_w[half] = placed([P, HALF], U32, f"last_w{half}", at)
             cols = slice(half * HALF, (half + 1) * HALF)
@@ -300,10 +306,12 @@ def tile_moe_bdx_mlp_relu_kernel(tc, dy_words, dy_scales, a, w2, w1, gate, offs,
             quantise_w1(e - 1)
             if e < 3:
                 w1_bf[e] = [round_columns(w1_raw[e], P, K, K, f"w1_high{e}")]
+        warm_up(turned[2])
         low = {e: round_columns(w1_half[e, 0], 0, P, P, f"w1_low{e}") for e in (3, 4)}
 
         make_mask_by_pairs(4)
         apply_mask(4)
+        warm_up(turned[0])
         quantise_w1_half(3, 0, low[3], MASK_AT[4] + 2 * KIB)
         second_product(3, 0, 0, C, sums[2], nc.scalar.copy)
         quantise_last_da(0, MASK_AT[4])

@@ -233,18 +233,18 @@ def tile_moe_bdx_mlp_relu_kernel(tc, dy_words, dy_scales, a, w2, w1, gate, offs,
             )
             copy(dx[h][:, e * C + lo : e * C + hi], bank[:, : hi - lo])
 
-        def second_products(e):
-            for h in range(2):
+        def second_products(e, halves):
+            for h in range(halves):
                 second_product(e, h, 0, C, sums[2 * (e % 2) + h], nc.scalar.copy)
 
-        def quantise_w1(e):
+        def quantise_w1(e, halves=2):
             words = placed([P, K], U32, f"w1_w{e}", W1_WORDS_AT[e])
             width = K // len(w1_bf[e])
             for j, grouped in enumerate(w1_bf[e]):
                 quantise(words, w1_s[e], j * width, (j + 1) * width, grouped, E4M3)
             for h in range(2):
                 w1_w[e, h] = words[:, h * P : (h + 1) * P]
-            second_products(e)
+            second_products(e, halves)
 
         def quantise_w1_half(e, h, grouped, at):
             words = placed([P, P], U32, f"w1_w{e}_{h}", at)
@@ -303,7 +303,7 @@ def tile_moe_bdx_mlp_relu_kernel(tc, dy_words, dy_scales, a, w2, w1, gate, offs,
             apply_mask(e)
             for half in range(2):
                 quantise_da(e, half)
-            quantise_w1(e - 1)
+            quantise_w1(e - 1, 2 if e < 3 else 1)
             if e < 3:
                 w1_bf[e] = [round_columns(w1_raw[e], P, K, K, f"w1_high{e}")]
         warm_up(turned[2])
@@ -311,7 +311,7 @@ def tile_moe_bdx_mlp_relu_kernel(tc, dy_words, dy_scales, a, w2, w1, gate, offs,
 
         make_mask_by_pairs(4)
         apply_mask(4)
-        warm_up(turned[0])
+        second_product(2, 1, 0, C, turned[0], nc.scalar.copy)
         quantise_w1_half(3, 0, low[3], MASK_AT[4] + 2 * KIB)
         second_product(3, 0, 0, C, sums[2], nc.scalar.copy)
         quantise_last_da(0, MASK_AT[4])

@@ -211,8 +211,8 @@ def tile_moe_bdx_mlp_relu_kernel(tc, dy_words, dy_scales, a, w2, w1, gate, offs,
                     source = a_pair[e, u][:, :, half * HALF : (half + 1) * HALF].rearrange("p x n -> p n x")
                     nc.vector.tensor_scalar(mask[e, half][:, u], source, 0.0, None, IS_GT)
 
-        def apply_mask(e):
-            for half in range(2):
+        def apply_mask(e, halves=(0, 1)):
+            for half in halves:
                 da_bf[e, half] = placed([P, HALF, PACK], BF16, f"da_bf{e}_{half}", DA_AT[e] + half * 2 * KIB)
                 nc.vector.tensor_tensor(
                     da_bf[e, half][:].rearrange("p n (u x) -> p n u x", u=2),
@@ -310,16 +310,17 @@ def tile_moe_bdx_mlp_relu_kernel(tc, dy_words, dy_scales, a, w2, w1, gate, offs,
         low = {e: round_columns(w1_half[e, 0], 0, P, P, f"w1_low{e}") for e in (3, 4)}
 
         make_mask_by_pairs(4)
-        apply_mask(4)
+        apply_mask(4, (0,))
+        quantise_w1_half(3, 0, low[3], A_AT[4] + 6 * KIB)
+        apply_mask(4, (1,))
         second_product(2, 1, 0, C, turned[0], nc.scalar.copy)
-        quantise_w1_half(3, 0, low[3], MASK_AT[4] + 2 * KIB)
         second_product(3, 0, 0, C, sums[2], nc.scalar.copy)
         quantise_last_da(0, MASK_AT[4])
-        quantise_w1_half(4, 0, low[4], A_AT[4])
+        quantise_w1_half(4, 0, low[4], MASK_AT[4] + KIB)
         quantise_last_da(1, RAW1_AT[4])
         high = {}
         for e in (3, 4):
-            high[e] = kept([P, P, PACK], BF16, f"w1_high{e}")
+            high[e] = placed([P, P, PACK], BF16, f"w1_high{e}", DA_AT[4] + (e - 3) * KIB)
             nc.vector.tensor_copy(packed_view(high[e][:]), planes_view(w1_half[e, 1][:]))
         for e in (3, 4):
             quantise_w1_half(e, 1, high[e], A_AT[4] + e * KIB)
@@ -342,7 +343,7 @@ def tile_moe_bdx_mlp_relu_kernel(tc, dy_words, dy_scales, a, w2, w1, gate, offs,
 
         opening = LOW_CUTS[0]
         first = gather_on_scalar(0, 0, 0, opening)
-        second = kept([P, opening], F32, "second")
+        second = placed([P, opening], F32, "second", DA_AT[4] - 512)
         nc.vector.tensor_copy(second[:], picked(0, 1, 0, opening))
         second_product(3, 1, 0, C, sums[3], nc.vector.tensor_copy)
         add_and_store(0, 0, opening, second[:], first)

@@ -252,12 +252,6 @@ def tile_moe_bdx_mlp_relu_kernel(tc, dy_words, dy_scales, a, w2, w1, gate, offs,
             nc.vector.quantize_mx(out=words[:].bitcast(E4M3), scales=w1_s[e][:, cols], in_=flat(grouped[:]))
             w1_w[e, h] = words[:]
 
-        def warm_up(bank):
-            nc.tensor.matmul_mx(
-                out=bank[:], lhsT=w1_w[2, 0].bitcast(E4M3), lhsT_scale=w1_s[2][:, :P],
-                rhs=da_w[2][:].bitcast(E5M2), rhs_scale=da_s[2][:], start=True, stop=True,
-            )
-
         def quantise_last_da(half, at):
             last_w[half] = placed([P, HALF], U32, f"last_w{half}", at)
             cols = slice(half * HALF, (half + 1) * HALF)
@@ -306,7 +300,6 @@ def tile_moe_bdx_mlp_relu_kernel(tc, dy_words, dy_scales, a, w2, w1, gate, offs,
             quantise_w1(e - 1, 2 if e < 3 else 1)
             if e < 3:
                 w1_bf[e] = [round_columns(w1_raw[e], P, K, K, f"w1_high{e}")]
-        warm_up(turned[2])
         low = {e: round_columns(w1_half[e, 0], 0, P, P, f"w1_low{e}") for e in (3, 4)}
 
         make_mask_by_pairs(4)

from contextlib import ExitStack

import concourse.mybir as mybir
from concourse.masks import make_identity

K, T, E, C, H, N = 256, 1280, 5, 512, 512, 512
S = E * C

FLOPS = 2 * S * N * H + 2 * S * H * K
BYTES = N * T + (N // 32) * T + 4 * (H * S + E * N * H + E * H * K + S + K * T) + 2 * 128 * (S + 2 * T) // 16

F32 = mybir.dt.float32
BF16 = mybir.dt.bfloat16
I32 = mybir.dt.int32
U32 = mybir.dt.uint32
U16 = mybir.dt.uint16
U8 = mybir.dt.uint8
E4M3 = mybir.dt.float8_e4m3fn_x4
E5M2 = mybir.dt.float8_e5m2_x4
COPY = mybir.ActivationFunctionType.Copy
MULT = mybir.AluOpType.mult
ADD = mybir.AluOpType.add
IS_GT = mybir.AluOpType.is_gt

P = 128
PACK = 4
LIST = 16
HALF = C // 2
KIB = 1024

RAW2_AT = tuple(8 * KIB * e for e in range(E))
A_AT = tuple(40 * KIB + 8 * KIB * e for e in range(E))
CAST_A = 80 * KIB
CAST_B = 84 * KIB
SPARE = tuple(88 * KIB + 4 * KIB * j for j in range(4))
DA_AT = tuple(104 * KIB + 4 * KIB * e for e in range(E))
ROUNDED_AT = (SPARE[0], SPARE[1], SPARE[0], RAW2_AT[4], SPARE[1])
MASK_AT = (RAW2_AT[3], RAW2_AT[3] + 4 * KIB, SPARE[2], SPARE[3], CAST_B)
RAW1_AT = tuple(124 * KIB + 4 * KIB * e for e in range(E))
W1_WORDS_AT = (MASK_AT[1] + 2 * KIB, MASK_AT[2] + 2 * KIB, MASK_AT[3] + 2 * KIB)
FIRST_ON_SCALAR = 304
W2_ON_SCALAR = (224, 128, 160)
WORD_CUTS = (4, 11, 16, 20)
SCALE_CUTS = (13, 16, 20)
LOW_CUTS = (320, 800, T)
HIGH_CUTS = (0, 448, 800, 1056)


def planes_view(raw):
    return raw.rearrange("p t (c i) -> p c t i", i=4)


def packed_view(grouped):
    return grouped.rearrange("p (c i) t -> p c t i", i=4)


def pairs_view(raw):
    return raw.rearrange("p (u x) n -> p u n x", x=2)


def flat(grouped):
    return grouped.rearrange("p n t -> p (n t)")


def tile_moe_bdx_mlp_relu_kernel(tc, dy_words, dy_scales, a, w2, w1, gate, offs, pos1, pos2, out):
    nc = tc.nc
    with ExitStack() as ctx:
        keep = ctx.enter_context(tc.tile_pool(name="keep", bufs=1))
        arena = ctx.enter_context(tc.tile_pool(name="arena", bufs=1))
        psum = ctx.enter_context(tc.psum_pool(name="psum", bufs=1))

        def placed(shape, dtype, name, offset):
            return arena.tile(shape, dtype, name=name, offset=offset, align_bytes=64)

        def kept(shape, dtype, name):
            return keep.tile(shape, dtype, name=name, align_bytes=64)

        offs_sb = keep.tile([P, S // LIST], U16, name="offs_sb")
        pos_sb = [keep.tile([P, T // LIST], U16, name=f"pos{r}_sb") for r in (1, 2)]
        dy_w = kept([P, T], U32, "dy_w")
        dy_s = kept([P, T], U8, "dy_s")
        gate_rows = kept([P, P], F32, "gate_rows")
        gate_cols = kept([P, S // P], F32, "gate_cols")
        ident = kept([P, P], F32, "ident")
        w2_raw = [placed([P, PACK, H], F32, f"w2_raw{e}", RAW2_AT[e]) for e in range(E)]
        w1_raw = [placed([P, PACK, K], F32, f"w1_raw{e}", RAW1_AT[e]) for e in range(3)]
        w1_half = {(e, h): placed([P, PACK, P], F32, f"w1_half{e}_{h}", RAW1_AT[e] + 2 * KIB * h) for e in (3, 4) for h in range(2)}
        a_raw = [placed([P, PACK, C], F32, f"a_raw{e}", A_AT[e]) for e in range(3)]
        a_pair = {(e, u): placed([P, 2, C], F32, f"a_pair{e}_{u}", A_AT[e] + u * 4 * KIB) for e in (3, 4) for u in range(2)}
        w2_w = [kept([P, H], U32, f"w2_w{e}") for e in range(E)]
        w2_s = [kept([P, H], U8, f"w2_s{e}") for e in range(E)]
        w1_w = {}
        w1_s = [kept([P, K], U8, f"w1_s{e}") for e in range(E)]
        da_w = [kept([P, C], U32, f"da_w{e}") for e in range(E - 1)]
        da_s = [kept([P, C], U8, f"da_s{e}") for e in range(E)]
        dx = [kept([P, S], F32, f"dx{h}") for h in range(K // P)]
        sums = [psum.tile([P, C], F32, name=f"sums{b}") for b in range(4)]
        turned = [psum.tile([P, C], F32, name=f"turned{b}") for b in range(4)]

        nc.gpsimd.memset(gate_rows[:], 0.0)
        make_identity(nc, ident[:])

        a_rows = a.rearrange("(p t) s -> p t s", t=PACK)

        def load_w2(e):
            nc.sync.dma_start(w2_raw[e][:], w2[e].rearrange("(p t) i -> p t i", t=PACK))

        def load_w1(e):
            nc.sync.dma_start(w1_raw[e][:], w1[e].rearrange("(p t) k -> p t k", t=PACK))

        def load_w1_half(e, h):
            nc.sync.dma_start(w1_half[e, h][:], w1[e].rearrange("(p t) k -> p t k", t=PACK)[:, :, h * P : (h + 1) * P])

        def load_a(e):
            nc.sync.dma_start(a_raw[e][:], a_rows[:, :, e * C : (e + 1) * C])

        def load_a_pairs(e):
            for u in range(2):
                nc.sync.dma_start(a_pair[e, u][:], a_rows[:, 2 * u : 2 * u + 2, e * C : (e + 1) * C])

        nc.sync.dma_start(offs_sb[:], offs)
        for q in range(4):
            rows = dy_scales[0, 4 * q : 4 * q + 4, :].bitcast(I32).unsqueeze(0).to_broadcast([8, 4, T // 4])
            (nc.scalar, nc.sync)[q % 2].dma_start(dy_s[32 * q : 32 * q + 32, :].bitcast(I32), rows)
        nc.scalar.dma_start(gate_rows[0 : S // P, :], gate[0].rearrange("(c p) -> c p", p=P))
        load_w2(0)
        nc.sync.dma_start(dy_w[:].bitcast(I32), dy_words[0].rearrange("p t d -> p (t d)").bitcast(I32))
        load_w2(1)
        load_w2(2)
        load_w2(3)
        load_a(0)
        load_w2(4)
        load_a(1)
        load_w1(0)
        load_a(2)
        load_w1(1)
        load_a_pairs(3)
        load_w1(2)
        load_a_pairs(4)
        for e in (3, 4):
            load_w1_half(e, 0)
        nc.sync.dma_start(pos_sb[0][:], pos1)
        nc.sync.dma_start(pos_sb[1][:], pos2)
        for e in (3, 4):
            load_w1_half(e, 1)

        nc.tensor.transpose(turned[3][:, 0:P], gate_rows[:], ident[:])
        nc.scalar.copy(gate_cols[:], turned[3][:, 0 : S // P])

        g_w, g_s, rounded, mask, da_bf, last_w = {}, {}, {}, {}, {}, {}

        def gather(window, dtype, into, lo, hi, at=None):
            shape, name = [P, (hi - lo) * P], f"gathered{len(g_w) + len(g_s)}"
            picked = kept(shape, dtype, name) if at is None else placed(shape, dtype, name, at)
            nc.vector.tensor_copy(picked[:], window[:].indirect(offs_sb[:, lo * P // LIST : hi * P // LIST]))
            for b in range(lo, hi):
                into[b] = picked[:, (b - lo) * P : (b - lo + 1) * P]

        def round_columns(raw, lo, cut, hi, name, at=None):
            shape = [P, hi - lo, PACK]
            grouped = kept(shape, BF16, name) if at is None else placed(shape, BF16, name, at)
            if cut > lo:
                nc.scalar.copy(packed_view(grouped[:, : cut - lo, :]), planes_view(raw[:, :, lo:cut]))
            if hi > cut:
                nc.gpsimd.tensor_scalar(grouped[:, cut - lo :, :], raw[:, :, cut:hi].rearrange("p t i -> p i t"), 1.0, 0.0, MULT, ADD)
            return grouped

        def quantise(words, scales, lo, hi, grouped, fmt):
            nc.vector.quantize_mx(out=words[:, lo:hi].bitcast(fmt), scales=scales[:, lo:hi], in_=flat(grouped[:]))

        def first_products(e):
            for s in range(4):
                b = e * (C // P) + s
                nc.tensor.matmul_mx(
                    out=sums[s][:], lhsT=g_w[b].bitcast(E5M2), lhsT_scale=g_s[b],
                    rhs=w2_w[e][:].bitcast(E4M3), rhs_scale=w2_s[e][:], start=True, stop=True,
                )
            for s in range(4):
                dh_bf = placed([P, H], BF16, f"dh_bf{e}_{s}", ROUNDED_AT[e] + s * KIB)
                col = e * (C // P) + s
                nc.scalar.activation(
                    dh_bf[:].rearrange("s (u p x) -> s u p x", u=2, x=2),
                    sums[s][:].rearrange("s (p u x) -> s u p x", u=2, x=2),
                    COPY, scale=gate_cols[:, col : col + 1],
                )
                rounded[e, s] = dh_bf
                if s % 2 == 1 and e < 2:
                    turn(e, s // 2)

        def turn(e, half):
            bank = turned[2 * (e % 2) + half]
            for s in range(2):
                pairs = rounded[e, 2 * half + s][:].bitcast(F32)
                for u in range(2):
                    at = u * HALF + s * P
                    nc.tensor.transpose(bank[:, at : at + P], pairs[:, u * P : (u + 1) * P], ident[:])

        def mask_tiles(e):
            for half in range(2):
                mask[e, half] = placed([P, 2, HALF, 2], BF16, f"mask{e}_{half}", MASK_AT[e] + half * 2 * KIB)

        def make_mask(e, source):
            mask_tiles(e)
            for half in range(2):
                nc.vector.tensor_scalar(mask[e, half][:], source[:, :, half * HALF : (half + 1) * HALF, :], 0.0, None, IS_GT)

        def make_mask_by_pairs(e):
            mask_tiles(e)
            for u in range(2):
                for half in range(2):
                    source = a_pair[e, u][:, :, half * HALF : (half + 1) * HALF].rearrange("p x n -> p n x")
                    nc.vector.tensor_scalar(mask[e, half][:, u], source, 0.0, None, IS_GT)

        def apply_mask(e, halves=(0, 1)):
            for half in halves:
                da_bf[e, half] = placed([P, HALF, PACK], BF16, f"da_bf{e}_{half}", DA_AT[e] + half * 2 * KIB)
                nc.vector.tensor_tensor(
                    da_bf[e, half][:].rearrange("p n (u x) -> p n u x", u=2),
                    turned[2 * (e % 2) + half][:].bitcast(BF16).rearrange("p (u n x) -> p n u x", u=2, x=2),
                    mask[e, half][:].rearrange("p u n x -> p n u x"),
                    MULT,
                )
                if e + 2 < E:
                    turn(e + 2, half)

        def quantise_da(e, half):
            quantise(da_w[e], da_s[e], half * HALF, (half + 1) * HALF, da_bf[e, half], E5M2)

        def second_product(e, h, lo, hi, bank, copy):
            nc.tensor.matmul_mx(
                out=bank[:, : hi - lo], lhsT=w1_w[e, h].bitcast(E4M3), lhsT_scale=w1_s[e][:, h * P : (h + 1) * P],
                rhs=da_w[e][:, lo:hi].bitcast(E5M2), rhs_scale=da_s[e][:, lo:hi], start=True, stop=True,
            )
            copy(dx[h][:, e * C + lo : e * C + hi], bank[:, : hi - lo])

        def second_products(e, halves):
            for h in range(halves):
                second_product(e, h, 0, C, sums[2 * (e % 2) + h], nc.scalar.copy)

        def quantise_w1(e, halves=2):
            words = placed([P, K], U32, f"w1_w{e}", W1_WORDS_AT[e])
            width = K // len(w1_bf[e])
            for j, grouped in enumerate(w1_bf[e]):
                quantise(words, w1_s[e], j * width, (j + 1) * width, grouped, E4M3)
            for h in range(2):
                w1_w[e, h] = words[:, h * P : (h + 1) * P]
            second_products(e, halves)

        def quantise_w1_half(e, h, grouped, at):
            words = placed([P, P], U32, f"w1_w{e}_{h}", at)
            cols = slice(h * P, (h + 1) * P)
            nc.vector.quantize_mx(out=words[:].bitcast(E4M3), scales=w1_s[e][:, cols], in_=flat(grouped[:]))
            w1_w[e, h] = words[:]

        def quantise_last_da(half, at):
            last_w[half] = placed([P, HALF], U32, f"last_w{half}", at)
            cols = slice(half * HALF, (half + 1) * HALF)
            nc.vector.quantize_mx(out=last_w[half][:].bitcast(E5M2), scales=da_s[4][:, cols], in_=flat(da_bf[4, half][:]))

        def last_product(h, half, bank):
            nc.tensor.matmul_mx(
                out=bank, lhsT=w1_w[4, h].bitcast(E4M3), lhsT_scale=w1_s[4][:, h * P : (h + 1) * P],
                rhs=last_w[half][:].bitcast(E5M2), rhs_scale=da_s[4][:, half * HALF : (half + 1) * HALF], start=True, stop=True,
            )

        gather(dy_s, U8, g_s, 0, 7)
        gather(dy_s, U8, g_s, 7, SCALE_CUTS[0])
        part = round_columns(w2_raw[0], 0, FIRST_ON_SCALAR, H, "w2_bf0", CAST_A)
        quantise(w2_w[0], w2_s[0], 0, H, part, E4M3)
        gather(dy_w, U32, g_w, 0, 4, RAW2_AT[0] + 4 * KIB)
        for e in (1, 2, 3):
            part = round_columns(w2_raw[e], 0, W2_ON_SCALAR[e - 1], H, f"w2_bf{e}", CAST_A)
            first_products(e - 1)
            gather(dy_w, U32, g_w, WORD_CUTS[e - 1], WORD_CUTS[e], RAW2_AT[e - 1])
            if e > 1:
                gather(dy_s, U8, g_s, SCALE_CUTS[e - 2], SCALE_CUTS[e - 1], RAW2_AT[e - 1] + 4 * KIB)
            quantise(w2_w[e], w2_s[e], 0, H, part, E4M3)

        early = round_columns(w2_raw[4], 0, H - P, H - P, "w2_bf4a", CAST_B)
        make_mask(0, pairs_view(a_raw[0][:]))
        late = round_columns(w2_raw[4], H - P, H - P, H, "w2_bf4b", A_AT[0])
        first_products(3)
        apply_mask(0)
        for half in range(2):
            quantise_da(0, half)
        quantise(w2_w[4], w2_s[4], H - P, H, late, E4M3)
        quantise(w2_w[4], w2_s[4], 0, H - P, early, E4M3)
        w1_bf = {0: [round_columns(w1_raw[0], P, K, K, "w1_high0")]}
        first_products(4)

        for e in (1, 2, 3):
            if e < 3:
                make_mask(e, pairs_view(a_raw[e][:]))
            else:
                make_mask_by_pairs(e)
            w1_bf[e - 1] = [round_columns(w1_raw[e - 1], 0, 0, P, f"w1_low{e - 1}", A_AT[e] + 4 * KIB)] + w1_bf[e - 1]
            apply_mask(e)
            for half in range(2):
                quantise_da(e, half)
            quantise_w1(e - 1, 2 if e < 3 else 1)
            if e < 3:
                w1_bf[e] = [round_columns(w1_raw[e], P, K, K, f"w1_high{e}")]
        low = {e: round_columns(w1_half[e, 0], 0, P, P, f"w1_low{e}") for e in (3, 4)}

        make_mask_by_pairs(4)
        apply_mask(4, (0,))
        quantise_w1_half(3, 0, low[3], A_AT[4] + 6 * KIB)
        apply_mask(4, (1,))
        second_product(2, 1, 0, C, turned[0], nc.scalar.copy)
        second_product(3, 0, 0, C, sums[2], nc.scalar.copy)
        quantise_last_da(0, MASK_AT[4])
        quantise_w1_half(4, 0, low[4], MASK_AT[4] + KIB)
        quantise_last_da(1, RAW1_AT[4])
        high = {}
        for e in (3, 4):
            high[e] = placed([P, P, PACK], BF16, f"w1_high{e}", DA_AT[4] + (e - 3) * KIB)
            nc.vector.tensor_copy(packed_view(high[e][:]), planes_view(w1_half[e, 1][:]))
        for e in (3, 4):
            quantise_w1_half(e, 1, high[e], A_AT[4] + e * KIB)
        for half in range(2):
            last_product(0, half, turned[2 + half][:, :HALF])
            nc.scalar.copy(dx[0][:, 4 * C + half * HALF : 4 * C + (half + 1) * HALF], turned[2 + half][:, :HALF])

        def picked(h, r, lo, hi):
            return dx[h][:].indirect(pos_sb[r][:, lo // LIST : hi // LIST])

        def gather_on_scalar(h, r, lo, hi):
            values = kept([P, hi - lo], F32, f"values{h}_{r}_{lo}")
            nc.scalar.activation(values[:], picked(h, r, lo, hi), COPY)
            return values[:]

        def add_and_store(h, lo, hi, second, first):
            total = kept([P, hi - lo], F32, f"total{h}_{lo}")
            nc.vector.tensor_tensor(total[:], second, first, ADD)
            nc.sync.dma_start(out[h * P : (h + 1) * P, lo:hi], total[:])

        opening = LOW_CUTS[0]
        first = gather_on_scalar(0, 0, 0, opening)
        second = placed([P, opening], F32, "second", DA_AT[4] - 512)
        nc.vector.tensor_copy(second[:], picked(0, 1, 0, opening))
        second_product(3, 1, 0, C, sums[3], nc.vector.tensor_copy)
        add_and_store(0, 0, opening, second[:], first)
        for half in range(2):
            last_product(1, half, sums[0][:, half * HALF : (half + 1) * HALF])
        nc.vector.tensor_copy(dx[1][:, 4 * C :], sums[0][:])
        for h, cuts in enumerate((LOW_CUTS, HIGH_CUTS)):
            for lo, hi in zip(cuts, cuts[1:]):
                add_and_store(h, lo, hi, picked(h, 1, lo, hi), gather_on_scalar(h, 0, lo, hi))
        closing = HIGH_CUTS[-1]
        add_and_store(1, closing, T, gather_on_scalar(1, 1, closing, T), gather_on_scalar(1, 0, closing, T))
